import numpy as np
import ml_dtypes


def mxq(x, axis, fmt="e4m3"):
    dtype, down = {"e4m3": (ml_dtypes.float8_e4m3fn, 7), "e5m2": (ml_dtypes.float8_e5m2, 14)}[fmt]
    v = np.moveaxis(np.asarray(x, np.float32).astype(ml_dtypes.bfloat16).astype(np.float64), axis, -1)
    blocks = v.reshape(v.shape[:-1] + (-1, 32))
    amax = np.abs(blocks).max(-1, keepdims=True)
    byte = np.maximum(np.where(amax > 0, np.frexp(amax)[1] - 1 + 127, 0) - down, 1)
    scale = np.exp2(byte - 127.0)
    codes = (blocks / scale).astype(np.float32).astype(dtype).astype(np.float64)
    return np.moveaxis((codes * scale).reshape(v.shape), -1, axis)


WIDE = False


def mx_kscale(k):
    if not WIDE:
        return np.ones(k)
    levels = np.array([18, -18])
    if k % 512:
        return np.exp2(np.random.permutation(np.resize(levels, k // 32))).repeat(32)
    a = np.empty((k // 512, 16))
    for p in range(k // 512):
        a[p, :8] = np.random.permutation(np.resize(levels, 8))
        for g in range(8):
            far = levels[np.abs(levels - a[p, g]) >= 10]
            a[p, g + 8] = far[np.random.randint(len(far))]
    return np.exp2(a.ravel()).repeat(32)


def f64(x):
    return np.asarray(x).astype(np.float64)


def striped(idx):
    return np.tile(np.asarray(idx).reshape(-1, 16).T, (8, 1)).astype(np.uint16)


def unstriped(offs):
    return offs[:16].T.reshape(-1).astype(np.int64)


E2M1 = np.array([0.0, 0.5, 1.0, 1.5, 2.0, 3.0, 4.0, 6.0, -0.0, -0.5, -1.0, -1.5, -2.0, -3.0, -4.0, -6.0])


def pack_weight(w, fmt):
    k, n = w.shape
    w = f64(np.asarray(w, np.float32).astype(ml_dtypes.bfloat16)).reshape(k // 32, 32, n)
    amax = np.abs(w).max(1)
    if fmt == "e4m3":
        byte = np.frexp(amax)[1] - 1 + 127 - 7
    else:
        mant, ex = np.frexp(amax / 6.0)
        byte = np.where(mant > 0.5, ex, ex - 1) + 127
    byte = np.clip(np.where(amax > 0, byte, 1), 1, 254)
    scaled = (w * np.exp2(127.0 - byte)[:, None, :]).reshape(k, n).astype(np.float32)
    by_word = np.ascontiguousarray(scaled.reshape(k // 512, 128, 4, n).transpose(0, 1, 3, 2))
    if fmt == "e4m3":
        words = by_word.astype(ml_dtypes.float8_e4m3fn).view(np.uint8)
    else:
        c = by_word.astype(ml_dtypes.float4_e2m1fn).view(np.uint8) & 0xF
        words = (c[..., 0::2] | (c[..., 1::2] << 4)).reshape(k // 512, 128, 2 * n)
    return np.ascontiguousarray(words), np.ascontiguousarray(byte.astype(np.uint8).reshape(k // 512, 16, n))


def unpack_weight(words, scales, fmt):
    g, _, n = scales.shape
    words = np.ascontiguousarray(words).reshape(g, 128, n, -1)
    if fmt == "e4m3":
        vals = words.view(ml_dtypes.float8_e4m3fn).astype(np.float64)
    else:
        nib = np.empty((g, 128, n, 4), np.uint8)
        nib[..., 0::2] = words & 0xF
        nib[..., 1::2] = words >> 4
        vals = E2M1[nib]
    vals = vals * np.repeat(np.exp2(scales.astype(np.float64) - 127.0), 8, axis=1)[..., None]
    return vals.transpose(0, 1, 3, 2).reshape(g * 512, n)


B, N, T, D, R = 1, 512, 2048, 512, 1024


def setup_inputs():
    n = np.random.standard_normal
    idx = np.random.permutation(T)[:B * N]
    s = mx_kscale(D)[:, None]
    z = mx_kscale(R)[:, None]
    x = n((B, D, R))
    wp = pack_weight(n((D, T)) * (1.00 / np.sqrt(D)) / s, "e4m3")
    return {
        "xT": (x * s).astype(np.float32),
        "w_words": wp[0],
        "w_scales": wp[1],
        "vT": (n((D, T)) / np.sqrt(D) / s).astype(np.float32),
        "wt": (np.random.uniform(0.5, 1.5, (B, R, 1)) * 1.0 / np.sqrt(R) * z).astype(np.float32),
        "xm": (x.transpose(0, 2, 1) / z).astype(np.float32),
        "offs": striped(idx),
    }


def reference(xT, w_words, w_scales, vT, wt, xm, offs):
    idx = unstriped(offs)
    w = unpack_weight(w_words, w_scales, "e4m3")
    pick = lambda x: x[:, idx].reshape(x.shape[0], B, N).transpose(1, 0, 2)
    xq = mxq(f64(xT), 1, "e4m3").transpose(0, 2, 1)
    a = xq @ pick(w)
    av = xq @ mxq(pick(f64(vT)), 1, "e4m3")
    p = 1.0 / (1.0 + np.exp(-a))
    g = f64(wt) * p * (1.0 - p) * av
    dw = mxq(f64(xm), 1, "e4m3").transpose(0, 2, 1) @ mxq(g, 1, "e5m2")
    gw = np.zeros((D, T))
    gw[:, idx] = dw.transpose(1, 0, 2).reshape(D, B * N)
    return gw

@@ -1,0 +1,200 @@
+from contextlib import ExitStack
+
+import concourse.mybir as mybir
+
+N, T, D, R = 512, 2048, 512, 1024
+FLOPS = 3 * 2 * D * R * N
+
+F32 = mybir.dt.float32
+BF16 = mybir.dt.bfloat16
+I32 = mybir.dt.int32
+U32 = mybir.dt.uint32
+U16 = mybir.dt.uint16
+U8 = mybir.dt.uint8
+E4M3 = mybir.dt.float8_e4m3fn_x4
+E5M2 = mybir.dt.float8_e5m2_x4
+ACT = mybir.ActivationFunctionType
+ALU = mybir.AluOpType
+
+P = 128
+PACK = 4
+HALF = P * PACK
+HALVES = R // HALF
+SLOT_BLOCKS = N // P
+D_BLOCKS = D // P
+WINDOWS = 3
+
+
+def tile_attend_ghv_nce_kernel(tc, xT, w_words, w_scales, vT, wt, xm, offs, out):
+    nc = tc.nc
+    with ExitStack() as ctx:
+        sb = ctx.enter_context(tc.tile_pool(name="sb", bufs=1))
+        ps = ctx.enter_context(tc.psum_pool(name="ps", bufs=4))
+
+        def tile(name, shape, dtype):
+            return sb.tile(shape, dtype, name=name, align_bytes=64)
+
+        offsets = sb.tile([P, N // 16], U16, name="offsets")
+        w_table = tile("w_table", [P, T], U32)
+        s_table = tile("s_table", [P, T], U8)
+        x_raw = [tile("x_raw%d" % h, [P, PACK, HALF], F32) for h in range(HALVES)]
+        v_table = [tile("v_table%d" % j, [P, T], F32) for j in range(PACK)]
+        m_raw = [tile("m_raw%d" % h, [P, PACK, D], F32) for h in range(HALVES)]
+        wt_sb = tile("wt_sb", [P, HALVES, PACK], F32)
+        windows = [tile("window%d" % j, [P, T], F32) for j in range(WINDOWS)]
+
+        nc.vector.memset(s_table[:].bitcast(I32), 0)
+
+        nc.sync.dma_start(offsets[:], offs)
+        nc.sync.dma_start(w_table[:].bitcast(I32), w_words[0].rearrange("p n t -> p (n t)").bitcast(I32))
+        for q in range(4):
+            nc.sync.dma_start(s_table[32 * q : 32 * q + 4, :].bitcast(I32), w_scales[0][4 * q : 4 * q + 4, :].bitcast(I32))
+        x_rows = xT[0].rearrange("(p j) r -> p j r", j=PACK)
+        for h in range(HALVES):
+            nc.sync.dma_start(x_raw[h][:], x_rows[:, :, h * HALF : (h + 1) * HALF])
+        nc.sync.dma_start(wt_sb[:], wt[0].rearrange("(h p t) o -> p h (t o)", h=HALVES, t=PACK))
+        v_rows = vT.rearrange("(p j) c -> p j c", j=PACK)
+        for j in range(PACK):
+            nc.sync.dma_start(v_table[j][:], v_rows[:, j, :])
+        for h in range(HALVES):
+            nc.sync.dma_start(m_raw[h][:], xm[0][h * HALF : (h + 1) * HALF, :].rearrange("(p t) d -> p t d", t=PACK))
+
+        for j in range(WINDOWS):
+            nc.vector.memset(windows[j][:].bitcast(I32), 0)
+
+        w_codes = tile("w_codes", [P, N], U32)
+        w_bytes = tile("w_bytes", [P, N], U8)
+        nc.vector.tensor_copy(w_codes[:], w_table[:].indirect(offsets[:]))
+        nc.vector.tensor_copy(w_bytes[:], s_table[:].indirect(offsets[:]))
+
+        x_bf = [tile("x_bf%d" % h, [P, HALF * PACK], BF16) for h in range(HALVES)]
+        x_codes = [tile("x_codes%d" % h, [P, HALF], U32) for h in range(HALVES)]
+        x_bytes = [tile("x_bytes%d" % h, [P, HALF], U8) for h in range(HALVES)]
+        for h in range(HALVES):
+            nc.vector.tensor_copy(
+                x_bf[h][:].rearrange("p (t m j) -> p m j t", t=PACK, j=PACK),
+                x_raw[h][:].rearrange("p j (m t) -> p m j t", t=PACK),
+            )
+            nc.vector.quantize_mx(x_codes[h][:].bitcast(E4M3), x_bytes[h][:], x_bf[h][:])
+
+        quarter = tile("quarter", [P, HALVES, PACK], F32)
+        minus_quarter = tile("minus_quarter", [P, HALVES, PACK], F32)
+        nc.vector.tensor_scalar(quarter[:], wt_sb[:], 0.25, None, ALU.mult)
+        nc.vector.tensor_scalar(minus_quarter[:], wt_sb[:], -0.25, None, ALU.mult)
+
+        def stationary(codes, scale_bytes, block):
+            cols = slice(block * P, (block + 1) * P)
+            return dict(lhsT=codes[:, cols].bitcast(E4M3), lhsT_scale=scale_bytes[:, cols])
+
+        th = [tile("th%d" % h, [P, PACK, N], F32) for h in range(HALVES)]
+        sq = [tile("sq%d" % h, [P, PACK, N], F32) for h in range(HALVES)]
+        factor = [tile("factor%d" % h, [P, PACK, N], F32) for h in range(HALVES)]
+        v_bf = tile("v_bf", [P, N, PACK], BF16)
+
+        def score(h, t):
+            a = ps.tile([P, N], F32, name="wide")
+            nc.tensor.matmul_mx(a[:], rhs=w_codes[:].bitcast(E4M3), rhs_scale=w_bytes[:], start=True, stop=True,
+                                **stationary(x_codes[h], x_bytes[h], t))
+            nc.scalar.activation(th[h][:, t, :], a[:], ACT.Tanh, scale=0.5)
+            nc.scalar.activation(sq[h][:, t, :], th[h][:, t, :], ACT.Square)
+
+        def affine(h, t):
+            c, mc = quarter[:, h, t : t + 1], minus_quarter[:, h, t : t + 1]
+            if h == 0:
+                nc.vector.tensor_scalar(factor[h][:, t, :], sq[h][:, t, :], mc, c, ALU.mult, ALU.add)
+            else:
+                nc.scalar.activation(factor[h][:, t, :], sq[h][:, t, :], ACT.Identity, bias=c, scale=mc)
+
+        for t in range(PACK):
+            score(0, t)
+        for t in range(PACK):
+            score(1, t)
+            affine(1, t)
+        for j in range(PACK - 1):
+            nc.vector.tensor_copy(v_bf[:, :, j], v_table[j][:].indirect(offsets[:]))
+            affine(0, j)
+        affine(0, PACK - 1)
+
+        v_codes = tile("v_codes", [P, N], U32)
+        v_bytes = tile("v_bytes", [P, N], U8)
+        hn = N // 2
+        for s in range(2):
+            nc.vector.tensor_copy(v_bf[:, s * hn : (s + 1) * hn, PACK - 1],
+                                  v_table[PACK - 1][:].indirect(offsets[:, s * hn // 16 : (s + 1) * hn // 16]))
+        for s in range(2):
+            cols = slice(s * hn, (s + 1) * hn)
+            nc.vector.quantize_mx(v_codes[:, cols].bitcast(E4M3), v_bytes[:, cols],
+                                  v_bf[:, cols, :].rearrange("p n j -> p (n j)"))
+
+        m_bf = [tile("m_bf%d" % h, [P, D * PACK], BF16) for h in range(HALVES)]
+        m_codes = [tile("m_codes%d" % h, [P, D], U32) for h in range(HALVES)]
+        m_bytes = [tile("m_bytes%d" % h, [P, D], U8) for h in range(HALVES)]
+        hd = D // 2
+
+        def cast_m(h, s):
+            nc.scalar.activation(
+                m_bf[h][:, s * hd * PACK : (s + 1) * hd * PACK].rearrange("p (c i t) -> p c t i", i=4, t=PACK),
+                m_raw[h][:, :, s * hd : (s + 1) * hd].rearrange("p t (c i) -> p c t i", i=4),
+                ACT.Copy,
+            )
+
+        def quant_m(h, s):
+            cols = slice(s * hd, (s + 1) * hd)
+            nc.vector.quantize_mx(m_codes[h][:, cols].bitcast(E4M3), m_bytes[h][:, cols],
+                                  m_bf[h][:, s * hd * PACK : (s + 1) * hd * PACK])
+
+        for h in range(HALVES):
+            for s in range(2):
+                cast_m(h, s)
+
+        g_bf = [tile("g_bf%d" % h, [P, N * PACK], BF16) for h in range(HALVES)]
+        g_codes = [tile("g_codes%d" % h, [P, N], U32) for h in range(HALVES)]
+        g_bytes = [tile("g_bytes%d" % h, [P, N], U8) for h in range(HALVES)]
+
+        def product(h, b):
+            cols = slice(b * P, (b + 1) * P)
+            av = ps.tile([P, PACK, P], F32, name="av")
+            for t in range(PACK):
+                nc.tensor.matmul_mx(av[:, t, :], rhs=v_codes[:, cols].bitcast(E4M3), rhs_scale=v_bytes[:, cols],
+                                    start=True, stop=True, **stationary(x_codes[h], x_bytes[h], t))
+            nc.vector.tensor_tensor(
+                g_bf[h][:, b * P * PACK : (b + 1) * P * PACK].rearrange("p (c i t) -> p c t i", i=4, t=PACK),
+                av[:].rearrange("p t (c i) -> p c t i", i=4),
+                factor[h][:, :, cols].rearrange("p t (c i) -> p c t i", i=4),
+                ALU.mult,
+            )
+
+        def quant_g(h, s):
+            cols = slice(s * hn, (s + 1) * hn)
+            nc.vector.quantize_mx(g_codes[h][:, cols].bitcast(E5M2), g_bytes[h][:, cols],
+                                  g_bf[h][:, s * hn * PACK : (s + 1) * hn * PACK])
+
+        sums = [ps.tile([P, N], F32, name="wide") for j in range(D_BLOCKS)]
+
+        def dw_pass(h, j):
+            nc.tensor.matmul_mx(sums[j][:], rhs=g_codes[h][:].bitcast(E5M2), rhs_scale=g_bytes[h][:],
+                                start=(h == 0), stop=(h == HALVES - 1), **stationary(m_codes[h], m_bytes[h], j))
+
+        for b in range(SLOT_BLOCKS):
+            product(0, b)
+        quant_g(0, 0)
+        product(1, 0)
+        quant_g(0, 1)
+        product(1, 1)
+        quant_m(0, 0)
+        quant_m(0, 1)
+        product(1, 2)
+        quant_g(1, 0)
+        product(1, 3)
+        for j in range(D_BLOCKS):
+            dw_pass(0, j)
+        quant_m(1, 0)
+        quant_g(1, 1)
+        quant_m(1, 1)
+
+        for j in range(D_BLOCKS):
+            dw_pass(1, j)
+            staged = tile("staged%d" % j, [P, N], F32)
+            nc.scalar.activation(staged[:], sums[j][:], ACT.Copy)
+            nc.vector.tensor_copy(windows[j % WINDOWS][:].indirect(offsets[:]), staged[:])
+            nc.sync.dma_start(out[j * P : (j + 1) * P, :], windows[j % WINDOWS][:])

@@ -23,6 +23,7 @@ HALVES = R // HALF
 SLOT_BLOCKS = N // P
 D_BLOCKS = D // P
 WINDOWS = 3
+VECTOR_SHARE = 768
 
 
 def tile_attend_ghv_nce_kernel(tc, xT, w_words, w_scales, vT, wt, xm, offs, out):
@@ -43,24 +44,31 @@ def tile_attend_ghv_nce_kernel(tc, xT, w_words, w_scales, vT, wt, xm, offs, out)
         wt_sb = tile("wt_sb", [P, HALVES, PACK], F32)
         windows = [tile("window%d" % j, [P, T], F32) for j in range(WINDOWS)]
 
-        nc.vector.memset(s_table[:].bitcast(I32), 0)
+        def zero_on_vector(words):
+            odd = words.shape[1] // 2 - 1
+            nc.vector.memset(words[:, :odd], 0)
+            nc.vector.memset(words[:, odd:], 0)
+
+        zero_on_vector(s_table[:].bitcast(I32))
 
         nc.sync.dma_start(offsets[:], offs)
         nc.sync.dma_start(w_table[:].bitcast(I32), w_words[0].rearrange("p n t -> p (n t)").bitcast(I32))
         for q in range(4):
             nc.sync.dma_start(s_table[32 * q : 32 * q + 4, :].bitcast(I32), w_scales[0][4 * q : 4 * q + 4, :].bitcast(I32))
+        nc.sync.dma_start(wt_sb[:], wt[0].rearrange("(h p t) o -> p h (t o)", h=HALVES, t=PACK))
         x_rows = xT[0].rearrange("(p j) r -> p j r", j=PACK)
         for h in range(HALVES):
             nc.sync.dma_start(x_raw[h][:], x_rows[:, :, h * HALF : (h + 1) * HALF])
-        nc.sync.dma_start(wt_sb[:], wt[0].rearrange("(h p t) o -> p h (t o)", h=HALVES, t=PACK))
         v_rows = vT.rearrange("(p j) c -> p j c", j=PACK)
         for j in range(PACK):
             nc.sync.dma_start(v_table[j][:], v_rows[:, j, :])
         for h in range(HALVES):
             nc.sync.dma_start(m_raw[h][:], xm[0][h * HALF : (h + 1) * HALF, :].rearrange("(p t) d -> p t d", t=PACK))
 
-        for j in range(WINDOWS):
-            nc.vector.memset(windows[j][:].bitcast(I32), 0)
+        zero_on_vector(windows[0][:].bitcast(I32))
+        zero_on_vector(windows[1][:, :VECTOR_SHARE].bitcast(I32))
+        nc.gpsimd.memset(windows[1][:, VECTOR_SHARE:].bitcast(I32), 0)
+        nc.gpsimd.memset(windows[2][:].bitcast(I32), 0)
 
         w_codes = tile("w_codes", [P, N], U32)
         w_bytes = tile("w_bytes", [P, N], U8)
@@ -70,17 +78,31 @@ def tile_attend_ghv_nce_kernel(tc, xT, w_words, w_scales, vT, wt, xm, offs, out)
         x_bf = [tile("x_bf%d" % h, [P, HALF * PACK], BF16) for h in range(HALVES)]
         x_codes = [tile("x_codes%d" % h, [P, HALF], U32) for h in range(HALVES)]
         x_bytes = [tile("x_bytes%d" % h, [P, HALF], U8) for h in range(HALVES)]
-        for h in range(HALVES):
+        quarter = tile("quarter", [P, HALVES, PACK], F32)
+        minus_quarter = tile("minus_quarter", [P, HALVES, PACK], F32)
+
+        def cast_x(h):
             nc.vector.tensor_copy(
                 x_bf[h][:].rearrange("p (t m j) -> p m j t", t=PACK, j=PACK),
                 x_raw[h][:].rearrange("p j (m t) -> p m j t", t=PACK),
             )
+
+        def quant_x(h):
             nc.vector.quantize_mx(x_codes[h][:].bitcast(E4M3), x_bytes[h][:], x_bf[h][:])
 
-        quarter = tile("quarter", [P, HALVES, PACK], F32)
-        minus_quarter = tile("minus_quarter", [P, HALVES, PACK], F32)
+        g_bf = [tile("g_bf%d" % h, [P, N * PACK], BF16) for h in range(HALVES)]
+        g_codes = [tile("g_codes%d" % h, [P, N], U32) for h in range(HALVES)]
+        g_bytes = [tile("g_bytes%d" % h, [P, N], U8) for h in range(HALVES)]
+        hn = N // 2
+
+        cast_x(0)
         nc.vector.tensor_scalar(quarter[:], wt_sb[:], 0.25, None, ALU.mult)
         nc.vector.tensor_scalar(minus_quarter[:], wt_sb[:], -0.25, None, ALU.mult)
+        quant_x(0)
+        cast_x(1)
+        nc.vector.memset(g_codes[1][:, hn:].bitcast(I32), 0)
+        nc.vector.memset(g_bytes[1][:, hn:].bitcast(I32), 0)
+        quant_x(1)
 
         def stationary(codes, scale_bytes, block):
             cols = slice(block * P, (block + 1) * P)
@@ -96,7 +118,9 @@ def tile_attend_ghv_nce_kernel(tc, xT, w_words, w_scales, vT, wt, xm, offs, out)
             nc.tensor.matmul_mx(a[:], rhs=w_codes[:].bitcast(E4M3), rhs_scale=w_bytes[:], start=True, stop=True,
                                 **stationary(x_codes[h], x_bytes[h], t))
             nc.scalar.activation(th[h][:, t, :], a[:], ACT.Tanh, scale=0.5)
-            nc.scalar.activation(sq[h][:, t, :], th[h][:, t, :], ACT.Square)
+
+        def square(h, t0, t1):
+            nc.scalar.activation(sq[h][:, t0:t1, :], th[h][:, t0:t1, :], ACT.Square)
 
         def affine(h, t):
             c, mc = quarter[:, h, t : t + 1], minus_quarter[:, h, t : t + 1]
@@ -105,23 +129,26 @@ def tile_attend_ghv_nce_kernel(tc, xT, w_words, w_scales, vT, wt, xm, offs, out)
             else:
                 nc.scalar.activation(factor[h][:, t, :], sq[h][:, t, :], ACT.Identity, bias=c, scale=mc)
 
+        for h in range(HALVES):
+            for t in range(PACK):
+                score(h, t)
+            square(h, 0, 2)
+            square(h, 2, 4)
         for t in range(PACK):
-            score(0, t)
-        for t in range(PACK):
-            score(1, t)
             affine(1, t)
         for j in range(PACK - 1):
             nc.vector.tensor_copy(v_bf[:, :, j], v_table[j][:].indirect(offsets[:]))
-            affine(0, j)
-        affine(0, PACK - 1)
+            for t in range(2 * j, min(2 * j + 2, PACK)):
+                affine(0, t)
 
         v_codes = tile("v_codes", [P, N], U32)
         v_bytes = tile("v_bytes", [P, N], U8)
-        hn = N // 2
-        for s in range(2):
+
+        def gather_last(s):
             nc.vector.tensor_copy(v_bf[:, s * hn : (s + 1) * hn, PACK - 1],
                                   v_table[PACK - 1][:].indirect(offsets[:, s * hn // 16 : (s + 1) * hn // 16]))
-        for s in range(2):
+
+        def quant_v(s):
             cols = slice(s * hn, (s + 1) * hn)
             nc.vector.quantize_mx(v_codes[:, cols].bitcast(E4M3), v_bytes[:, cols],
                                   v_bf[:, cols, :].rearrange("p n j -> p (n j)"))
@@ -129,34 +156,34 @@ def tile_attend_ghv_nce_kernel(tc, xT, w_words, w_scales, vT, wt, xm, offs, out)
         m_bf = [tile("m_bf%d" % h, [P, D * PACK], BF16) for h in range(HALVES)]
         m_codes = [tile("m_codes%d" % h, [P, D], U32) for h in range(HALVES)]
         m_bytes = [tile("m_bytes%d" % h, [P, D], U8) for h in range(HALVES)]
-        hd = D // 2
 
-        def cast_m(h, s):
+        def cast_m(h, j0, j1):
             nc.scalar.activation(
-                m_bf[h][:, s * hd * PACK : (s + 1) * hd * PACK].rearrange("p (c i t) -> p c t i", i=4, t=PACK),
-                m_raw[h][:, :, s * hd : (s + 1) * hd].rearrange("p t (c i) -> p c t i", i=4),
+                m_bf[h][:, j0 * P * PACK : j1 * P * PACK].rearrange("p (c i t) -> p c t i", i=4, t=PACK),
+                m_raw[h][:, :, j0 * P : j1 * P].rearrange("p t (c i) -> p c t i", i=4),
                 ACT.Copy,
             )
 
-        def quant_m(h, s):
-            cols = slice(s * hd, (s + 1) * hd)
+        def quant_m(h, j0, j1):
+            cols = slice(j0 * P, j1 * P)
             nc.vector.quantize_mx(m_codes[h][:, cols].bitcast(E4M3), m_bytes[h][:, cols],
-                                  m_bf[h][:, s * hd * PACK : (s + 1) * hd * PACK])
+                                  m_bf[h][:, j0 * P * PACK : j1 * P * PACK])
 
-        for h in range(HALVES):
-            for s in range(2):
-                cast_m(h, s)
+        cast_m(0, 0, 4)
+        cast_m(1, 0, 1)
+        cast_m(1, 1, 2)
+        cast_m(1, 2, 4)
 
-        g_bf = [tile("g_bf%d" % h, [P, N * PACK], BF16) for h in range(HALVES)]
-        g_codes = [tile("g_codes%d" % h, [P, N], U32) for h in range(HALVES)]
-        g_bytes = [tile("g_bytes%d" % h, [P, N], U8) for h in range(HALVES)]
-
-        def product(h, b):
+        def direction(h, b):
             cols = slice(b * P, (b + 1) * P)
             av = ps.tile([P, PACK, P], F32, name="av")
             for t in range(PACK):
                 nc.tensor.matmul_mx(av[:, t, :], rhs=v_codes[:, cols].bitcast(E4M3), rhs_scale=v_bytes[:, cols],
                                     start=True, stop=True, **stationary(x_codes[h], x_bytes[h], t))
+            return av
+
+        def product(h, b, av):
+            cols = slice(b * P, (b + 1) * P)
             nc.vector.tensor_tensor(
                 g_bf[h][:, b * P * PACK : (b + 1) * P * PACK].rearrange("p (c i t) -> p c t i", i=4, t=PACK),
                 av[:].rearrange("p t (c i) -> p c t i", i=4),
@@ -164,37 +191,53 @@ def tile_attend_ghv_nce_kernel(tc, xT, w_words, w_scales, vT, wt, xm, offs, out)
                 ALU.mult,
             )
 
-        def quant_g(h, s):
-            cols = slice(s * hn, (s + 1) * hn)
+        def quant_g(h, b0, b1):
+            cols = slice(b0 * P, b1 * P)
             nc.vector.quantize_mx(g_codes[h][:, cols].bitcast(E5M2), g_bytes[h][:, cols],
-                                  g_bf[h][:, s * hn * PACK : (s + 1) * hn * PACK])
+                                  g_bf[h][:, b0 * P * PACK : b1 * P * PACK])
 
         sums = [ps.tile([P, N], F32, name="wide") for j in range(D_BLOCKS)]
 
-        def dw_pass(h, j):
-            nc.tensor.matmul_mx(sums[j][:], rhs=g_codes[h][:].bitcast(E5M2), rhs_scale=g_bytes[h][:],
+        def dw_pass(bank, h, j):
+            nc.tensor.matmul_mx(bank[:], rhs=g_codes[h][:].bitcast(E5M2), rhs_scale=g_bytes[h][:],
                                 start=(h == 0), stop=(h == HALVES - 1), **stationary(m_codes[h], m_bytes[h], j))
 
-        for b in range(SLOT_BLOCKS):
-            product(0, b)
-        quant_g(0, 0)
-        product(1, 0)
-        quant_g(0, 1)
-        product(1, 1)
-        quant_m(0, 0)
-        quant_m(0, 1)
-        product(1, 2)
-        quant_g(1, 0)
-        product(1, 3)
-        for j in range(D_BLOCKS):
-            dw_pass(0, j)
-        quant_m(1, 0)
-        quant_g(1, 1)
-        quant_m(1, 1)
+        gather_last(0)
+        quant_v(0)
+        gather_last(1)
+        product(0, 0, direction(0, 0))
+        quant_v(1)
+        for b in range(1, SLOT_BLOCKS):
+            product(0, b, direction(0, b))
+        product(1, 0, direction(1, 0))
+        quant_g(0, 0, 4)
+        product(1, 1, direction(1, 1))
+        late = [direction(1, b) for b in (2, 3)]
+        quant_m(0, 0, 4)
+        quant_m(1, 0, 1)
+        quant_g(1, 0, 2)
 
+        staged = [tile("staged%d" % j, [P, N], F32) for j in range(D_BLOCKS)]
+        early = ps.tile([P, N], F32, name="av")
+        dw_pass(early, 0, 0)
+        dw_pass(early, 1, 0)
+        nc.scalar.activation(staged[0][:, :hn], early[:, :hn], ACT.Copy)
+        product(1, 2, late[0])
+        product(1, 3, late[1])
         for j in range(D_BLOCKS):
-            dw_pass(1, j)
-            staged = tile("staged%d" % j, [P, N], F32)
-            nc.scalar.activation(staged[:], sums[j][:], ACT.Copy)
-            nc.vector.tensor_copy(windows[j % WINDOWS][:].indirect(offsets[:]), staged[:])
+            dw_pass(sums[j], 0, j)
+        quant_m(1, 1, 2)
+        quant_g(1, 2, 4)
+        quant_m(1, 2, 4)
+
+        def scatter(j, cols):
+            nc.vector.tensor_copy(windows[j % WINDOWS][:].indirect(offsets[:, cols.start // 16 : cols.stop // 16]),
+                                  staged[j][:, cols])
+
+        scatter(0, slice(0, hn))
+        for j in range(D_BLOCKS):
+            cols = slice(hn if j == 0 else 0, N)
+            dw_pass(sums[j], 1, j)
+            nc.scalar.activation(staged[j][:, cols], sums[j][:, cols], ACT.Copy)
+            scatter(j, cols)
             nc.sync.dma_start(out[j * P : (j + 1) * P, :], windows[j % WINDOWS][:])

@@ -51,10 +51,10 @@ def tile_attend_ghv_nce_kernel(tc, xT, w_words, w_scales, vT, wt, xm, offs, out)
 
         zero_on_vector(s_table[:].bitcast(I32))
 
-        nc.sync.dma_start(offsets[:], offs)
         nc.sync.dma_start(w_table[:].bitcast(I32), w_words[0].rearrange("p n t -> p (n t)").bitcast(I32))
-        for q in range(4):
-            nc.sync.dma_start(s_table[32 * q : 32 * q + 4, :].bitcast(I32), w_scales[0][4 * q : 4 * q + 4, :].bitcast(I32))
+        nc.sync.dma_start(offsets[:], offs)
+        for i in range(4):
+            nc.sync.dma_start(s_table[i:P:32, :].bitcast(I32), w_scales[0][i:16:4, :].bitcast(I32))
         nc.sync.dma_start(wt_sb[:], wt[0].rearrange("(h p t) o -> p h (t o)", h=HALVES, t=PACK))
         x_rows = xT[0].rearrange("(p j) r -> p j r", j=PACK)
         for h in range(HALVES):
@@ -81,28 +81,32 @@ def tile_attend_ghv_nce_kernel(tc, xT, w_words, w_scales, vT, wt, xm, offs, out)
         quarter = tile("quarter", [P, HALVES, PACK], F32)
         minus_quarter = tile("minus_quarter", [P, HALVES, PACK], F32)
 
-        def cast_x(h):
+        def cast_x(h, t0, t1):
             nc.vector.tensor_copy(
-                x_bf[h][:].rearrange("p (t m j) -> p m j t", t=PACK, j=PACK),
-                x_raw[h][:].rearrange("p j (m t) -> p m j t", t=PACK),
+                x_bf[h][:].rearrange("p (t m j) -> p m j t", t=PACK, j=PACK)[:, :, :, t0:t1],
+                x_raw[h][:].rearrange("p j (m t) -> p m j t", t=PACK)[:, :, :, t0:t1],
             )
 
-        def quant_x(h):
-            nc.vector.quantize_mx(x_codes[h][:].bitcast(E4M3), x_bytes[h][:], x_bf[h][:])
+        def quant_x(h, t0, t1):
+            cols = slice(t0 * P, t1 * P)
+            nc.vector.quantize_mx(x_codes[h][:, cols].bitcast(E4M3), x_bytes[h][:, cols],
+                                  x_bf[h][:, t0 * P * PACK : t1 * P * PACK])
 
         g_bf = [tile("g_bf%d" % h, [P, N * PACK], BF16) for h in range(HALVES)]
         g_codes = [tile("g_codes%d" % h, [P, N], U32) for h in range(HALVES)]
         g_bytes = [tile("g_bytes%d" % h, [P, N], U8) for h in range(HALVES)]
         hn = N // 2
 
-        cast_x(0)
-        nc.vector.tensor_scalar(quarter[:], wt_sb[:], 0.25, None, ALU.mult)
-        nc.vector.tensor_scalar(minus_quarter[:], wt_sb[:], -0.25, None, ALU.mult)
-        quant_x(0)
-        cast_x(1)
         nc.vector.memset(g_codes[1][:, hn:].bitcast(I32), 0)
         nc.vector.memset(g_bytes[1][:, hn:].bitcast(I32), 0)
-        quant_x(1)
+        nc.vector.tensor_scalar(quarter[:], wt_sb[:], 0.25, None, ALU.mult)
+        nc.vector.tensor_scalar(minus_quarter[:], wt_sb[:], -0.25, None, ALU.mult)
+        cast_x(0, 0, 2)
+        quant_x(0, 0, 2)
+        cast_x(0, 2, 4)
+        quant_x(0, 2, 4)
+        cast_x(1, 0, 4)
+        quant_x(1, 0, 4)
 
         def stationary(codes, scale_bytes, block):
             cols = slice(block * P, (block + 1) * P)
@@ -144,9 +148,8 @@ def tile_attend_ghv_nce_kernel(tc, xT, w_words, w_scales, vT, wt, xm, offs, out)
         v_codes = tile("v_codes", [P, N], U32)
         v_bytes = tile("v_bytes", [P, N], U8)
 
-        def gather_last(s):
-            nc.vector.tensor_copy(v_bf[:, s * hn : (s + 1) * hn, PACK - 1],
-                                  v_table[PACK - 1][:].indirect(offsets[:, s * hn // 16 : (s + 1) * hn // 16]))
+        def gather_last(n0, n1):
+            nc.vector.tensor_copy(v_bf[:, n0:n1, PACK - 1], v_table[PACK - 1][:].indirect(offsets[:, n0 // 16 : n1 // 16]))
 
         def quant_v(s):
             cols = slice(s * hn, (s + 1) * hn)
@@ -202,12 +205,11 @@ def tile_attend_ghv_nce_kernel(tc, xT, w_words, w_scales, vT, wt, xm, offs, out)
             nc.tensor.matmul_mx(bank[:], rhs=g_codes[h][:].bitcast(E5M2), rhs_scale=g_bytes[h][:],
                                 start=(h == 0), stop=(h == HALVES - 1), **stationary(m_codes[h], m_bytes[h], j))
 
-        gather_last(0)
+        gather_last(0, hn + 32)
         quant_v(0)
-        gather_last(1)
-        product(0, 0, direction(0, 0))
+        gather_last(hn, N)
         quant_v(1)
-        for b in range(1, SLOT_BLOCKS):
+        for b in range(SLOT_BLOCKS):
             product(0, b, direction(0, b))
         product(1, 0, direction(1, 0))
         quant_g(0, 0, 4)

@@ -188,9 +188,9 @@ def tile_attend_ghv_nce_kernel(tc, xT, w_words, w_scales, vT, wt, xm, offs, out)
         def product(h, b, av):
             cols = slice(b * P, (b + 1) * P)
             nc.vector.tensor_tensor(
-                g_bf[h][:, b * P * PACK : (b + 1) * P * PACK].rearrange("p (c i t) -> p c t i", i=4, t=PACK),
-                av[:].rearrange("p t (c i) -> p c t i", i=4),
-                factor[h][:, :, cols].rearrange("p t (c i) -> p c t i", i=4),
+                g_bf[h][:, b * P * PACK : (b + 1) * P * PACK].rearrange("p (c i t) -> p c t i", i=2, t=PACK),
+                av[:].rearrange("p t (c i) -> p c t i", i=2),
+                factor[h][:, :, cols].rearrange("p t (c i) -> p c t i", i=2),
                 ALU.mult,
             )
 
@@ -232,14 +232,20 @@ def tile_attend_ghv_nce_kernel(tc, xT, w_words, w_scales, vT, wt, xm, offs, out)
         quant_g(1, 2, 4)
         quant_m(1, 2, 4)
 
+        window_of = [windows[0], windows[1], windows[2], windows[1]]
+
         def scatter(j, cols):
-            nc.vector.tensor_copy(windows[j % WINDOWS][:].indirect(offsets[:, cols.start // 16 : cols.stop // 16]),
+            nc.vector.tensor_copy(window_of[j][:].indirect(offsets[:, cols.start // 16 : cols.stop // 16]),
                                   staged[j][:, cols])
 
         scatter(0, slice(0, hn))
-        for j in range(D_BLOCKS):
+        for j in (1, 0, 2, 3):
             cols = slice(hn if j == 0 else 0, N)
             dw_pass(sums[j], 1, j)
             nc.scalar.activation(staged[j][:, cols], sums[j][:, cols], ACT.Copy)
             scatter(j, cols)
-            nc.sync.dma_start(out[j * P : (j + 1) * P, :], windows[j % WINDOWS][:])
+            if j < D_BLOCKS - 1:
+                nc.sync.dma_start(out[j * P : (j + 1) * P, :], window_of[j][:])
+        rows = slice(D - P, D)
+        nc.sync.dma_start(out[rows, : T // 2], window_of[3][:, : T // 2])
+        nc.scalar.dma_start(out[rows, T // 2 :], window_of[3][:, T // 2 :])

@@ -1,6 +1,7 @@
 from contextlib import ExitStack
 
 import concourse.mybir as mybir
+from concourse.masks import make_identity
 
 N, T, D, R = 512, 2048, 512, 1024
 FLOPS = 3 * 2 * D * R * N
@@ -41,7 +42,8 @@ def tile_attend_ghv_nce_kernel(tc, xT, w_words, w_scales, vT, wt, xm, offs, out)
         x_raw = [tile("x_raw%d" % h, [P, PACK, HALF], F32) for h in range(HALVES)]
         v_table = [tile("v_table%d" % j, [P, T], F32) for j in range(PACK)]
         m_raw = [tile("m_raw%d" % h, [P, PACK, D], F32) for h in range(HALVES)]
-        wt_sb = tile("wt_sb", [P, HALVES, PACK], F32)
+        wt_rows = tile("wt_rows", [P, HALF], F32)
+        identity = tile("identity", [P, P], F32)
         windows = [tile("window%d" % j, [P, T], F32) for j in range(WINDOWS)]
 
         def zero_on_vector(words):
@@ -50,15 +52,17 @@ def tile_attend_ghv_nce_kernel(tc, xT, w_words, w_scales, vT, wt, xm, offs, out)
             nc.vector.memset(words[:, odd:], 0)
 
         zero_on_vector(s_table[:].bitcast(I32))
+        zero_on_vector(wt_rows[:].bitcast(I32))
+        make_identity(nc, identity[:])
 
         nc.sync.dma_start(w_table[:].bitcast(I32), w_words[0].rearrange("p n t -> p (n t)").bitcast(I32))
         nc.sync.dma_start(offsets[:], offs)
         for i in range(4):
             nc.sync.dma_start(s_table[i:P:32, :].bitcast(I32), w_scales[0][i:16:4, :].bitcast(I32))
-        nc.sync.dma_start(wt_sb[:], wt[0].rearrange("(h p t) o -> p h (t o)", h=HALVES, t=PACK))
         x_rows = xT[0].rearrange("(p j) r -> p j r", j=PACK)
-        for h in range(HALVES):
-            nc.sync.dma_start(x_raw[h][:], x_rows[:, :, h * HALF : (h + 1) * HALF])
+        nc.sync.dma_start(x_raw[0][:], x_rows[:, :, :HALF])
+        nc.sync.dma_start(wt_rows[16:P:64, :], wt[0].rearrange("(h r) o -> h (r o)", h=HALVES))
+        nc.sync.dma_start(x_raw[1][:], x_rows[:, :, HALF:])
         v_rows = vT.rearrange("(p j) c -> p j c", j=PACK)
         for j in range(PACK):
             nc.sync.dma_start(v_table[j][:], v_rows[:, j, :])
@@ -99,13 +103,17 @@ def tile_attend_ghv_nce_kernel(tc, xT, w_words, w_scales, vT, wt, xm, offs, out)
 
         nc.vector.memset(g_codes[1][:, hn:].bitcast(I32), 0)
         nc.vector.memset(g_bytes[1][:, hn:].bitcast(I32), 0)
-        nc.vector.tensor_scalar(quarter[:], wt_sb[:], 0.25, None, ALU.mult)
-        nc.vector.tensor_scalar(minus_quarter[:], wt_sb[:], -0.25, None, ALU.mult)
         cast_x(0, 0, 2)
         quant_x(0, 0, 2)
         cast_x(0, 2, 4)
         quant_x(0, 2, 4)
         cast_x(1, 0, 4)
+        wt_turned = ps.tile([P, PACK, P], F32, name="av")
+        for t in range(PACK):
+            nc.tensor.transpose(wt_turned[:, t, :], wt_rows[:, t:HALF:PACK], identity[:])
+        wt_columns = wt_turned[:, :, 16:P:64].rearrange("p t h -> p h t")
+        nc.vector.tensor_scalar(quarter[:], wt_columns, 0.25, None, ALU.mult)
+        nc.vector.tensor_scalar(minus_quarter[:], wt_columns, -0.25, None, ALU.mult)
         quant_x(1, 0, 4)
 
         def stationary(codes, scale_bytes, block):

@@ -31,17 +31,21 @@ def tile_attend_ghv_nce_kernel(tc, xT, w_words, w_scales, vT, wt, xm, offs, out)
     nc = tc.nc
     with ExitStack() as ctx:
         sb = ctx.enter_context(tc.tile_pool(name="sb", bufs=1))
+        reused = ctx.enter_context(tc.tile_pool(name="reused", bufs=1))
         ps = ctx.enter_context(tc.psum_pool(name="ps", bufs=4))
 
         def tile(name, shape, dtype):
             return sb.tile(shape, dtype, name=name, align_bytes=64)
+
+        def placed(name, shape, dtype, offset):
+            return reused.tile(shape, dtype, name=name, align_bytes=64, offset=offset)
 
         offsets = sb.tile([P, N // 16], U16, name="offsets")
         w_table = tile("w_table", [P, T], U32)
         s_table = tile("s_table", [P, T], U8)
         x_raw = [tile("x_raw%d" % h, [P, PACK, HALF], F32) for h in range(HALVES)]
         v_table = [tile("v_table%d" % j, [P, T], F32) for j in range(PACK)]
-        m_raw = [tile("m_raw%d" % h, [P, PACK, D], F32) for h in range(HALVES)]
+        m_raw = [[tile("m_raw%d%d" % (u, h), [P, PACK, D // 2], F32) for h in range(HALVES)] for u in range(2)]
         wt_rows = tile("wt_rows", [P, HALF], F32)
         identity = tile("identity", [P, P], F32)
         windows = [tile("window%d" % j, [P, T], F32) for j in range(WINDOWS)]
@@ -66,8 +70,10 @@ def tile_attend_ghv_nce_kernel(tc, xT, w_words, w_scales, vT, wt, xm, offs, out)
         v_rows = vT.rearrange("(p j) c -> p j c", j=PACK)
         for j in range(PACK):
             nc.sync.dma_start(v_table[j][:], v_rows[:, j, :])
-        for h in range(HALVES):
-            nc.sync.dma_start(m_raw[h][:], xm[0][h * HALF : (h + 1) * HALF, :].rearrange("(p t) d -> p t d", t=PACK))
+        for u in range(2):
+            for h in range(HALVES):
+                rows = xm[0][h * HALF : (h + 1) * HALF, u * D // 2 : (u + 1) * D // 2]
+                nc.sync.dma_start(m_raw[u][h][:], rows.rearrange("(p t) d -> p t d", t=PACK))
 
         zero_on_vector(windows[0][:].bitcast(I32))
         zero_on_vector(windows[1][:, :VECTOR_SHARE].bitcast(I32))
@@ -96,13 +102,13 @@ def tile_attend_ghv_nce_kernel(tc, xT, w_words, w_scales, vT, wt, xm, offs, out)
             nc.vector.quantize_mx(x_codes[h][:, cols].bitcast(E4M3), x_bytes[h][:, cols],
                                   x_bf[h][:, t0 * P * PACK : t1 * P * PACK])
 
-        g_bf = [tile("g_bf%d" % h, [P, N * PACK], BF16) for h in range(HALVES)]
         g_codes = [tile("g_codes%d" % h, [P, N], U32) for h in range(HALVES)]
         g_bytes = [tile("g_bytes%d" % h, [P, N], U8) for h in range(HALVES)]
         hn = N // 2
 
-        nc.vector.memset(g_codes[1][:, hn:].bitcast(I32), 0)
-        nc.vector.memset(g_bytes[1][:, hn:].bitcast(I32), 0)
+        for h in range(HALVES):
+            nc.vector.memset(g_codes[h][:, hn:].bitcast(I32), 0)
+            nc.vector.memset(g_bytes[h][:, hn:].bitcast(I32), 0)
         cast_x(0, 0, 2)
         quant_x(0, 0, 2)
         cast_x(0, 2, 4)
@@ -122,8 +128,8 @@ def tile_attend_ghv_nce_kernel(tc, xT, w_words, w_scales, vT, wt, xm, offs, out)
 
         th = [tile("th%d" % h, [P, PACK, N], F32) for h in range(HALVES)]
         sq = [tile("sq%d" % h, [P, PACK, N], F32) for h in range(HALVES)]
-        factor = [tile("factor%d" % h, [P, PACK, N], F32) for h in range(HALVES)]
-        v_bf = tile("v_bf", [P, N, PACK], BF16)
+        factor = tile("factor", [P, HALVES, PACK, N], F32)
+        v_bf = placed("v_bf", [P, N, PACK], BF16, 0)
 
         def score(h, t):
             a = ps.tile([P, N], F32, name="wide")
@@ -137,9 +143,9 @@ def tile_attend_ghv_nce_kernel(tc, xT, w_words, w_scales, vT, wt, xm, offs, out)
         def affine(h, t):
             c, mc = quarter[:, h, t : t + 1], minus_quarter[:, h, t : t + 1]
             if h == 0:
-                nc.vector.tensor_scalar(factor[h][:, t, :], sq[h][:, t, :], mc, c, ALU.mult, ALU.add)
+                nc.vector.tensor_scalar(factor[:, h, t, :], sq[h][:, t, :], mc, c, ALU.mult, ALU.add)
             else:
-                nc.scalar.activation(factor[h][:, t, :], sq[h][:, t, :], ACT.Identity, bias=c, scale=mc)
+                nc.scalar.activation(factor[:, h, t, :], sq[h][:, t, :], ACT.Identity, bias=c, scale=mc)
 
         for h in range(HALVES):
             for t in range(PACK):
@@ -164,96 +170,111 @@ def tile_attend_ghv_nce_kernel(tc, xT, w_words, w_scales, vT, wt, xm, offs, out)
             nc.vector.quantize_mx(v_codes[:, cols].bitcast(E4M3), v_bytes[:, cols],
                                   v_bf[:, cols, :].rearrange("p n j -> p (n j)"))
 
-        m_bf = [tile("m_bf%d" % h, [P, D * PACK], BF16) for h in range(HALVES)]
-        m_codes = [tile("m_codes%d" % h, [P, D], U32) for h in range(HALVES)]
-        m_bytes = [tile("m_bytes%d" % h, [P, D], U8) for h in range(HALVES)]
-
-        def cast_m(h, j0, j1):
-            nc.scalar.activation(
-                m_bf[h][:, j0 * P * PACK : j1 * P * PACK].rearrange("p (c i t) -> p c t i", i=4, t=PACK),
-                m_raw[h][:, :, j0 * P : j1 * P].rearrange("p t (c i) -> p c t i", i=4),
-                ACT.Copy,
-            )
-
-        def quant_m(h, j0, j1):
-            cols = slice(j0 * P, j1 * P)
-            nc.vector.quantize_mx(m_codes[h][:, cols].bitcast(E4M3), m_bytes[h][:, cols],
-                                  m_bf[h][:, j0 * P * PACK : j1 * P * PACK])
-
-        cast_m(0, 0, 4)
-        cast_m(1, 0, 1)
-        cast_m(1, 1, 2)
-        cast_m(1, 2, 4)
-
-        def direction(h, b):
+        def direction(h, b, tag):
             cols = slice(b * P, (b + 1) * P)
-            av = ps.tile([P, PACK, P], F32, name="av")
+            av = ps.tile([P, PACK, P], F32, name=tag)
             for t in range(PACK):
                 nc.tensor.matmul_mx(av[:, t, :], rhs=v_codes[:, cols].bitcast(E4M3), rhs_scale=v_bytes[:, cols],
                                     start=True, stop=True, **stationary(x_codes[h], x_bytes[h], t))
             return av
 
-        def product(h, b, av):
-            cols = slice(b * P, (b + 1) * P)
+        def product(g_block, h, b, av):
             nc.vector.tensor_tensor(
-                g_bf[h][:, b * P * PACK : (b + 1) * P * PACK].rearrange("p (c i t) -> p c t i", i=2, t=PACK),
+                g_block.rearrange("p (c i t) -> p c t i", i=2, t=PACK),
                 av[:].rearrange("p t (c i) -> p c t i", i=2),
-                factor[h][:, :, cols].rearrange("p t (c i) -> p c t i", i=2),
+                factor[:, h, :, b * P : (b + 1) * P].rearrange("p t (c i) -> p c t i", i=2),
                 ALU.mult,
             )
 
-        def quant_g(h, b0, b1):
-            cols = slice(b0 * P, b1 * P)
-            nc.vector.quantize_mx(g_codes[h][:, cols].bitcast(E5M2), g_bytes[h][:, cols],
-                                  g_bf[h][:, b0 * P * PACK : b1 * P * PACK])
+        def quant_g(h, s, g_half):
+            cols = slice(s * hn, (s + 1) * hn)
+            nc.vector.quantize_mx(g_codes[h][:, cols].bitcast(E5M2), g_bytes[h][:, cols], g_half)
 
-        sums = [ps.tile([P, N], F32, name="wide") for j in range(D_BLOCKS)]
+        def cast_m(m_bf, u, h, j):
+            nc.scalar.activation(
+                m_bf[:, j, h, :].rearrange("p (c i t) -> p c t i", i=4, t=PACK),
+                m_raw[u][h][:, :, j * P : (j + 1) * P].rearrange("p t (c i) -> p c t i", i=4),
+                ACT.Copy,
+            )
 
-        def dw_pass(bank, h, j):
-            nc.tensor.matmul_mx(bank[:], rhs=g_codes[h][:].bitcast(E5M2), rhs_scale=g_bytes[h][:],
-                                start=(h == 0), stop=(h == HALVES - 1), **stationary(m_codes[h], m_bytes[h], j))
+        def quant_m(codes, scale_bytes, m_bf, j0, j1):
+            cols = slice(j0 * HALVES * P, j1 * HALVES * P)
+            nc.vector.quantize_mx(codes[:, cols].bitcast(E4M3), scale_bytes[:, cols],
+                                  m_bf[:, j0:j1].rearrange("p j h n -> p (j h n)"))
 
-        gather_last(0, hn + 32)
+        gather_last(0, hn)
         quant_v(0)
         gather_last(hn, N)
         quant_v(1)
-        for b in range(SLOT_BLOCKS):
-            product(0, b, direction(0, b))
-        product(1, 0, direction(1, 0))
-        quant_g(0, 0, 4)
-        product(1, 1, direction(1, 1))
-        late = [direction(1, b) for b in (2, 3)]
-        quant_m(0, 0, 4)
-        quant_m(1, 0, 1)
-        quant_g(1, 0, 2)
 
+        block = P * PACK
+        first_av = [[direction(h, b, "av") for b in range(2)] for h in range(HALVES)]
+        last_av = [direction(h, 3, "wide") for h in range(HALVES)]
+        third_av = [direction(h, 2, "wide") for h in range(HALVES)]
+
+        m_bf_a = placed("m_bf_a", [P, 2, HALVES, block], BF16, 0)
+        for j in range(2):
+            cast_m(m_bf_a, 0, 0, j)
+        nc.gpsimd.tensor_scalar(m_bf_a[:, :, 1, :].rearrange("p j (c t) -> p j c t", t=PACK),
+                                m_raw[0][1][:].rearrange("p t (j c) -> p j c t", j=2), 1.0, 0.0, ALU.mult, ALU.add)
+        av_words = placed("av_words", [P, HALVES, P, PACK], F32, 6144)
+        for h in range(HALVES):
+            nc.scalar.activation(av_words[:, h], last_av[h][:].rearrange("p t n -> p n t"), ACT.Copy)
+
+        g_first = [tile("g_first0", [P, 2 * block], BF16), placed("g_first1", [P, 2 * block], BF16, 4096)]
+        m_codes = [tile("m_codes_a", [P, HALVES * 2 * P], U32)]
+        m_bytes = [tile("m_bytes_a", [P, HALVES * 2 * P], U8), tile("m_bytes_b", [P, HALVES * 2 * P], U8)]
+        product(g_first[0][:, :block], 0, 0, first_av[0][0])
+        product(g_first[0][:, block:], 0, 1, first_av[0][1])
+        product(g_first[1][:, :block], 1, 0, first_av[1][0])
+        quant_g(0, 0, g_first[0][:])
+        product(g_first[1][:, block:], 1, 1, first_av[1][1])
+        quant_m(m_codes[0], m_bytes[0], m_bf_a, 0, 1)
+        quant_g(1, 0, g_first[1][:])
+        quant_m(m_codes[0], m_bytes[0], m_bf_a, 1, 2)
+
+        def dw_pass(bank, h, j):
+            nc.tensor.matmul_mx(bank[:], rhs=g_codes[h][:].bitcast(E5M2), rhs_scale=g_bytes[h][:],
+                                start=(h == 0), stop=(h == HALVES - 1),
+                                **stationary(m_codes[j // 2], m_bytes[j // 2], HALVES * (j % 2) + h))
+
+        def scatter(j, cols, values):
+            nc.vector.tensor_copy(windows[j % WINDOWS][:].indirect(offsets[:, cols.start // 16 : cols.stop // 16]), values)
+
+        early = [ps.tile([P, N], F32, name="av") for j in range(2)]
+        for j in range(2):
+            for h in range(HALVES):
+                dw_pass(early[j], h, j)
         staged = [tile("staged%d" % j, [P, N], F32) for j in range(D_BLOCKS)]
-        early = ps.tile([P, N], F32, name="av")
-        dw_pass(early, 0, 0)
-        dw_pass(early, 1, 0)
-        nc.scalar.activation(staged[0][:, :hn], early[:, :hn], ACT.Copy)
-        product(1, 2, late[0])
-        product(1, 3, late[1])
+        for j in range(2):
+            nc.scalar.activation(staged[j][:, :hn], early[j][:, :hn], ACT.Copy)
+
+        g_second = placed("g_second", [P, HALVES, 2 * block], BF16, 2048)
+        nc.gpsimd.tensor_tensor(g_second[:, :, block:].rearrange("p h (n t) -> p h n t", t=PACK), av_words[:],
+                                factor[:, :, :, N - P :].rearrange("p h t n -> p h n t"), ALU.mult)
+        for h in range(HALVES):
+            product(g_second[:, h, :block], h, 2, third_av[h])
+        m_bf_b = tile("m_bf_b", [P, 2, HALVES, block], BF16)
+        for h in range(HALVES):
+            for j in range(2):
+                cast_m(m_bf_b, 1, h, j)
+
+        scatter(0, slice(0, hn), staged[0][:, :hn])
+        for h in range(HALVES):
+            quant_g(h, 1, g_second[:, h, :])
+        m_codes.append(placed("m_codes_b", [P, HALVES * 2 * P], U32, 6144))
+        quant_m(m_codes[1], m_bytes[1], m_bf_b, 0, 2)
+        scatter(1, slice(0, hn), staged[1][:, :hn])
+
         for j in range(D_BLOCKS):
-            dw_pass(sums[j], 0, j)
-        quant_m(1, 1, 2)
-        quant_g(1, 2, 4)
-        quant_m(1, 2, 4)
-
-        window_of = [windows[0], windows[1], windows[2], windows[1]]
-
-        def scatter(j, cols):
-            nc.vector.tensor_copy(window_of[j][:].indirect(offsets[:, cols.start // 16 : cols.stop // 16]),
-                                  staged[j][:, cols])
-
-        scatter(0, slice(0, hn))
-        for j in (1, 0, 2, 3):
-            cols = slice(hn if j == 0 else 0, N)
-            dw_pass(sums[j], 1, j)
-            nc.scalar.activation(staged[j][:, cols], sums[j][:, cols], ACT.Copy)
-            scatter(j, cols)
+            cols = slice(hn if j < 2 else 0, N)
+            sums = ps.tile([P, N], F32, name="wide")
+            for h in range(HALVES):
+                dw_pass(sums, h, j)
+            nc.scalar.activation(staged[j][:, cols], sums[:, cols], ACT.Copy)
+            scatter(j, cols, staged[j][:, cols])
             if j < D_BLOCKS - 1:
-                nc.sync.dma_start(out[j * P : (j + 1) * P, :], window_of[j][:])
+                nc.sync.dma_start(out[j * P : (j + 1) * P, :], windows[j][:])
         rows = slice(D - P, D)
-        nc.sync.dma_start(out[rows, : T // 2], window_of[3][:, : T // 2])
-        nc.scalar.dma_start(out[rows, T // 2 :], window_of[3][:, T // 2 :])
+        nc.sync.dma_start(out[rows, : T // 2], windows[0][:, : T // 2])
+        nc.scalar.dma_start(out[rows, T // 2 :], windows[0][:, T // 2 :])

@@ -71,7 +71,7 @@ def tile_attend_ghv_nce_kernel(tc, xT, w_words, w_scales, vT, wt, xm, offs, out)
         for j in range(PACK):
             nc.sync.dma_start(v_table[j][:], v_rows[:, j, :])
         for u in range(2):
-            for h in range(HALVES):
+            for h in ((1, 0) if u == 0 else (0, 1)):
                 rows = xm[0][h * HALF : (h + 1) * HALF, u * D // 2 : (u + 1) * D // 2]
                 nc.sync.dma_start(m_raw[u][h][:], rows.rearrange("(p t) d -> p t d", t=PACK))
 
@@ -209,7 +209,7 @@ def tile_attend_ghv_nce_kernel(tc, xT, w_words, w_scales, vT, wt, xm, offs, out)
 
         block = P * PACK
         first_av = [[direction(h, b, "av") for b in range(2)] for h in range(HALVES)]
-        last_av = [direction(h, 3, "wide") for h in range(HALVES)]
+        last_av = {h: direction(h, 3, "wide") for h in (1, 0)}
         third_av = [direction(h, 2, "wide") for h in range(HALVES)]
 
         m_bf_a = placed("m_bf_a", [P, 2, HALVES, block], BF16, 0)
@@ -217,9 +217,10 @@ def tile_attend_ghv_nce_kernel(tc, xT, w_words, w_scales, vT, wt, xm, offs, out)
             cast_m(m_bf_a, 0, 0, j)
         nc.gpsimd.tensor_scalar(m_bf_a[:, :, 1, :].rearrange("p j (c t) -> p j c t", t=PACK),
                                 m_raw[0][1][:].rearrange("p t (j c) -> p j c t", j=2), 1.0, 0.0, ALU.mult, ALU.add)
-        av_words = placed("av_words", [P, HALVES, P, PACK], F32, 6144)
-        for h in range(HALVES):
-            nc.scalar.activation(av_words[:, h], last_av[h][:].rearrange("p t n -> p n t"), ACT.Copy)
+        av_words = placed("av_words", [P, HALVES, block], F32, 6144)
+        for h in (1, 0):
+            nc.scalar.activation(av_words[:, h, :].rearrange("p (c t i) -> p c t i", t=PACK, i=2),
+                                 last_av[h][:].rearrange("p t (c i) -> p c t i", i=2), ACT.Copy)
 
         g_first = [tile("g_first0", [P, 2 * block], BF16), placed("g_first1", [P, 2 * block], BF16, 4096)]
         m_codes = [tile("m_codes_a", [P, HALVES * 2 * P], U32)]
@@ -250,8 +251,10 @@ def tile_attend_ghv_nce_kernel(tc, xT, w_words, w_scales, vT, wt, xm, offs, out)
             nc.scalar.activation(staged[j][:, :hn], early[j][:, :hn], ACT.Copy)
 
         g_second = placed("g_second", [P, HALVES, 2 * block], BF16, 2048)
-        nc.gpsimd.tensor_tensor(g_second[:, :, block:].rearrange("p h (n t) -> p h n t", t=PACK), av_words[:],
-                                factor[:, :, :, N - P :].rearrange("p h t n -> p h n t"), ALU.mult)
+        for h in (1, 0):
+            nc.gpsimd.tensor_tensor(g_second[:, h, block:].rearrange("p (c i t) -> p c t i", i=2, t=PACK),
+                                    av_words[:, h, :].rearrange("p (c t i) -> p c t i", t=PACK, i=2),
+                                    factor[:, h, :, N - P :].rearrange("p t (c i) -> p c t i", i=2), ALU.mult)
         for h in range(HALVES):
             product(g_second[:, h, :block], h, 2, third_av[h])
         m_bf_b = tile("m_bf_b", [P, 2, HALVES, block], BF16)

@@ -45,7 +45,8 @@ def tile_attend_ghv_nce_kernel(tc, xT, w_words, w_scales, vT, wt, xm, offs, out)
         s_table = tile("s_table", [P, T], U8)
         x_raw = [tile("x_raw%d" % h, [P, PACK, HALF], F32) for h in range(HALVES)]
         v_table = [tile("v_table%d" % j, [P, T], F32) for j in range(PACK)]
-        m_raw = [[tile("m_raw%d%d" % (u, h), [P, PACK, D // 2], F32) for h in range(HALVES)] for u in range(2)]
+        m_raw = [[placed("m_raw00", [P, PACK, D // 2], F32, 6144), tile("m_raw01", [P, PACK, D // 2], F32)],
+                 [tile("m_raw1%d" % h, [P, PACK, D // 2], F32) for h in range(HALVES)]]
         wt_rows = tile("wt_rows", [P, HALF], F32)
         identity = tile("identity", [P, P], F32)
         windows = [tile("window%d" % j, [P, T], F32) for j in range(WINDOWS)]

@@ -43,7 +43,7 @@ def tile_attend_ghv_nce_kernel(tc, xT, w_words, w_scales, vT, wt, xm, offs, out)
         offsets = sb.tile([P, N // 16], U16, name="offsets")
         w_table = tile("w_table", [P, T], U32)
         s_table = tile("s_table", [P, T], U8)
-        x_raw = [tile("x_raw%d" % h, [P, PACK, HALF], F32) for h in range(HALVES)]
+        x_raw = [tile("x_raw%d" % u, [P, 2, R], F32) for u in range(2)]
         v_table = [tile("v_table%d" % j, [P, T], F32) for j in range(PACK)]
         m_raw = [[placed("m_raw00", [P, PACK, D // 2], F32, 6144), tile("m_raw01", [P, PACK, D // 2], F32)],
                  [tile("m_raw1%d" % h, [P, PACK, D // 2], F32) for h in range(HALVES)]]
@@ -65,9 +65,9 @@ def tile_attend_ghv_nce_kernel(tc, xT, w_words, w_scales, vT, wt, xm, offs, out)
         for i in range(4):
             nc.sync.dma_start(s_table[i:P:32, :].bitcast(I32), w_scales[0][i:16:4, :].bitcast(I32))
         x_rows = xT[0].rearrange("(p j) r -> p j r", j=PACK)
-        nc.sync.dma_start(x_raw[0][:], x_rows[:, :, :HALF])
+        nc.sync.dma_start(x_raw[0][:], x_rows[:, :2, :])
         nc.sync.dma_start(wt_rows[16:P:64, :], wt[0].rearrange("(h r) o -> h (r o)", h=HALVES))
-        nc.sync.dma_start(x_raw[1][:], x_rows[:, :, HALF:])
+        nc.sync.dma_start(x_raw[1][:], x_rows[:, 2:, :])
         v_rows = vT.rearrange("(p j) c -> p j c", j=PACK)
         for j in range(PACK):
             nc.sync.dma_start(v_table[j][:], v_rows[:, j, :])
@@ -92,10 +92,10 @@ def tile_attend_ghv_nce_kernel(tc, xT, w_words, w_scales, vT, wt, xm, offs, out)
         quarter = tile("quarter", [P, HALVES, PACK], F32)
         minus_quarter = tile("minus_quarter", [P, HALVES, PACK], F32)
 
-        def cast_x(h, t0, t1):
+        def cast_x(u, h, t0, t1):
             nc.vector.tensor_copy(
-                x_bf[h][:].rearrange("p (t m j) -> p m j t", t=PACK, j=PACK)[:, :, :, t0:t1],
-                x_raw[h][:].rearrange("p j (m t) -> p m j t", t=PACK)[:, :, :, t0:t1],
+                x_bf[h][:].rearrange("p (t m j) -> p m j t", t=PACK, j=PACK)[:, :, 2 * u : 2 * u + 2, t0:t1],
+                x_raw[u][:, :, h * HALF : (h + 1) * HALF].rearrange("p j (m t) -> p m j t", t=PACK)[:, :, :, t0:t1],
             )
 
         def quant_x(h, t0, t1):
@@ -110,17 +110,19 @@ def tile_attend_ghv_nce_kernel(tc, xT, w_words, w_scales, vT, wt, xm, offs, out)
         for h in range(HALVES):
             nc.vector.memset(g_codes[h][:, hn:].bitcast(I32), 0)
             nc.vector.memset(g_bytes[h][:, hn:].bitcast(I32), 0)
-        cast_x(0, 0, 2)
-        quant_x(0, 0, 2)
-        cast_x(0, 2, 4)
-        quant_x(0, 2, 4)
-        cast_x(1, 0, 4)
+        for h in range(HALVES):
+            cast_x(0, h, 0, 4)
         wt_turned = ps.tile([P, PACK, P], F32, name="av")
         for t in range(PACK):
             nc.tensor.transpose(wt_turned[:, t, :], wt_rows[:, t:HALF:PACK], identity[:])
         wt_columns = wt_turned[:, :, 16:P:64].rearrange("p t h -> p h t")
         nc.vector.tensor_scalar(quarter[:], wt_columns, 0.25, None, ALU.mult)
         nc.vector.tensor_scalar(minus_quarter[:], wt_columns, -0.25, None, ALU.mult)
+        cast_x(1, 0, 0, 2)
+        quant_x(0, 0, 2)
+        cast_x(1, 0, 2, 4)
+        quant_x(0, 2, 4)
+        cast_x(1, 1, 0, 4)
         quant_x(1, 0, 4)
 
         def stationary(codes, scale_bytes, block):
@@ -143,22 +145,24 @@ def tile_attend_ghv_nce_kernel(tc, xT, w_words, w_scales, vT, wt, xm, offs, out)
 
         def affine(h, t):
             c, mc = quarter[:, h, t : t + 1], minus_quarter[:, h, t : t + 1]
-            if h == 0:
-                nc.vector.tensor_scalar(factor[:, h, t, :], sq[h][:, t, :], mc, c, ALU.mult, ALU.add)
+            if h == 0 or t < 2:
+                nc.gpsimd.tensor_scalar(factor[:, h, t, :], sq[h][:, t, :], mc, c, ALU.mult, ALU.add)
             else:
                 nc.scalar.activation(factor[:, h, t, :], sq[h][:, t, :], ACT.Identity, bias=c, scale=mc)
 
+        for t in range(PACK):
+            score(0, t)
+        square(0, 0, 2)
+        square(0, 2, 4)
+        for t0 in (0, 2):
+            score(1, t0)
+            score(1, t0 + 1)
+            square(1, t0, t0 + 2)
         for h in range(HALVES):
             for t in range(PACK):
-                score(h, t)
-            square(h, 0, 2)
-            square(h, 2, 4)
-        for t in range(PACK):
-            affine(1, t)
+                affine(h, t)
         for j in range(PACK - 1):
             nc.vector.tensor_copy(v_bf[:, :, j], v_table[j][:].indirect(offsets[:]))
-            for t in range(2 * j, min(2 * j + 2, PACK)):
-                affine(0, t)
 
         v_codes = tile("v_codes", [P, N], U32)
         v_bytes = tile("v_bytes", [P, N], U8)

@@ -24,7 +24,6 @@ HALVES = R // HALF
 SLOT_BLOCKS = N // P
 D_BLOCKS = D // P
 WINDOWS = 3
-VECTOR_SHARE = 768
 
 
 def tile_attend_ghv_nce_kernel(tc, xT, w_words, w_scales, vT, wt, xm, offs, out):
@@ -77,16 +76,15 @@ def tile_attend_ghv_nce_kernel(tc, xT, w_words, w_scales, vT, wt, xm, offs, out)
                 nc.sync.dma_start(m_raw[u][h][:], rows.rearrange("(p t) d -> p t d", t=PACK))
 
         zero_on_vector(windows[0][:].bitcast(I32))
-        zero_on_vector(windows[1][:, :VECTOR_SHARE].bitcast(I32))
-        nc.gpsimd.memset(windows[1][:, VECTOR_SHARE:].bitcast(I32), 0)
-        nc.gpsimd.memset(windows[2][:].bitcast(I32), 0)
+        for window in windows[1:]:
+            nc.gpsimd.memset(window[:].bitcast(I32), 0)
 
         w_codes = tile("w_codes", [P, N], U32)
         w_bytes = tile("w_bytes", [P, N], U8)
         nc.vector.tensor_copy(w_codes[:], w_table[:].indirect(offsets[:]))
         nc.vector.tensor_copy(w_bytes[:], s_table[:].indirect(offsets[:]))
 
-        x_bf = [tile("x_bf%d" % h, [P, HALF * PACK], BF16) for h in range(HALVES)]
+        x_bf = [tile("x_bf0", [P, HALF * PACK], BF16), placed("x_bf1", [P, HALF * PACK], BF16, 10240)]
         x_codes = [tile("x_codes%d" % h, [P, HALF], U32) for h in range(HALVES)]
         x_bytes = [tile("x_bytes%d" % h, [P, HALF], U8) for h in range(HALVES)]
         quarter = tile("quarter", [P, HALVES, PACK], F32)
@@ -108,8 +106,8 @@ def tile_attend_ghv_nce_kernel(tc, xT, w_words, w_scales, vT, wt, xm, offs, out)
         hn = N // 2
 
         for h in range(HALVES):
-            nc.vector.memset(g_codes[h][:, hn:].bitcast(I32), 0)
-            nc.vector.memset(g_bytes[h][:, hn:].bitcast(I32), 0)
+            nc.gpsimd.memset(g_codes[h][:, hn:].bitcast(I32), 0)
+            nc.gpsimd.memset(g_bytes[h][:, hn:].bitcast(I32), 0)
         for h in range(HALVES):
             cast_x(0, h, 0, 4)
         wt_turned = ps.tile([P, PACK, P], F32, name="av")
@@ -118,12 +116,12 @@ def tile_attend_ghv_nce_kernel(tc, xT, w_words, w_scales, vT, wt, xm, offs, out)
         wt_columns = wt_turned[:, :, 16:P:64].rearrange("p t h -> p h t")
         nc.vector.tensor_scalar(quarter[:], wt_columns, 0.25, None, ALU.mult)
         nc.vector.tensor_scalar(minus_quarter[:], wt_columns, -0.25, None, ALU.mult)
-        cast_x(1, 0, 0, 2)
-        quant_x(0, 0, 2)
-        cast_x(1, 0, 2, 4)
-        quant_x(0, 2, 4)
-        cast_x(1, 1, 0, 4)
-        quant_x(1, 0, 4)
+        pieces = [(0, 0, 1), (0, 1, 3), (0, 3, 4), (1, 0, 2), (1, 2, 4)]
+        cast_x(1, *pieces[0])
+        for done, ahead in zip(pieces, pieces[1:]):
+            cast_x(1, *ahead)
+            quant_x(*done)
+        quant_x(*pieces[-1])
 
         def stationary(codes, scale_bytes, block):
             cols = slice(block * P, (block + 1) * P)
@@ -146,18 +144,22 @@ def tile_attend_ghv_nce_kernel(tc, xT, w_words, w_scales, vT, wt, xm, offs, out)
         def affine(h, t):
             c, mc = quarter[:, h, t : t + 1], minus_quarter[:, h, t : t + 1]
             if h == 0 or t < 2:
-                nc.gpsimd.tensor_scalar(factor[:, h, t, :], sq[h][:, t, :], mc, c, ALU.mult, ALU.add)
+                squared = sq_first[:] if (h, t) == (0, 0) else sq[h][:, t, :]
+                nc.gpsimd.tensor_scalar(factor[:, h, t, :], squared, mc, c, ALU.mult, ALU.add)
             else:
                 nc.scalar.activation(factor[:, h, t, :], sq[h][:, t, :], ACT.Identity, bias=c, scale=mc)
 
         for t in range(PACK):
             score(0, t)
-        square(0, 0, 2)
+        sq_first = placed("sq_first", [P, N], F32, 12288)
+        nc.gpsimd.tensor_tensor(sq_first[:], th[0][:, 0, :], th[0][:, 0, :], ALU.mult)
+        square(0, 1, 2)
         square(0, 2, 4)
         for t0 in (0, 2):
             score(1, t0)
             score(1, t0 + 1)
-            square(1, t0, t0 + 2)
+            square(1, t0, t0 + 1)
+            square(1, t0 + 1, t0 + 2)
         for h in range(HALVES):
             for t in range(PACK):
                 affine(h, t)

@@ -96,6 +96,12 @@ def tile_attend_ghv_nce_kernel(tc, xT, w_words, w_scales, vT, wt, xm, offs, out)
                 x_raw[u][:, :, h * HALF : (h + 1) * HALF].rearrange("p j (m t) -> p m j t", t=PACK)[:, :, :, t0:t1],
             )
 
+        def cast_x_on_scalar(u):
+            nc.scalar.copy(
+                x_bf[1][:].rearrange("p (t m i j) -> p m t i j", t=PACK, i=2, j=PACK)[:, :, :, :, 2 * u : 2 * u + 2],
+                x_raw[u][:, :, HALF:].rearrange("p j (m i t) -> p m t i j", i=2, t=PACK),
+            )
+
         def quant_x(h, t0, t1):
             cols = slice(t0 * P, t1 * P)
             nc.vector.quantize_mx(x_codes[h][:, cols].bitcast(E4M3), x_bytes[h][:, cols],
@@ -108,20 +114,22 @@ def tile_attend_ghv_nce_kernel(tc, xT, w_words, w_scales, vT, wt, xm, offs, out)
         for h in range(HALVES):
             nc.gpsimd.memset(g_codes[h][:, hn:].bitcast(I32), 0)
             nc.gpsimd.memset(g_bytes[h][:, hn:].bitcast(I32), 0)
-        for h in range(HALVES):
-            cast_x(0, h, 0, 4)
+        cast_x(0, 0, 0, 4)
+        for u in range(2):
+            cast_x_on_scalar(u)
         wt_turned = ps.tile([P, PACK, P], F32, name="av")
         for t in range(PACK):
             nc.tensor.transpose(wt_turned[:, t, :], wt_rows[:, t:HALF:PACK], identity[:])
         wt_columns = wt_turned[:, :, 16:P:64].rearrange("p t h -> p h t")
         nc.vector.tensor_scalar(quarter[:], wt_columns, 0.25, None, ALU.mult)
         nc.vector.tensor_scalar(minus_quarter[:], wt_columns, -0.25, None, ALU.mult)
-        pieces = [(0, 0, 1), (0, 1, 3), (0, 3, 4), (1, 0, 2), (1, 2, 4)]
+        pieces = [(0, 0, 1), (0, 1, 3), (0, 3, 4)]
         cast_x(1, *pieces[0])
         for done, ahead in zip(pieces, pieces[1:]):
             cast_x(1, *ahead)
             quant_x(*done)
         quant_x(*pieces[-1])
+        quant_x(1, 0, 4)
 
         def stationary(codes, scale_bytes, block):
             cols = slice(block * P, (block + 1) * P)

@@ -291,8 +291,4 @@ def tile_attend_ghv_nce_kernel(tc, xT, w_words, w_scales, vT, wt, xm, offs, out)
                 dw_pass(sums, h, j)
             nc.scalar.activation(staged[j][:, cols], sums[:, cols], ACT.Copy)
             scatter(j, cols, staged[j][:, cols])
-            if j < D_BLOCKS - 1:
-                nc.sync.dma_start(out[j * P : (j + 1) * P, :], windows[j][:])
-        rows = slice(D - P, D)
-        nc.sync.dma_start(out[rows, : T // 2], windows[0][:, : T // 2])
-        nc.scalar.dma_start(out[rows, T // 2 :], windows[0][:, T // 2 :])
+            nc.sync.dma_start(out[j * P : (j + 1) * P, :], windows[j % WINDOWS][:])

@@ -23,7 +23,8 @@ HALF = P * PACK
 HALVES = R // HALF
 SLOT_BLOCKS = N // P
 D_BLOCKS = D // P
-WINDOWS = 3
+WINDOWS = 4
+EARLY = 3
 
 
 def tile_attend_ghv_nce_kernel(tc, xT, w_words, w_scales, vT, wt, xm, offs, out):
@@ -44,8 +45,9 @@ def tile_attend_ghv_nce_kernel(tc, xT, w_words, w_scales, vT, wt, xm, offs, out)
         s_table = tile("s_table", [P, T], U8)
         x_raw = [tile("x_raw%d" % u, [P, 2, R], F32) for u in range(2)]
         v_table = [tile("v_table%d" % j, [P, T], F32) for j in range(PACK)]
-        m_raw = [[placed("m_raw00", [P, PACK, D // 2], F32, 6144), tile("m_raw01", [P, PACK, D // 2], F32)],
-                 [tile("m_raw1%d" % h, [P, PACK, D // 2], F32) for h in range(HALVES)]]
+        m_raw = [[placed("m_raw00", [P, PACK, 2 * P], F32, 8192), tile("m_raw01", [P, PACK, 2 * P], F32)],
+                 [placed("m_raw10", [P, PACK, P], F32, 12288), tile("m_raw11", [P, PACK, P], F32)],
+                 [tile("m_raw2%d" % h, [P, PACK, P], F32) for h in range(HALVES)]]
         wt_rows = tile("wt_rows", [P, HALF], F32)
         identity = tile("identity", [P, P], F32)
         windows = [tile("window%d" % j, [P, T], F32) for j in range(WINDOWS)]
@@ -70,9 +72,9 @@ def tile_attend_ghv_nce_kernel(tc, xT, w_words, w_scales, vT, wt, xm, offs, out)
         v_rows = vT.rearrange("(p j) c -> p j c", j=PACK)
         for j in range(PACK):
             nc.sync.dma_start(v_table[j][:], v_rows[:, j, :])
-        for u in range(2):
-            for h in ((1, 0) if u == 0 else (0, 1)):
-                rows = xm[0][h * HALF : (h + 1) * HALF, u * D // 2 : (u + 1) * D // 2]
+        for u, (d0, d1) in enumerate(((0, 2 * P), (2 * P, 3 * P), (3 * P, D))):
+            for h in (1, 0):
+                rows = xm[0][h * HALF : (h + 1) * HALF, d0:d1]
                 nc.sync.dma_start(m_raw[u][h][:], rows.rearrange("(p t) d -> p t d", t=PACK))
 
         zero_on_vector(windows[0][:].bitcast(I32))
@@ -84,7 +86,7 @@ def tile_attend_ghv_nce_kernel(tc, xT, w_words, w_scales, vT, wt, xm, offs, out)
         nc.vector.tensor_copy(w_codes[:], w_table[:].indirect(offsets[:]))
         nc.vector.tensor_copy(w_bytes[:], s_table[:].indirect(offsets[:]))
 
-        x_bf = [tile("x_bf0", [P, HALF * PACK], BF16), placed("x_bf1", [P, HALF * PACK], BF16, 10240)]
+        x_bf = [tile("x_bf0", [P, HALF * PACK], BF16), placed("x_bf1", [P, HALF * PACK], BF16, 16384)]
         x_codes = [tile("x_codes%d" % h, [P, HALF], U32) for h in range(HALVES)]
         x_bytes = [tile("x_bytes%d" % h, [P, HALF], U8) for h in range(HALVES)]
         quarter = tile("quarter", [P, HALVES, PACK], F32)
@@ -159,7 +161,7 @@ def tile_attend_ghv_nce_kernel(tc, xT, w_words, w_scales, vT, wt, xm, offs, out)
 
         for t in range(PACK):
             score(0, t)
-        sq_first = placed("sq_first", [P, N], F32, 12288)
+        sq_first = placed("sq_first", [P, N], F32, 18432)
         nc.gpsimd.tensor_tensor(sq_first[:], th[0][:, 0, :], th[0][:, 0, :], ALU.mult)
         square(0, 1, 2)
         square(0, 2, 4)
@@ -205,12 +207,9 @@ def tile_attend_ghv_nce_kernel(tc, xT, w_words, w_scales, vT, wt, xm, offs, out)
             cols = slice(s * hn, (s + 1) * hn)
             nc.vector.quantize_mx(g_codes[h][:, cols].bitcast(E5M2), g_bytes[h][:, cols], g_half)
 
-        def cast_m(m_bf, u, h, j):
-            nc.scalar.activation(
-                m_bf[:, j, h, :].rearrange("p (c i t) -> p c t i", i=4, t=PACK),
-                m_raw[u][h][:, :, j * P : (j + 1) * P].rearrange("p t (c i) -> p c t i", i=4),
-                ACT.Copy,
-            )
+        def cast_m(m_half, raw):
+            nc.scalar.activation(m_half.rearrange("p (c i t) -> p c t i", i=4, t=PACK),
+                                 raw.rearrange("p t (c i) -> p c t i", i=4), ACT.Copy)
 
         def quant_m(codes, scale_bytes, m_bf, j0, j1):
             cols = slice(j0 * HALVES * P, j1 * HALVES * P)
@@ -224,71 +223,84 @@ def tile_attend_ghv_nce_kernel(tc, xT, w_words, w_scales, vT, wt, xm, offs, out)
 
         block = P * PACK
         first_av = [[direction(h, b, "av") for b in range(2)] for h in range(HALVES)]
-        last_av = {h: direction(h, 3, "wide") for h in (1, 0)}
-        third_av = [direction(h, 2, "wide") for h in range(HALVES)]
+        late_blocks = [(1, 3), (0, 3), (1, 2)]
+        late_av = [direction(h, b, "wide") for h, b in late_blocks]
+        fill_av = direction(0, 2, "wide")
 
-        m_bf_a = placed("m_bf_a", [P, 2, HALVES, block], BF16, 0)
+        m_bf_a = placed("m_bf_a", [P, EARLY, HALVES, block], BF16, 0)
         for j in range(2):
-            cast_m(m_bf_a, 0, 0, j)
-        nc.gpsimd.tensor_scalar(m_bf_a[:, :, 1, :].rearrange("p j (c t) -> p j c t", t=PACK),
+            cast_m(m_bf_a[:, j, 0, :], m_raw[0][0][:, :, j * P : (j + 1) * P])
+        nc.gpsimd.tensor_scalar(m_bf_a[:, :2, 1, :].rearrange("p j (c t) -> p j c t", t=PACK),
                                 m_raw[0][1][:].rearrange("p t (j c) -> p j c t", j=2), 1.0, 0.0, ALU.mult, ALU.add)
-        av_words = placed("av_words", [P, HALVES, block], F32, 6144)
-        for h in (1, 0):
-            nc.scalar.activation(av_words[:, h, :].rearrange("p (c t i) -> p c t i", t=PACK, i=2),
-                                 last_av[h][:].rearrange("p t (c i) -> p c t i", i=2), ACT.Copy)
+        nc.gpsimd.tensor_scalar(m_bf_a[:, 2, 1, :].rearrange("p (c t) -> p c t", t=PACK),
+                                m_raw[1][1][:].rearrange("p t c -> p c t"), 1.0, 0.0, ALU.mult, ALU.add)
+        av_first = placed("av_first", [P, block], F32, 8192)
 
-        g_first = [tile("g_first0", [P, 2 * block], BF16), placed("g_first1", [P, 2 * block], BF16, 4096)]
-        m_codes = [tile("m_codes_a", [P, HALVES * 2 * P], U32)]
-        m_bytes = [tile("m_bytes_a", [P, HALVES * 2 * P], U8), tile("m_bytes_b", [P, HALVES * 2 * P], U8)]
-        product(g_first[0][:, :block], 0, 0, first_av[0][0])
-        product(g_first[0][:, block:], 0, 1, first_av[0][1])
-        product(g_first[1][:, :block], 1, 0, first_av[1][0])
+        def copy_av(words, av):
+            nc.scalar.activation(words.rearrange("p (c t i) -> p c t i", t=PACK, i=2),
+                                 av[:].rearrange("p t (c i) -> p c t i", i=2), ACT.Copy)
+
+        copy_av(av_first[:], late_av[0])
+        cast_m(m_bf_a[:, 2, 0, :], m_raw[1][0][:])
+        av_rest = placed("av_rest", [P, 2, block], F32, 12288)
+        for k in range(2):
+            copy_av(av_rest[:, k, :], late_av[1 + k])
+        av_words = [av_first[:], av_rest[:, 0, :], av_rest[:, 1, :]]
+
+        g_first = [tile("g_first0", [P, 2 * block], BF16), placed("g_first1", [P, 2 * block], BF16, 6144)]
+        m_codes = [tile("m_codes_a", [P, EARLY * HALVES * P], U32)]
+        m_bytes = [tile("m_bytes_a", [P, EARLY * HALVES * P], U8), tile("m_bytes_b", [P, HALVES * P], U8)]
+        for h in range(HALVES):
+            for b in range(2):
+                product(g_first[h][:, b * block : (b + 1) * block], h, b, first_av[h][b])
         quant_g(0, 0, g_first[0][:])
-        product(g_first[1][:, block:], 1, 1, first_av[1][1])
         quant_m(m_codes[0], m_bytes[0], m_bf_a, 0, 1)
         quant_g(1, 0, g_first[1][:])
         quant_m(m_codes[0], m_bytes[0], m_bf_a, 1, 2)
+        quant_m(m_codes[0], m_bytes[0], m_bf_a, 2, 3)
 
         def dw_pass(bank, h, j):
             nc.tensor.matmul_mx(bank[:], rhs=g_codes[h][:].bitcast(E5M2), rhs_scale=g_bytes[h][:],
                                 start=(h == 0), stop=(h == HALVES - 1),
-                                **stationary(m_codes[j // 2], m_bytes[j // 2], HALVES * (j % 2) + h))
+                                **stationary(m_codes[j // EARLY], m_bytes[j // EARLY], HALVES * (j % EARLY) + h))
 
         def scatter(j, cols, values):
-            nc.vector.tensor_copy(windows[j % WINDOWS][:].indirect(offsets[:, cols.start // 16 : cols.stop // 16]), values)
+            nc.vector.tensor_copy(windows[j][:].indirect(offsets[:, cols.start // 16 : cols.stop // 16]), values)
 
         early = [ps.tile([P, N], F32, name="av") for j in range(2)]
+        staged = [tile("staged%d" % j, [P, N], F32) for j in range(D_BLOCKS)]
         for j in range(2):
             for h in range(HALVES):
                 dw_pass(early[j], h, j)
-        staged = [tile("staged%d" % j, [P, N], F32) for j in range(D_BLOCKS)]
-        for j in range(2):
             nc.scalar.activation(staged[j][:, :hn], early[j][:, :hn], ACT.Copy)
-
-        g_second = placed("g_second", [P, HALVES, 2 * block], BF16, 2048)
-        for h in (1, 0):
-            nc.gpsimd.tensor_tensor(g_second[:, h, block:].rearrange("p (c i t) -> p c t i", i=2, t=PACK),
-                                    av_words[:, h, :].rearrange("p (c t i) -> p c t i", t=PACK, i=2),
-                                    factor[:, h, :, N - P :].rearrange("p t (c i) -> p c t i", i=2), ALU.mult)
         for h in range(HALVES):
-            product(g_second[:, h, :block], h, 2, third_av[h])
-        m_bf_b = tile("m_bf_b", [P, 2, HALVES, block], BF16)
-        for h in range(HALVES):
-            for j in range(2):
-                cast_m(m_bf_b, 1, h, j)
+            dw_pass(early[1], h, 2)
 
-        scatter(0, slice(0, hn), staged[0][:, :hn])
+        g_second = placed("g_second", [P, HALVES, 2 * block], BF16, 4096)
+        for k, (h, b) in enumerate(late_blocks):
+            nc.gpsimd.tensor_tensor(g_second[:, h, (b - 2) * block : (b - 1) * block].rearrange("p (c i t) -> p c t i", i=2, t=PACK),
+                                    av_words[k].rearrange("p (c t i) -> p c t i", t=PACK, i=2),
+                                    factor[:, h, :, b * P : (b + 1) * P].rearrange("p t (c i) -> p c t i", i=2), ALU.mult)
+        product(g_second[:, 0, :block], 0, 2, fill_av)
+        m_bf_b = tile("m_bf_b", [P, 1, HALVES, block], BF16)
+        for h in range(HALVES):
+            cast_m(m_bf_b[:, 0, h, :], m_raw[2][h][:])
+
+        for j in range(2):
+            scatter(j, slice(0, hn), staged[j][:, :hn])
+        staged_early = placed("staged_early", [P, hn], F32, 12288)
+        nc.scalar.activation(staged_early[:], early[1][:, :hn], ACT.Copy)
         for h in range(HALVES):
             quant_g(h, 1, g_second[:, h, :])
-        m_codes.append(placed("m_codes_b", [P, HALVES * 2 * P], U32, 6144))
-        quant_m(m_codes[1], m_bytes[1], m_bf_b, 0, 2)
-        scatter(1, slice(0, hn), staged[1][:, :hn])
+        m_codes.append(placed("m_codes_b", [P, HALVES * P], U32, 14336))
+        quant_m(m_codes[1], m_bytes[1], m_bf_b, 0, 1)
+        scatter(2, slice(0, hn), staged_early[:])
 
         for j in range(D_BLOCKS):
-            cols = slice(hn if j < 2 else 0, N)
+            cols = slice(hn if j < EARLY else 0, N)
             sums = ps.tile([P, N], F32, name="wide")
             for h in range(HALVES):
                 dw_pass(sums, h, j)
             nc.scalar.activation(staged[j][:, cols], sums[:, cols], ACT.Copy)
             scatter(j, cols, staged[j][:, cols])
-            nc.sync.dma_start(out[j * P : (j + 1) * P, :], windows[j % WINDOWS][:])
+            nc.sync.dma_start(out[j * P : (j + 1) * P, :], windows[j][:])

@@ -25,6 +25,7 @@ SLOT_BLOCKS = N // P
 D_BLOCKS = D // P
 WINDOWS = 4
 EARLY = 3
+KEPT = 32
 
 
 def tile_attend_ghv_nce_kernel(tc, xT, w_words, w_scales, vT, wt, xm, offs, out):
@@ -237,15 +238,15 @@ def tile_attend_ghv_nce_kernel(tc, xT, w_words, w_scales, vT, wt, xm, offs, out)
         av_first = placed("av_first", [P, block], F32, 8192)
 
         def copy_av(words, av):
-            nc.scalar.activation(words.rearrange("p (c t i) -> p c t i", t=PACK, i=2),
-                                 av[:].rearrange("p t (c i) -> p c t i", i=2), ACT.Copy)
+            nc.scalar.activation(words.rearrange("p (t c) -> p t c", t=PACK), av[:], ACT.Copy)
 
         copy_av(av_first[:], late_av[0])
         cast_m(m_bf_a[:, 2, 0, :], m_raw[1][0][:])
         av_rest = placed("av_rest", [P, 2, block], F32, 12288)
-        for k in range(2):
-            copy_av(av_rest[:, k, :], late_av[1 + k])
-        av_words = [av_first[:], av_rest[:, 0, :], av_rest[:, 1, :]]
+        copy_av(av_rest[:, 0, :], late_av[1])
+        nc.scalar.activation(av_rest[:, 1, KEPT * PACK :].rearrange("p (c t i) -> p c t i", t=PACK, i=2),
+                             late_av[2][:, :, KEPT:].rearrange("p t (c i) -> p c t i", i=2), ACT.Copy)
+        av_words = [av_first[:], av_rest[:, 0, :]]
 
         g_first = [tile("g_first0", [P, 2 * block], BF16), placed("g_first1", [P, 2 * block], BF16, 6144)]
         m_codes = [tile("m_codes_a", [P, EARLY * HALVES * P], U32)]
@@ -277,11 +278,19 @@ def tile_attend_ghv_nce_kernel(tc, xT, w_words, w_scales, vT, wt, xm, offs, out)
             dw_pass(early[1], h, 2)
 
         g_second = placed("g_second", [P, HALVES, 2 * block], BF16, 4096)
-        for k, (h, b) in enumerate(late_blocks):
-            nc.gpsimd.tensor_tensor(g_second[:, h, (b - 2) * block : (b - 1) * block].rearrange("p (c i t) -> p c t i", i=2, t=PACK),
-                                    av_words[k].rearrange("p (c t i) -> p c t i", t=PACK, i=2),
-                                    factor[:, h, :, b * P : (b + 1) * P].rearrange("p t (c i) -> p c t i", i=2), ALU.mult)
+        g_rows = placed("g_rows", [P, 2, PACK, P], BF16, 0)
+        for k, (h, b) in enumerate(late_blocks[:2]):
+            nc.gpsimd.tensor_tensor(g_rows[:, k], av_words[k].rearrange("p (t c) -> p t c", t=PACK),
+                                    factor[:, h, :, b * P : (b + 1) * P], ALU.mult)
+        nc.gpsimd.tensor_tensor(g_second[:, 1, KEPT * PACK : block].rearrange("p (c i t) -> p c t i", i=2, t=PACK),
+                                av_rest[:, 1, KEPT * PACK :].rearrange("p (c t i) -> p c t i", t=PACK, i=2),
+                                factor[:, 1, :, 2 * P + KEPT : 3 * P].rearrange("p t (c i) -> p c t i", i=2), ALU.mult)
+        for k, (h, b) in enumerate(late_blocks[:2]):
+            cast_m(g_second[:, h, block:], g_rows[:, k])
         product(g_second[:, 0, :block], 0, 2, fill_av)
+        nc.vector.tensor_tensor(g_second[:, 1, : KEPT * PACK].rearrange("p (c i t) -> p c t i", i=2, t=PACK),
+                                late_av[2][:, :, :KEPT].rearrange("p t (c i) -> p c t i", i=2),
+                                factor[:, 1, :, 2 * P : 2 * P + KEPT].rearrange("p t (c i) -> p c t i", i=2), ALU.mult)
         m_bf_b = tile("m_bf_b", [P, 1, HALVES, block], BF16)
         for h in range(HALVES):
             cast_m(m_bf_b[:, 0, h, :], m_raw[2][h][:])

@@ -155,16 +155,16 @@ def tile_attend_ghv_nce_kernel(tc, xT, w_words, w_scales, vT, wt, xm, offs, out)
         def affine(h, t):
             c, mc = quarter[:, h, t : t + 1], minus_quarter[:, h, t : t + 1]
             if h == 0 or t < 2:
-                squared = sq_first[:] if (h, t) == (0, 0) else sq[h][:, t, :]
+                squared = sq_first[:, t, :] if h == 0 and t < 2 else sq[h][:, t, :]
                 nc.gpsimd.tensor_scalar(factor[:, h, t, :], squared, mc, c, ALU.mult, ALU.add)
             else:
                 nc.scalar.activation(factor[:, h, t, :], sq[h][:, t, :], ACT.Identity, bias=c, scale=mc)
 
         for t in range(PACK):
             score(0, t)
-        sq_first = placed("sq_first", [P, N], F32, 18432)
-        nc.gpsimd.tensor_tensor(sq_first[:], th[0][:, 0, :], th[0][:, 0, :], ALU.mult)
-        square(0, 1, 2)
+        sq_first = placed("sq_first", [P, 2, N], F32, 16384)
+        for t in range(2):
+            nc.gpsimd.tensor_tensor(sq_first[:, t, :], th[0][:, t, :], th[0][:, t, :], ALU.mult)
         square(0, 2, 4)
         for t0 in (0, 2):
             score(1, t0)
@@ -229,12 +229,12 @@ def tile_attend_ghv_nce_kernel(tc, xT, w_words, w_scales, vT, wt, xm, offs, out)
         fill_av = direction(0, 2, "wide")
 
         m_bf_a = placed("m_bf_a", [P, EARLY, HALVES, block], BF16, 0)
+        cast_m(m_bf_a[:, 0, 1, :], m_raw[0][1][:, :, :P])
         for j in range(2):
             cast_m(m_bf_a[:, j, 0, :], m_raw[0][0][:, :, j * P : (j + 1) * P])
-        nc.gpsimd.tensor_scalar(m_bf_a[:, :2, 1, :].rearrange("p j (c t) -> p j c t", t=PACK),
-                                m_raw[0][1][:].rearrange("p t (j c) -> p j c t", j=2), 1.0, 0.0, ALU.mult, ALU.add)
-        nc.gpsimd.tensor_scalar(m_bf_a[:, 2, 1, :].rearrange("p (c t) -> p c t", t=PACK),
-                                m_raw[1][1][:].rearrange("p t c -> p c t"), 1.0, 0.0, ALU.mult, ALU.add)
+        for j, raw in ((1, m_raw[0][1][:, :, P:]), (2, m_raw[1][1][:])):
+            nc.gpsimd.tensor_scalar(m_bf_a[:, j, 1, :].rearrange("p (c t) -> p c t", t=PACK),
+                                    raw.rearrange("p t c -> p c t"), 1.0, 0.0, ALU.mult, ALU.add)
         av_first = placed("av_first", [P, block], F32, 8192)
 
         def copy_av(words, av):

@@ -25,7 +25,7 @@ SLOT_BLOCKS = N // P
 D_BLOCKS = D // P
 WINDOWS = 4
 EARLY = 3
-KEPT = 32
+KEPT = 64
 
 
 def tile_attend_ghv_nce_kernel(tc, xT, w_words, w_scales, vT, wt, xm, offs, out):
@@ -141,7 +141,8 @@ def tile_attend_ghv_nce_kernel(tc, xT, w_words, w_scales, vT, wt, xm, offs, out)
         th = [tile("th%d" % h, [P, PACK, N], F32) for h in range(HALVES)]
         sq = [tile("sq%d" % h, [P, PACK, N], F32) for h in range(HALVES)]
         factor = tile("factor", [P, HALVES, PACK, N], F32)
-        v_bf = placed("v_bf", [P, N, PACK], BF16, 0)
+        v_bf = placed("v_bf", [P, SLOT_BLOCKS, P, PACK], BF16, 4096)
+        v_place = (slice(0, 4, 3), slice(1, 3))
 
         def score(h, t):
             a = ps.tile([P, N], F32, name="wide")
@@ -174,19 +175,20 @@ def tile_attend_ghv_nce_kernel(tc, xT, w_words, w_scales, vT, wt, xm, offs, out)
         for h in range(HALVES):
             for t in range(PACK):
                 affine(h, t)
+
+        def gather_v(j, s):
+            nc.vector.tensor_copy(v_bf[:, v_place[s], :, j], v_table[j][:].indirect(offsets[:, s * hn // 16 : (s + 1) * hn // 16]))
+
         for j in range(PACK - 1):
-            nc.vector.tensor_copy(v_bf[:, :, j], v_table[j][:].indirect(offsets[:]))
+            for s in range(2):
+                gather_v(j, s)
 
         v_codes = tile("v_codes", [P, N], U32)
         v_bytes = tile("v_bytes", [P, N], U8)
 
-        def gather_last(n0, n1):
-            nc.vector.tensor_copy(v_bf[:, n0:n1, PACK - 1], v_table[PACK - 1][:].indirect(offsets[:, n0 // 16 : n1 // 16]))
-
-        def quant_v(s):
-            cols = slice(s * hn, (s + 1) * hn)
-            nc.vector.quantize_mx(v_codes[:, cols].bitcast(E4M3), v_bytes[:, cols],
-                                  v_bf[:, cols, :].rearrange("p n j -> p (n j)"))
+        def quant_v(b0, b1, places):
+            cols = slice(b0 * P, b1 * P)
+            nc.vector.quantize_mx(v_codes[:, cols].bitcast(E4M3), v_bytes[:, cols], v_bf[:, places].rearrange("p b n j -> p (b n j)"))
 
         def direction(h, b, tag):
             cols = slice(b * P, (b + 1) * P)
@@ -204,112 +206,115 @@ def tile_attend_ghv_nce_kernel(tc, xT, w_words, w_scales, vT, wt, xm, offs, out)
                 ALU.mult,
             )
 
-        def quant_g(h, s, g_half):
-            cols = slice(s * hn, (s + 1) * hn)
-            nc.vector.quantize_mx(g_codes[h][:, cols].bitcast(E5M2), g_bytes[h][:, cols], g_half)
+        def quant_g(h, n0, n1, g_blocks):
+            cols = slice(n0, n1)
+            nc.vector.quantize_mx(g_codes[h][:, cols].bitcast(E5M2), g_bytes[h][:, cols], g_blocks)
 
         def cast_m(m_half, raw):
             nc.scalar.activation(m_half.rearrange("p (c i t) -> p c t i", i=4, t=PACK),
                                  raw.rearrange("p t (c i) -> p c t i", i=4), ACT.Copy)
 
-        def quant_m(codes, scale_bytes, m_bf, j0, j1):
-            cols = slice(j0 * HALVES * P, j1 * HALVES * P)
-            nc.vector.quantize_mx(codes[:, cols].bitcast(E4M3), scale_bytes[:, cols],
-                                  m_bf[:, j0:j1].rearrange("p j h n -> p (j h n)"))
+        def quant_m(j, m_block):
+            nc.vector.quantize_mx(m_codes[j][:].bitcast(E4M3), m_bytes[j][:], m_block.rearrange("p h n -> p (h n)"))
 
-        gather_last(0, hn)
-        quant_v(0)
-        gather_last(hn, N)
-        quant_v(1)
+        gather_v(PACK - 1, 0)
+        quant_v(0, 1, slice(0, 1))
+        quant_v(1, 2, slice(3, 4))
+        gather_v(PACK - 1, 1)
 
         block = P * PACK
         first_av = [[direction(h, b, "av") for b in range(2)] for h in range(HALVES)]
-        late_blocks = [(1, 3), (0, 3), (1, 2)]
-        late_av = [direction(h, b, "wide") for h, b in late_blocks]
-        fill_av = direction(0, 2, "wide")
-
-        m_bf_a = placed("m_bf_a", [P, EARLY, HALVES, block], BF16, 0)
-        cast_m(m_bf_a[:, 0, 1, :], m_raw[0][1][:, :, :P])
-        for j in range(2):
-            cast_m(m_bf_a[:, j, 0, :], m_raw[0][0][:, :, j * P : (j + 1) * P])
-        for j, raw in ((1, m_raw[0][1][:, :, P:]), (2, m_raw[1][1][:])):
-            nc.gpsimd.tensor_scalar(m_bf_a[:, j, 1, :].rearrange("p (c t) -> p c t", t=PACK),
-                                    raw.rearrange("p t c -> p c t"), 1.0, 0.0, ALU.mult, ALU.add)
-        av_first = placed("av_first", [P, block], F32, 8192)
-
-        def copy_av(words, av):
-            nc.scalar.activation(words.rearrange("p (t c) -> p t c", t=PACK), av[:], ACT.Copy)
-
-        copy_av(av_first[:], late_av[0])
-        cast_m(m_bf_a[:, 2, 0, :], m_raw[1][0][:])
-        av_rest = placed("av_rest", [P, 2, block], F32, 12288)
-        copy_av(av_rest[:, 0, :], late_av[1])
-        nc.scalar.activation(av_rest[:, 1, KEPT * PACK :].rearrange("p (c t i) -> p c t i", t=PACK, i=2),
-                             late_av[2][:, :, KEPT:].rearrange("p t (c i) -> p c t i", i=2), ACT.Copy)
-        av_words = [av_first[:], av_rest[:, 0, :]]
-
         g_first = [tile("g_first0", [P, 2 * block], BF16), placed("g_first1", [P, 2 * block], BF16, 6144)]
-        m_codes = [tile("m_codes_a", [P, EARLY * HALVES * P], U32)]
-        m_bytes = [tile("m_bytes_a", [P, EARLY * HALVES * P], U8), tile("m_bytes_b", [P, HALVES * P], U8)]
-        for h in range(HALVES):
-            for b in range(2):
-                product(g_first[h][:, b * block : (b + 1) * block], h, b, first_av[h][b])
-        quant_g(0, 0, g_first[0][:])
-        quant_m(m_codes[0], m_bytes[0], m_bf_a, 0, 1)
-        quant_g(1, 0, g_first[1][:])
-        quant_m(m_codes[0], m_bytes[0], m_bf_a, 1, 2)
-        quant_m(m_codes[0], m_bytes[0], m_bf_a, 2, 3)
+        product(g_first[0][:, :block], 0, 0, first_av[0][0])
+        quant_v(2, 4, slice(1, 3))
+        late_av = {(h, b): direction(h, b, "wide") for h, b in ((0, 3), (1, 3), (1, 2), (0, 2))}
+
+        m_bf_a = placed("m_bf_a", [P, 2, 2, block], BF16, 0)
+        m_bf_g = placed("m_bf_g", [P, 2, block], BF16, 4096)
+        cast_m(m_bf_a[:, 0, 1, :], m_raw[0][1][:, :, :P])
+        cast_m(m_bf_a[:, 0, 0, :], m_raw[0][0][:, :, :P])
+        cast_m(m_bf_a[:, 1, 0, :], m_raw[0][0][:, :, P:])
+        for k, raw in enumerate((m_raw[0][1][:, :, P:], m_raw[1][1][:])):
+            nc.gpsimd.tensor_scalar(m_bf_g[:, k, :].rearrange("p (c t) -> p c t", t=PACK), raw.rearrange("p t c -> p c t"),
+                                    1.0, 0.0, ALU.mult, ALU.add)
+        av_first = placed("av_first", [P, PACK, P], F32, 8192)
+        nc.scalar.activation(av_first[:], late_av[0, 3][:], ACT.Copy)
+        cast_m(m_bf_a[:, 1, 1, :], m_raw[1][0][:])
+        av_rest = placed("av_rest", [P, 2, block], F32, 12288)
+        av_second = av_rest[:, 0, :].rearrange("p (t c) -> p t c", t=PACK)
+        nc.scalar.activation(av_second, late_av[1, 3][:], ACT.Copy)
+        av_third = av_rest[:, 1, : PACK * (P - KEPT)].rearrange("p (c t i) -> p c t i", t=PACK, i=2)
+        nc.scalar.activation(av_third, late_av[1, 2][:, :, : P - KEPT].rearrange("p t (c i) -> p c t i", i=2), ACT.Copy)
+
+        m_codes = [tile("m_codes%d" % j, [P, HALVES * P], U32) for j in range(D_BLOCKS)]
+        m_place = {(0, 0): (0, 0), (0, 1): (0, 1), (1, 1): (1, 0), (2, 1): (1, 1), (1, 0): (2, 0), (2, 0): (2, 1), (3, 0): (3, 0), (3, 1): (3, 1)}
+        m_bytes = [tile("m_bytes%d" % j, [P, HALVES * P], U8) for j in range(D_BLOCKS)]
+        for h, b in ((0, 1), (1, 0), (1, 1)):
+            product(g_first[h][:, b * block : (b + 1) * block], h, b, first_av[h][b])
+        quant_g(0, 0, hn, g_first[0][:])
+        quant_m(0, m_bf_a[:, 0])
+        quant_g(1, 0, hn, g_first[1][:])
+        quant_m(1, m_bf_g[:])
+        quant_m(2, m_bf_a[:, 1])
 
         def dw_pass(bank, h, j):
+            pair, place = m_place[j, h]
             nc.tensor.matmul_mx(bank[:], rhs=g_codes[h][:].bitcast(E5M2), rhs_scale=g_bytes[h][:],
                                 start=(h == 0), stop=(h == HALVES - 1),
-                                **stationary(m_codes[j // EARLY], m_bytes[j // EARLY], HALVES * (j % EARLY) + h))
+                                **stationary(m_codes[pair], m_bytes[pair], place))
 
         def scatter(j, cols, values):
             nc.vector.tensor_copy(windows[j][:].indirect(offsets[:, cols.start // 16 : cols.stop // 16]), values)
 
-        early = [ps.tile([P, N], F32, name="av") for j in range(2)]
-        staged = [tile("staged%d" % j, [P, N], F32) for j in range(D_BLOCKS)]
-        for j in range(2):
+        early = [ps.tile([P, N], F32, name="av") for j in range(EARLY)]
+        for j in range(EARLY):
             for h in range(HALVES):
                 dw_pass(early[j], h, j)
-            nc.scalar.activation(staged[j][:, :hn], early[j][:, :hn], ACT.Copy)
-        for h in range(HALVES):
-            dw_pass(early[1], h, 2)
+        staged = [tile("staged%d" % j, [P, N], F32) for j in range(D_BLOCKS)]
+        nc.scalar.activation(staged[0][:, :hn], early[0][:, :hn], ACT.Copy)
 
-        g_second = placed("g_second", [P, HALVES, 2 * block], BF16, 4096)
-        g_rows = placed("g_rows", [P, 2, PACK, P], BF16, 0)
-        for k, (h, b) in enumerate(late_blocks[:2]):
-            nc.gpsimd.tensor_tensor(g_rows[:, k], av_words[k].rearrange("p (t c) -> p t c", t=PACK),
-                                    factor[:, h, :, b * P : (b + 1) * P], ALU.mult)
-        nc.gpsimd.tensor_tensor(g_second[:, 1, KEPT * PACK : block].rearrange("p (c i t) -> p c t i", i=2, t=PACK),
-                                av_rest[:, 1, KEPT * PACK :].rearrange("p (c t i) -> p c t i", t=PACK, i=2),
-                                factor[:, 1, :, 2 * P + KEPT : 3 * P].rearrange("p t (c i) -> p c t i", i=2), ALU.mult)
-        for k, (h, b) in enumerate(late_blocks[:2]):
-            cast_m(g_second[:, h, block:], g_rows[:, k])
-        product(g_second[:, 0, :block], 0, 2, fill_av)
-        nc.vector.tensor_tensor(g_second[:, 1, : KEPT * PACK].rearrange("p (c i t) -> p c t i", i=2, t=PACK),
-                                late_av[2][:, :, :KEPT].rearrange("p t (c i) -> p c t i", i=2),
-                                factor[:, 1, :, 2 * P : 2 * P + KEPT].rearrange("p t (c i) -> p c t i", i=2), ALU.mult)
-        m_bf_b = tile("m_bf_b", [P, 1, HALVES, block], BF16)
-        for h in range(HALVES):
-            cast_m(m_bf_b[:, 0, h, :], m_raw[2][h][:])
+        g_late0 = placed("g_late0", [P, 2 * block], BF16, 1024)
+        g_late1 = placed("g_late1", [P, KEPT * PACK + block], BF16, 6144)
+        g_rows0 = placed("g_rows0", [P, PACK, P], BF16, 3584)
+        g_rows1 = placed("g_rows1", [P, PACK, P], BF16, 0)
+        nc.gpsimd.tensor_tensor(g_rows0[:], av_first[:], factor[:, 0, :, 3 * P :], ALU.mult)
+        nc.gpsimd.tensor_tensor(g_rows1[:], av_second, factor[:, 1, :, 3 * P :], ALU.mult)
+        product(g_late0[:, :block], 0, 2, late_av[0, 2])
+        nc.vector.tensor_tensor(g_late1[:, : KEPT * PACK].rearrange("p (c i t) -> p c t i", i=2, t=PACK),
+                                late_av[1, 2][:, :, P - KEPT :].rearrange("p t (c i) -> p c t i", i=2),
+                                factor[:, 1, :, 3 * P - KEPT : 3 * P].rearrange("p t (c i) -> p c t i", i=2), ALU.mult)
+        cast_m(g_late0[:, block:], g_rows0[:])
+        staged_second = placed("staged_second", [P, hn], F32, 8192)
+        nc.scalar.activation(staged_second[:], early[1][:, :hn], ACT.Copy)
+        cast_m(g_late1[:, KEPT * PACK :], g_rows1[:])
 
-        for j in range(2):
-            scatter(j, slice(0, hn), staged[j][:, :hn])
-        staged_early = placed("staged_early", [P, hn], F32, 12288)
-        nc.scalar.activation(staged_early[:], early[1][:, :hn], ACT.Copy)
+        scatter(0, slice(0, hn), staged[0][:, :hn])
+        quant_g(0, hn, N, g_late0[:])
+        g_last = placed("g_last", [P, (P - KEPT) * PACK], BF16, 1024)
+        nc.gpsimd.tensor_tensor(g_last[:].rearrange("p (c i t) -> p c t i", i=2, t=PACK), av_third,
+                                factor[:, 1, :, 2 * P : 3 * P - KEPT].rearrange("p t (c i) -> p c t i", i=2), ALU.mult)
+        sums = [ps.tile([P, N], F32, name="wide") for j in range(D_BLOCKS)]
+        for j in range(EARLY):
+            dw_pass(sums[j], 0, j)
+        scatter(1, slice(0, hn), staged_second[:])
+        staged_third = placed("staged_third", [P, hn], F32, 12288)
+        nc.scalar.activation(staged_third[:], early[2][:, :hn], ACT.Copy)
+        quant_g(1, 3 * P - KEPT, 4 * P - KEPT, g_late1[:, :block])
+        quant_g(1, 4 * P - KEPT, 4 * P, g_late1[:, block:])
+        quant_g(1, 2 * P, 3 * P - KEPT, g_last[:])
+        m_bf_b = placed("m_bf_b", [P, HALVES, block], BF16, 1024)
         for h in range(HALVES):
-            quant_g(h, 1, g_second[:, h, :])
-        m_codes.append(placed("m_codes_b", [P, HALVES * P], U32, 14336))
-        quant_m(m_codes[1], m_bytes[1], m_bf_b, 0, 1)
-        scatter(2, slice(0, hn), staged_early[:])
+            nc.gpsimd.tensor_scalar(m_bf_b[:, h, :].rearrange("p (c t) -> p c t", t=PACK),
+                                    m_raw[2][h][:].rearrange("p t c -> p c t"), 1.0, 0.0, ALU.mult, ALU.add)
+        scatter(2, slice(0, hn), staged_third[:])
 
         for j in range(D_BLOCKS):
             cols = slice(hn if j < EARLY else 0, N)
-            sums = ps.tile([P, N], F32, name="wide")
-            for h in range(HALVES):
-                dw_pass(sums, h, j)
-            nc.scalar.activation(staged[j][:, cols], sums[:, cols], ACT.Copy)
+            if j == EARLY:
+                dw_pass(sums[j], 0, j)
+            dw_pass(sums[j], 1, j)
+            nc.scalar.activation(staged[j][:, cols], sums[j][:, cols], ACT.Copy)
+            if j == 1:
+                quant_m(3, m_bf_b[:])
             scatter(j, cols, staged[j][:, cols])
             nc.sync.dma_start(out[j * P : (j + 1) * P, :], windows[j][:])

@@ -155,7 +155,7 @@ def tile_attend_ghv_nce_kernel(tc, xT, w_words, w_scales, vT, wt, xm, offs, out)
 
         def affine(h, t):
             c, mc = quarter[:, h, t : t + 1], minus_quarter[:, h, t : t + 1]
-            if h == 0 or t < 2:
+            if h == 0 or t < 1:
                 squared = sq_first[:, t, :] if h == 0 and t < 2 else sq[h][:, t, :]
                 nc.gpsimd.tensor_scalar(factor[:, h, t, :], squared, mc, c, ALU.mult, ALU.add)
             else:
@@ -234,9 +234,10 @@ def tile_attend_ghv_nce_kernel(tc, xT, w_words, w_scales, vT, wt, xm, offs, out)
         cast_m(m_bf_a[:, 0, 1, :], m_raw[0][1][:, :, :P])
         cast_m(m_bf_a[:, 0, 0, :], m_raw[0][0][:, :, :P])
         cast_m(m_bf_a[:, 1, 0, :], m_raw[0][0][:, :, P:])
-        for k, raw in enumerate((m_raw[0][1][:, :, P:], m_raw[1][1][:])):
-            nc.gpsimd.tensor_scalar(m_bf_g[:, k, :].rearrange("p (c t) -> p c t", t=PACK), raw.rearrange("p t c -> p c t"),
+        for m_part, raw in ((m_bf_g[:, 0, :], m_raw[0][1][:, :, P:]), (m_bf_g[:, 1, : 96 * PACK], m_raw[1][1][:, :, :96])):
+            nc.gpsimd.tensor_scalar(m_part.rearrange("p (c t) -> p c t", t=PACK), raw.rearrange("p t c -> p c t"),
                                     1.0, 0.0, ALU.mult, ALU.add)
+        cast_m(m_bf_g[:, 1, 96 * PACK :], m_raw[1][1][:, :, 96:])
         av_first = placed("av_first", [P, PACK, P], F32, 8192)
         nc.scalar.activation(av_first[:], late_av[0, 3][:], ACT.Copy)
         cast_m(m_bf_a[:, 1, 1, :], m_raw[1][0][:])

@@ -23,9 +23,15 @@ HALF = P * PACK
 HALVES = R // HALF
 SLOT_BLOCKS = N // P
 D_BLOCKS = D // P
-WINDOWS = 4
-EARLY = 3
-KEPT = 64
+BLOCK = P * PACK
+EARLY_SLOTS = N // 2
+EARLY_BLOCKS = 3
+PSUM_BUFS = 4
+WT_ROW = 16
+KEPT = 44
+LAST = 96
+CAST_SHARE = 96
+KIB = 1024
 
 
 def tile_attend_ghv_nce_kernel(tc, xT, w_words, w_scales, vT, wt, xm, offs, out):
@@ -33,7 +39,7 @@ def tile_attend_ghv_nce_kernel(tc, xT, w_words, w_scales, vT, wt, xm, offs, out)
     with ExitStack() as ctx:
         sb = ctx.enter_context(tc.tile_pool(name="sb", bufs=1))
         reused = ctx.enter_context(tc.tile_pool(name="reused", bufs=1))
-        ps = ctx.enter_context(tc.psum_pool(name="ps", bufs=4))
+        ps = ctx.enter_context(tc.psum_pool(name="ps", bufs=PSUM_BUFS))
 
         def tile(name, shape, dtype):
             return sb.tile(shape, dtype, name=name, align_bytes=64)
@@ -46,12 +52,12 @@ def tile_attend_ghv_nce_kernel(tc, xT, w_words, w_scales, vT, wt, xm, offs, out)
         s_table = tile("s_table", [P, T], U8)
         x_raw = [tile("x_raw%d" % u, [P, 2, R], F32) for u in range(2)]
         v_table = [tile("v_table%d" % j, [P, T], F32) for j in range(PACK)]
-        m_raw = [[placed("m_raw00", [P, PACK, 2 * P], F32, 8192), tile("m_raw01", [P, PACK, 2 * P], F32)],
-                 [placed("m_raw10", [P, PACK, P], F32, 12288), tile("m_raw11", [P, PACK, P], F32)],
+        m_raw = [[placed("m_raw00", [P, PACK, 2 * P], F32, 8 * KIB), tile("m_raw01", [P, PACK, 2 * P], F32)],
+                 [placed("m_raw10", [P, PACK, P], F32, 12 * KIB), tile("m_raw11", [P, PACK, P], F32)],
                  [tile("m_raw2%d" % h, [P, PACK, P], F32) for h in range(HALVES)]]
         wt_rows = tile("wt_rows", [P, HALF], F32)
         identity = tile("identity", [P, P], F32)
-        windows = [tile("window%d" % j, [P, T], F32) for j in range(WINDOWS)]
+        windows = [tile("window%d" % j, [P, T], F32) for j in range(D_BLOCKS)]
 
         def zero_on_vector(words):
             odd = words.shape[1] // 2 - 1
@@ -68,7 +74,7 @@ def tile_attend_ghv_nce_kernel(tc, xT, w_words, w_scales, vT, wt, xm, offs, out)
             nc.sync.dma_start(s_table[i:P:32, :].bitcast(I32), w_scales[0][i:16:4, :].bitcast(I32))
         x_rows = xT[0].rearrange("(p j) r -> p j r", j=PACK)
         nc.sync.dma_start(x_raw[0][:], x_rows[:, :2, :])
-        nc.sync.dma_start(wt_rows[16:P:64, :], wt[0].rearrange("(h r) o -> h (r o)", h=HALVES))
+        nc.sync.dma_start(wt_rows[WT_ROW:P:64, :], wt[0].rearrange("(h r) o -> h (r o)", h=HALVES))
         nc.sync.dma_start(x_raw[1][:], x_rows[:, 2:, :])
         v_rows = vT.rearrange("(p j) c -> p j c", j=PACK)
         for j in range(PACK):
@@ -87,7 +93,7 @@ def tile_attend_ghv_nce_kernel(tc, xT, w_words, w_scales, vT, wt, xm, offs, out)
         nc.vector.tensor_copy(w_codes[:], w_table[:].indirect(offsets[:]))
         nc.vector.tensor_copy(w_bytes[:], s_table[:].indirect(offsets[:]))
 
-        x_bf = [tile("x_bf0", [P, HALF * PACK], BF16), placed("x_bf1", [P, HALF * PACK], BF16, 16384)]
+        x_bf = [tile("x_bf0", [P, HALF * PACK], BF16), placed("x_bf1", [P, HALF * PACK], BF16, 16 * KIB)]
         x_codes = [tile("x_codes%d" % h, [P, HALF], U32) for h in range(HALVES)]
         x_bytes = [tile("x_bytes%d" % h, [P, HALF], U8) for h in range(HALVES)]
         quarter = tile("quarter", [P, HALVES, PACK], F32)
@@ -112,18 +118,17 @@ def tile_attend_ghv_nce_kernel(tc, xT, w_words, w_scales, vT, wt, xm, offs, out)
 
         g_codes = [tile("g_codes%d" % h, [P, N], U32) for h in range(HALVES)]
         g_bytes = [tile("g_bytes%d" % h, [P, N], U8) for h in range(HALVES)]
-        hn = N // 2
 
         for h in range(HALVES):
-            nc.gpsimd.memset(g_codes[h][:, hn:].bitcast(I32), 0)
-            nc.gpsimd.memset(g_bytes[h][:, hn:].bitcast(I32), 0)
-        cast_x(0, 0, 0, 4)
+            nc.gpsimd.memset(g_codes[h][:, EARLY_SLOTS:].bitcast(I32), 0)
+            nc.gpsimd.memset(g_bytes[h][:, EARLY_SLOTS:].bitcast(I32), 0)
+        cast_x(0, 0, 0, PACK)
         for u in range(2):
             cast_x_on_scalar(u)
         wt_turned = ps.tile([P, PACK, P], F32, name="av")
         for t in range(PACK):
             nc.tensor.transpose(wt_turned[:, t, :], wt_rows[:, t:HALF:PACK], identity[:])
-        wt_columns = wt_turned[:, :, 16:P:64].rearrange("p t h -> p h t")
+        wt_columns = wt_turned[:, :, WT_ROW:P:64].rearrange("p t h -> p h t")
         nc.vector.tensor_scalar(quarter[:], wt_columns, 0.25, None, ALU.mult)
         nc.vector.tensor_scalar(minus_quarter[:], wt_columns, -0.25, None, ALU.mult)
         pieces = [(0, 0, 1), (0, 1, 3), (0, 3, 4)]
@@ -132,16 +137,16 @@ def tile_attend_ghv_nce_kernel(tc, xT, w_words, w_scales, vT, wt, xm, offs, out)
             cast_x(1, *ahead)
             quant_x(*done)
         quant_x(*pieces[-1])
-        quant_x(1, 0, 4)
+        quant_x(1, 0, PACK)
 
-        def stationary(codes, scale_bytes, block):
-            cols = slice(block * P, (block + 1) * P)
+        def stationary(codes, scale_bytes, place):
+            cols = slice(place * P, (place + 1) * P)
             return dict(lhsT=codes[:, cols].bitcast(E4M3), lhsT_scale=scale_bytes[:, cols])
 
         th = [tile("th%d" % h, [P, PACK, N], F32) for h in range(HALVES)]
         sq = [tile("sq%d" % h, [P, PACK, N], F32) for h in range(HALVES)]
         factor = tile("factor", [P, HALVES, PACK, N], F32)
-        v_bf = placed("v_bf", [P, SLOT_BLOCKS, P, PACK], BF16, 4096)
+        v_bf = placed("v_bf", [P, SLOT_BLOCKS, P, PACK], BF16, 4 * KIB)
         v_place = (slice(0, 4, 3), slice(1, 3))
 
         def score(h, t):
@@ -155,7 +160,7 @@ def tile_attend_ghv_nce_kernel(tc, xT, w_words, w_scales, vT, wt, xm, offs, out)
 
         def affine(h, t):
             c, mc = quarter[:, h, t : t + 1], minus_quarter[:, h, t : t + 1]
-            if h == 0 or t < 1:
+            if h == 0 or t == 0:
                 squared = sq_first[:, t, :] if h == 0 and t < 2 else sq[h][:, t, :]
                 nc.gpsimd.tensor_scalar(factor[:, h, t, :], squared, mc, c, ALU.mult, ALU.add)
             else:
@@ -163,7 +168,7 @@ def tile_attend_ghv_nce_kernel(tc, xT, w_words, w_scales, vT, wt, xm, offs, out)
 
         for t in range(PACK):
             score(0, t)
-        sq_first = placed("sq_first", [P, 2, N], F32, 16384)
+        sq_first = placed("sq_first", [P, 2, N], F32, 16 * KIB)
         for t in range(2):
             nc.gpsimd.tensor_tensor(sq_first[:, t, :], th[0][:, t, :], th[0][:, t, :], ALU.mult)
         square(0, 2, 4)
@@ -176,19 +181,24 @@ def tile_attend_ghv_nce_kernel(tc, xT, w_words, w_scales, vT, wt, xm, offs, out)
             for t in range(PACK):
                 affine(h, t)
 
-        def gather_v(j, s):
-            nc.vector.tensor_copy(v_bf[:, v_place[s], :, j], v_table[j][:].indirect(offsets[:, s * hn // 16 : (s + 1) * hn // 16]))
+        def listed(n0, n1):
+            return offsets[:, n0 // 16 : n1 // 16]
+
+        def gather_v(j, late):
+            nc.vector.tensor_copy(v_bf[:, v_place[late], :, j],
+                                  v_table[j][:].indirect(listed(late * EARLY_SLOTS, (late + 1) * EARLY_SLOTS)))
 
         for j in range(PACK - 1):
-            for s in range(2):
-                gather_v(j, s)
+            for late in range(2):
+                gather_v(j, late)
 
         v_codes = tile("v_codes", [P, N], U32)
         v_bytes = tile("v_bytes", [P, N], U8)
 
         def quant_v(b0, b1, places):
             cols = slice(b0 * P, b1 * P)
-            nc.vector.quantize_mx(v_codes[:, cols].bitcast(E4M3), v_bytes[:, cols], v_bf[:, places].rearrange("p b n j -> p (b n j)"))
+            nc.vector.quantize_mx(v_codes[:, cols].bitcast(E4M3), v_bytes[:, cols],
+                                  v_bf[:, places].rearrange("p b n j -> p (b n j)"))
 
         def direction(h, b, tag):
             cols = slice(b * P, (b + 1) * P)
@@ -198,63 +208,69 @@ def tile_attend_ghv_nce_kernel(tc, xT, w_words, w_scales, vT, wt, xm, offs, out)
                                     start=True, stop=True, **stationary(x_codes[h], x_bytes[h], t))
             return av
 
+        def as_words(g_slots):
+            return g_slots.rearrange("p (c i t) -> p c t i", i=2, t=PACK)
+
+        def as_tiles(rows):
+            return rows.rearrange("p t (c i) -> p c t i", i=2)
+
         def product(g_block, h, b, av):
-            nc.vector.tensor_tensor(
-                g_block.rearrange("p (c i t) -> p c t i", i=2, t=PACK),
-                av[:].rearrange("p t (c i) -> p c t i", i=2),
-                factor[:, h, :, b * P : (b + 1) * P].rearrange("p t (c i) -> p c t i", i=2),
-                ALU.mult,
-            )
+            nc.vector.tensor_tensor(as_words(g_block), as_tiles(av[:]), as_tiles(factor[:, h, :, b * P : (b + 1) * P]), ALU.mult)
 
-        def quant_g(h, n0, n1, g_blocks):
+        def quant_g(h, n0, n1, g_slots):
             cols = slice(n0, n1)
-            nc.vector.quantize_mx(g_codes[h][:, cols].bitcast(E5M2), g_bytes[h][:, cols], g_blocks)
+            nc.vector.quantize_mx(g_codes[h][:, cols].bitcast(E5M2), g_bytes[h][:, cols], g_slots)
 
-        def cast_m(m_half, raw):
-            nc.scalar.activation(m_half.rearrange("p (c i t) -> p c t i", i=4, t=PACK),
-                                 raw.rearrange("p t (c i) -> p c t i", i=4), ACT.Copy)
+        def weave(words, rows):
+            nc.scalar.activation(words.rearrange("p (c i t) -> p c t i", i=4, t=PACK),
+                                 rows.rearrange("p t (c i) -> p c t i", i=4), ACT.Copy)
 
-        def quant_m(j, m_block):
-            nc.vector.quantize_mx(m_codes[j][:].bitcast(E4M3), m_bytes[j][:], m_block.rearrange("p h n -> p (h n)"))
+        def weave_on_gpsimd(words, rows):
+            nc.gpsimd.tensor_scalar(words.rearrange("p (c t) -> p c t", t=PACK), rows.rearrange("p t c -> p c t"),
+                                    1.0, 0.0, ALU.mult, ALU.add)
+
+        def quant_m(pair, m_pair):
+            nc.vector.quantize_mx(m_codes[pair][:].bitcast(E4M3), m_bytes[pair][:], m_pair.rearrange("p k n -> p (k n)"))
 
         gather_v(PACK - 1, 0)
         quant_v(0, 1, slice(0, 1))
         quant_v(1, 2, slice(3, 4))
         gather_v(PACK - 1, 1)
 
-        block = P * PACK
-        first_av = [[direction(h, b, "av") for b in range(2)] for h in range(HALVES)]
-        g_first = [tile("g_first0", [P, 2 * block], BF16), placed("g_first1", [P, 2 * block], BF16, 6144)]
-        product(g_first[0][:, :block], 0, 0, first_av[0][0])
+        early_av = [[direction(h, b, "av") for b in range(2)] for h in range(HALVES)]
+        g_early = [tile("g_first0", [P, 2 * BLOCK], BF16), placed("g_first1", [P, 2 * BLOCK], BF16, 6 * KIB)]
+        product(g_early[0][:, :BLOCK], 0, 0, early_av[0][0])
         quant_v(2, 4, slice(1, 3))
         late_av = {(h, b): direction(h, b, "wide") for h, b in ((0, 3), (1, 3), (1, 2), (0, 2))}
 
-        m_bf_a = placed("m_bf_a", [P, 2, 2, block], BF16, 0)
-        m_bf_g = placed("m_bf_g", [P, 2, block], BF16, 4096)
-        cast_m(m_bf_a[:, 0, 1, :], m_raw[0][1][:, :, :P])
-        cast_m(m_bf_a[:, 0, 0, :], m_raw[0][0][:, :, :P])
-        cast_m(m_bf_a[:, 1, 0, :], m_raw[0][0][:, :, P:])
-        for m_part, raw in ((m_bf_g[:, 0, :], m_raw[0][1][:, :, P:]), (m_bf_g[:, 1, : 96 * PACK], m_raw[1][1][:, :, :96])):
-            nc.gpsimd.tensor_scalar(m_part.rearrange("p (c t) -> p c t", t=PACK), raw.rearrange("p t c -> p c t"),
-                                    1.0, 0.0, ALU.mult, ALU.add)
-        cast_m(m_bf_g[:, 1, 96 * PACK :], m_raw[1][1][:, :, 96:])
-        av_first = placed("av_first", [P, PACK, P], F32, 8192)
+        m_bf_a = placed("m_bf_a", [P, 2, 2, BLOCK], BF16, 0)
+        m_bf_g = placed("m_bf_g", [P, 2, BLOCK], BF16, 4 * KIB)
+        m_place = {(0, 0): (0, 0), (0, 1): (0, 1), (1, 1): (1, 0), (2, 1): (1, 1),
+                   (1, 0): (2, 0), (2, 0): (2, 1), (3, 0): (3, 0), (3, 1): (3, 1)}
+        weave(m_bf_a[:, 0, 1, :], m_raw[0][1][:, :, :P])
+        weave(m_bf_a[:, 0, 0, :], m_raw[0][0][:, :, :P])
+        weave(m_bf_a[:, 1, 0, :], m_raw[0][0][:, :, P:])
+        weave_on_gpsimd(m_bf_g[:, 0, :], m_raw[0][1][:, :, P:])
+        weave_on_gpsimd(m_bf_g[:, 1, : CAST_SHARE * PACK], m_raw[1][1][:, :, :CAST_SHARE])
+        weave(m_bf_g[:, 1, CAST_SHARE * PACK :], m_raw[1][1][:, :, CAST_SHARE:])
+        av_first = placed("av_first", [P, PACK, P], F32, 8 * KIB)
         nc.scalar.activation(av_first[:], late_av[0, 3][:], ACT.Copy)
-        cast_m(m_bf_a[:, 1, 1, :], m_raw[1][0][:])
-        av_rest = placed("av_rest", [P, 2, block], F32, 12288)
-        av_second = av_rest[:, 0, :].rearrange("p (t c) -> p t c", t=PACK)
-        nc.scalar.activation(av_second, late_av[1, 3][:], ACT.Copy)
-        av_third = av_rest[:, 1, : PACK * (P - KEPT)].rearrange("p (c t i) -> p c t i", t=PACK, i=2)
-        nc.scalar.activation(av_third, late_av[1, 2][:, :, : P - KEPT].rearrange("p t (c i) -> p c t i", i=2), ACT.Copy)
+        weave(m_bf_a[:, 1, 1, :], m_raw[1][0][:])
+        av_rest = placed("av_rest", [P, 2, BLOCK], F32, 12 * KIB)
+        middle = 2 * P - LAST - KEPT
+        av_second = av_rest[:, 0, : PACK * middle].rearrange("p (t c) -> p t c", t=PACK)
+        nc.scalar.activation(av_second[:, :, P - LAST :], late_av[1, 3][:, :, : P - KEPT], ACT.Copy)
+        nc.scalar.activation(av_second[:, :, : P - LAST], late_av[1, 2][:, :, LAST:], ACT.Copy)
+        av_third = av_rest[:, 1, : PACK * LAST].rearrange("p (c t i) -> p c t i", t=PACK, i=2)
+        nc.scalar.activation(av_third, as_tiles(late_av[1, 2][:, :, :LAST]), ACT.Copy)
 
-        m_codes = [tile("m_codes%d" % j, [P, HALVES * P], U32) for j in range(D_BLOCKS)]
-        m_place = {(0, 0): (0, 0), (0, 1): (0, 1), (1, 1): (1, 0), (2, 1): (1, 1), (1, 0): (2, 0), (2, 0): (2, 1), (3, 0): (3, 0), (3, 1): (3, 1)}
-        m_bytes = [tile("m_bytes%d" % j, [P, HALVES * P], U8) for j in range(D_BLOCKS)]
+        m_codes = [tile("m_codes%d" % pair, [P, 2 * P], U32) for pair in range(D_BLOCKS)]
+        m_bytes = [tile("m_bytes%d" % pair, [P, 2 * P], U8) for pair in range(D_BLOCKS)]
         for h, b in ((0, 1), (1, 0), (1, 1)):
-            product(g_first[h][:, b * block : (b + 1) * block], h, b, first_av[h][b])
-        quant_g(0, 0, hn, g_first[0][:])
+            product(g_early[h][:, b * BLOCK : (b + 1) * BLOCK], h, b, early_av[h][b])
+        quant_g(0, 0, EARLY_SLOTS, g_early[0][:])
         quant_m(0, m_bf_a[:, 0])
-        quant_g(1, 0, hn, g_first[1][:])
+        quant_g(1, 0, EARLY_SLOTS, g_early[1][:])
         quant_m(1, m_bf_g[:])
         quant_m(2, m_bf_a[:, 1])
 
@@ -265,53 +281,51 @@ def tile_attend_ghv_nce_kernel(tc, xT, w_words, w_scales, vT, wt, xm, offs, out)
                                 **stationary(m_codes[pair], m_bytes[pair], place))
 
         def scatter(j, cols, values):
-            nc.vector.tensor_copy(windows[j][:].indirect(offsets[:, cols.start // 16 : cols.stop // 16]), values)
+            nc.vector.tensor_copy(windows[j][:].indirect(listed(cols.start, cols.stop)), values)
 
-        early = [ps.tile([P, N], F32, name="av") for j in range(EARLY)]
-        for j in range(EARLY):
+        early_cols = slice(0, EARLY_SLOTS)
+        early_sums = [ps.tile([P, N], F32, name="av") for j in range(EARLY_BLOCKS)]
+        for j in range(EARLY_BLOCKS):
             for h in range(HALVES):
-                dw_pass(early[j], h, j)
+                dw_pass(early_sums[j], h, j)
         staged = [tile("staged%d" % j, [P, N], F32) for j in range(D_BLOCKS)]
-        nc.scalar.activation(staged[0][:, :hn], early[0][:, :hn], ACT.Copy)
+        nc.scalar.activation(staged[0][:, early_cols], early_sums[0][:, early_cols], ACT.Copy)
 
-        g_late0 = placed("g_late0", [P, 2 * block], BF16, 1024)
-        g_late1 = placed("g_late1", [P, KEPT * PACK + block], BF16, 6144)
-        g_rows0 = placed("g_rows0", [P, PACK, P], BF16, 3584)
-        g_rows1 = placed("g_rows1", [P, PACK, P], BF16, 0)
+        g_late0 = placed("g_late0", [P, 2 * BLOCK], BF16, KIB)
+        g_late1 = placed("g_late1", [P, BLOCK], BF16, 5 * KIB)
+        g_rows0 = placed("g_rows0", [P, PACK, P], BF16, 4 * KIB - KIB // 2)
+        g_rows1 = placed("g_rows1", [P, PACK, middle], BF16, 0)
         nc.gpsimd.tensor_tensor(g_rows0[:], av_first[:], factor[:, 0, :, 3 * P :], ALU.mult)
-        nc.gpsimd.tensor_tensor(g_rows1[:], av_second, factor[:, 1, :, 3 * P :], ALU.mult)
-        product(g_late0[:, :block], 0, 2, late_av[0, 2])
-        nc.vector.tensor_tensor(g_late1[:, : KEPT * PACK].rearrange("p (c i t) -> p c t i", i=2, t=PACK),
-                                late_av[1, 2][:, :, P - KEPT :].rearrange("p t (c i) -> p c t i", i=2),
-                                factor[:, 1, :, 3 * P - KEPT : 3 * P].rearrange("p t (c i) -> p c t i", i=2), ALU.mult)
-        cast_m(g_late0[:, block:], g_rows0[:])
-        staged_second = placed("staged_second", [P, hn], F32, 8192)
-        nc.scalar.activation(staged_second[:], early[1][:, :hn], ACT.Copy)
-        cast_m(g_late1[:, KEPT * PACK :], g_rows1[:])
+        nc.gpsimd.tensor_tensor(g_rows1[:], av_second, factor[:, 1, :, 2 * P + LAST : N - KEPT], ALU.mult)
+        nc.vector.tensor_tensor(as_words(g_late1[:, (P - KEPT) * PACK :]), as_tiles(late_av[1, 3][:, :, P - KEPT :]),
+                                as_tiles(factor[:, 1, :, N - KEPT :]), ALU.mult)
+        product(g_late0[:, :BLOCK], 0, 2, late_av[0, 2])
+        weave(g_late0[:, BLOCK:], g_rows0[:])
+        staged_second = placed("staged_second", [P, EARLY_SLOTS], F32, 8 * KIB)
+        nc.scalar.activation(staged_second[:], early_sums[1][:, early_cols], ACT.Copy)
+        weave(g_late1[:, : (P - KEPT) * PACK], g_rows1[:, :, P - LAST :])
 
-        scatter(0, slice(0, hn), staged[0][:, :hn])
-        quant_g(0, hn, N, g_late0[:])
-        g_last = placed("g_last", [P, (P - KEPT) * PACK], BF16, 1024)
-        nc.gpsimd.tensor_tensor(g_last[:].rearrange("p (c i t) -> p c t i", i=2, t=PACK), av_third,
-                                factor[:, 1, :, 2 * P : 3 * P - KEPT].rearrange("p t (c i) -> p c t i", i=2), ALU.mult)
+        scatter(0, early_cols, staged[0][:, early_cols])
+        quant_g(0, EARLY_SLOTS, N, g_late0[:])
+        g_last = placed("g_last", [P, BLOCK], BF16, KIB)
+        nc.gpsimd.tensor_tensor(as_words(g_last[:, : LAST * PACK]), av_third, as_tiles(factor[:, 1, :, 2 * P : 2 * P + LAST]), ALU.mult)
+        weave(g_last[:, LAST * PACK :], g_rows1[:, :, : P - LAST])
         sums = [ps.tile([P, N], F32, name="wide") for j in range(D_BLOCKS)]
-        for j in range(EARLY):
+        for j in range(EARLY_BLOCKS):
             dw_pass(sums[j], 0, j)
-        scatter(1, slice(0, hn), staged_second[:])
-        staged_third = placed("staged_third", [P, hn], F32, 12288)
-        nc.scalar.activation(staged_third[:], early[2][:, :hn], ACT.Copy)
-        quant_g(1, 3 * P - KEPT, 4 * P - KEPT, g_late1[:, :block])
-        quant_g(1, 4 * P - KEPT, 4 * P, g_late1[:, block:])
-        quant_g(1, 2 * P, 3 * P - KEPT, g_last[:])
-        m_bf_b = placed("m_bf_b", [P, HALVES, block], BF16, 1024)
+        scatter(1, early_cols, staged_second[:])
+        staged_third = placed("staged_third", [P, EARLY_SLOTS], F32, 0)
+        nc.scalar.activation(staged_third[:], early_sums[2][:, early_cols], ACT.Copy)
+        quant_g(1, 3 * P, N, g_late1[:])
+        quant_g(1, 2 * P, 3 * P, g_last[:])
+        m_bf_b = placed("m_bf_b", [P, HALVES, BLOCK], BF16, KIB)
         for h in range(HALVES):
-            nc.gpsimd.tensor_scalar(m_bf_b[:, h, :].rearrange("p (c t) -> p c t", t=PACK),
-                                    m_raw[2][h][:].rearrange("p t c -> p c t"), 1.0, 0.0, ALU.mult, ALU.add)
-        scatter(2, slice(0, hn), staged_third[:])
+            weave_on_gpsimd(m_bf_b[:, h, :], m_raw[2][h][:])
+        scatter(2, early_cols, staged_third[:])
 
         for j in range(D_BLOCKS):
-            cols = slice(hn if j < EARLY else 0, N)
-            if j == EARLY:
+            cols = slice(EARLY_SLOTS if j < EARLY_BLOCKS else 0, N)
+            if j == EARLY_BLOCKS:
                 dw_pass(sums[j], 0, j)
             dw_pass(sums[j], 1, j)
             nc.scalar.activation(staged[j][:, cols], sums[j][:, cols], ACT.Copy)

@@ -28,8 +28,9 @@ EARLY_SLOTS = N // 2
 EARLY_BLOCKS = 3
 PSUM_BUFS = 4
 WT_ROW = 16
-KEPT = 44
-LAST = 96
+LAST = 104
+KEPT = 52
+MIDDLE = EARLY_SLOTS - LAST - KEPT
 CAST_SHARE = 96
 KIB = 1024
 
@@ -257,8 +258,7 @@ def tile_attend_ghv_nce_kernel(tc, xT, w_words, w_scales, vT, wt, xm, offs, out)
         nc.scalar.activation(av_first[:], late_av[0, 3][:], ACT.Copy)
         weave(m_bf_a[:, 1, 1, :], m_raw[1][0][:])
         av_rest = placed("av_rest", [P, 2, BLOCK], F32, 12 * KIB)
-        middle = 2 * P - LAST - KEPT
-        av_second = av_rest[:, 0, : PACK * middle].rearrange("p (t c) -> p t c", t=PACK)
+        av_second = av_rest[:, 0, : PACK * MIDDLE].rearrange("p (t c) -> p t c", t=PACK)
         nc.scalar.activation(av_second[:, :, P - LAST :], late_av[1, 3][:, :, : P - KEPT], ACT.Copy)
         nc.scalar.activation(av_second[:, :, : P - LAST], late_av[1, 2][:, :, LAST:], ACT.Copy)
         av_third = av_rest[:, 1, : PACK * LAST].rearrange("p (c t i) -> p c t i", t=PACK, i=2)
@@ -294,7 +294,7 @@ def tile_attend_ghv_nce_kernel(tc, xT, w_words, w_scales, vT, wt, xm, offs, out)
         g_late0 = placed("g_late0", [P, 2 * BLOCK], BF16, KIB)
         g_late1 = placed("g_late1", [P, BLOCK], BF16, 5 * KIB)
         g_rows0 = placed("g_rows0", [P, PACK, P], BF16, 4 * KIB - KIB // 2)
-        g_rows1 = placed("g_rows1", [P, PACK, middle], BF16, 0)
+        g_rows1 = placed("g_rows1", [P, PACK, MIDDLE], BF16, 0)
         nc.gpsimd.tensor_tensor(g_rows0[:], av_first[:], factor[:, 0, :, 3 * P :], ALU.mult)
         nc.gpsimd.tensor_tensor(g_rows1[:], av_second, factor[:, 1, :, 2 * P + LAST : N - KEPT], ALU.mult)
         nc.vector.tensor_tensor(as_words(g_late1[:, (P - KEPT) * PACK :]), as_tiles(late_av[1, 3][:, :, P - KEPT :]),

@@ -28,6 +28,7 @@ EARLY_SLOTS = N // 2
 EARLY_BLOCKS = 3
 PSUM_BUFS = 4
 WT_ROW = 16
+SCALE_ROW = 4
 LAST = 104
 KEPT = 52
 MIDDLE = EARLY_SLOTS - LAST - KEPT
@@ -39,6 +40,7 @@ def tile_attend_ghv_nce_kernel(tc, xT, w_words, w_scales, vT, wt, xm, offs, out)
     nc = tc.nc
     with ExitStack() as ctx:
         sb = ctx.enter_context(tc.tile_pool(name="sb", bufs=1))
+        loads = ctx.enter_context(tc.tile_pool(name="loads", bufs=1))
         reused = ctx.enter_context(tc.tile_pool(name="reused", bufs=1))
         ps = ctx.enter_context(tc.psum_pool(name="ps", bufs=PSUM_BUFS))
 
@@ -48,14 +50,13 @@ def tile_attend_ghv_nce_kernel(tc, xT, w_words, w_scales, vT, wt, xm, offs, out)
         def placed(name, shape, dtype, offset):
             return reused.tile(shape, dtype, name=name, align_bytes=64, offset=offset)
 
+        def landed(name, shape, dtype, offset):
+            return loads.tile(shape, dtype, name=name, align_bytes=64, offset=offset)
+
         offsets = sb.tile([P, N // 16], U16, name="offsets")
         w_table = tile("w_table", [P, T], U32)
-        s_table = tile("s_table", [P, T], U8)
-        x_raw = [tile("x_raw%d" % u, [P, 2, R], F32) for u in range(2)]
-        v_table = [tile("v_table%d" % j, [P, T], F32) for j in range(PACK)]
-        m_raw = [[placed("m_raw00", [P, PACK, 2 * P], F32, 8 * KIB), tile("m_raw01", [P, PACK, 2 * P], F32)],
-                 [placed("m_raw10", [P, PACK, P], F32, 12 * KIB), tile("m_raw11", [P, PACK, P], F32)],
-                 [tile("m_raw2%d" % h, [P, PACK, P], F32) for h in range(HALVES)]]
+        s_table = landed("s_table", [P, T], U8, 7 * KIB)
+        x_raw = [landed("x_raw%d" % u, [P, 2, R], F32, (16 + 8 * u) * KIB) for u in range(2)]
         wt_rows = tile("wt_rows", [P, HALF], F32)
         identity = tile("identity", [P, P], F32)
         windows = [tile("window%d" % j, [P, T], F32) for j in range(D_BLOCKS)]
@@ -65,34 +66,30 @@ def tile_attend_ghv_nce_kernel(tc, xT, w_words, w_scales, vT, wt, xm, offs, out)
             nc.vector.memset(words[:, :odd], 0)
             nc.vector.memset(words[:, odd:], 0)
 
-        zero_on_vector(s_table[:].bitcast(I32))
+        s_spread = tile("s_spread", [P, N], U8)
+        w_bytes = tile("w_bytes", [P, N], U8)
+        nc.gpsimd.memset(s_table[:].bitcast(I32), 0)
         zero_on_vector(wt_rows[:].bitcast(I32))
+        zero_on_vector(w_bytes[:].bitcast(I32))
         make_identity(nc, identity[:])
 
         nc.sync.dma_start(w_table[:].bitcast(I32), w_words[0].rearrange("p n t -> p (n t)").bitcast(I32))
+        nc.sync.dma_start(s_table[SCALE_ROW:P:8, :].bitcast(I32), w_scales[0].bitcast(I32))
         nc.sync.dma_start(offsets[:], offs)
-        for i in range(4):
-            nc.sync.dma_start(s_table[i:P:32, :].bitcast(I32), w_scales[0][i:16:4, :].bitcast(I32))
         x_rows = xT[0].rearrange("(p j) r -> p j r", j=PACK)
         nc.sync.dma_start(x_raw[0][:], x_rows[:, :2, :])
         nc.sync.dma_start(wt_rows[WT_ROW:P:64, :], wt[0].rearrange("(h r) o -> h (r o)", h=HALVES))
         nc.sync.dma_start(x_raw[1][:], x_rows[:, 2:, :])
-        v_rows = vT.rearrange("(p j) c -> p j c", j=PACK)
-        for j in range(PACK):
-            nc.sync.dma_start(v_table[j][:], v_rows[:, j, :])
-        for u, (d0, d1) in enumerate(((0, 2 * P), (2 * P, 3 * P), (3 * P, D))):
-            for h in (1, 0):
-                rows = xm[0][h * HALF : (h + 1) * HALF, d0:d1]
-                nc.sync.dma_start(m_raw[u][h][:], rows.rearrange("(p t) d -> p t d", t=PACK))
 
         zero_on_vector(windows[0][:].bitcast(I32))
         for window in windows[1:]:
             nc.gpsimd.memset(window[:].bitcast(I32), 0)
 
         w_codes = tile("w_codes", [P, N], U32)
-        w_bytes = tile("w_bytes", [P, N], U8)
+        nc.vector.tensor_copy(s_spread[:], s_table[:].indirect(offsets[:]))
+        for i in range(4):
+            nc.sync.dma_start(w_bytes[i:P:32, :].bitcast(I32), s_spread[SCALE_ROW + 8 * i : P : 32, :].bitcast(I32))
         nc.vector.tensor_copy(w_codes[:], w_table[:].indirect(offsets[:]))
-        nc.vector.tensor_copy(w_bytes[:], s_table[:].indirect(offsets[:]))
 
         x_bf = [tile("x_bf0", [P, HALF * PACK], BF16), placed("x_bf1", [P, HALF * PACK], BF16, 16 * KIB)]
         x_codes = [tile("x_codes%d" % h, [P, HALF], U32) for h in range(HALVES)]
@@ -139,6 +136,11 @@ def tile_attend_ghv_nce_kernel(tc, xT, w_words, w_scales, vT, wt, xm, offs, out)
             quant_x(*done)
         quant_x(*pieces[-1])
         quant_x(1, 0, PACK)
+
+        v_table = [landed("v_table%d" % j, [P, T], F32, 8 * j * KIB) for j in range(PACK)]
+        v_rows = vT.rearrange("(p j) c -> p j c", j=PACK)
+        for j in range(PACK):
+            nc.sync.dma_start(v_table[j][:], v_rows[:, j, :])
 
         def stationary(codes, scale_bytes, place):
             cols = slice(place * P, (place + 1) * P)
@@ -192,6 +194,14 @@ def tile_attend_ghv_nce_kernel(tc, xT, w_words, w_scales, vT, wt, xm, offs, out)
         for j in range(PACK - 1):
             for late in range(2):
                 gather_v(j, late)
+
+        m_raw = [[landed("m_raw00", [P, PACK, 2 * P], F32, 4 * KIB), landed("m_raw01", [P, PACK, 2 * P], F32, 0)],
+                 [landed("m_raw10", [P, PACK, P], F32, 8 * KIB), landed("m_raw11", [P, PACK, P], F32, 12 * KIB)],
+                 [landed("m_raw20", [P, PACK, P], F32, 18 * KIB), landed("m_raw21", [P, PACK, P], F32, 16 * KIB)]]
+        for u, (d0, d1) in enumerate(((0, 2 * P), (2 * P, 3 * P), (3 * P, D))):
+            for h in (1, 0):
+                rows = xm[0][h * HALF : (h + 1) * HALF, d0:d1]
+                nc.sync.dma_start(m_raw[u][h][:], rows.rearrange("(p t) d -> p t d", t=PACK))
 
         v_codes = tile("v_codes", [P, N], U32)
         v_bytes = tile("v_bytes", [P, N], U8)
@@ -254,10 +264,10 @@ def tile_attend_ghv_nce_kernel(tc, xT, w_words, w_scales, vT, wt, xm, offs, out)
         weave_on_gpsimd(m_bf_g[:, 0, :], m_raw[0][1][:, :, P:])
         weave_on_gpsimd(m_bf_g[:, 1, : CAST_SHARE * PACK], m_raw[1][1][:, :, :CAST_SHARE])
         weave(m_bf_g[:, 1, CAST_SHARE * PACK :], m_raw[1][1][:, :, CAST_SHARE:])
-        av_first = placed("av_first", [P, PACK, P], F32, 8 * KIB)
+        av_first = landed("av_first", [P, PACK, P], F32, 4 * KIB)
         nc.scalar.activation(av_first[:], late_av[0, 3][:], ACT.Copy)
         weave(m_bf_a[:, 1, 1, :], m_raw[1][0][:])
-        av_rest = placed("av_rest", [P, 2, BLOCK], F32, 12 * KIB)
+        av_rest = landed("av_rest", [P, 2, BLOCK], F32, 8 * KIB)
         av_second = av_rest[:, 0, : PACK * MIDDLE].rearrange("p (t c) -> p t c", t=PACK)
         nc.scalar.activation(av_second[:, :, P - LAST :], late_av[1, 3][:, :, : P - KEPT], ACT.Copy)
         nc.scalar.activation(av_second[:, :, : P - LAST], late_av[1, 2][:, :, LAST:], ACT.Copy)
@@ -301,7 +311,7 @@ def tile_attend_ghv_nce_kernel(tc, xT, w_words, w_scales, vT, wt, xm, offs, out)
                                 as_tiles(factor[:, 1, :, N - KEPT :]), ALU.mult)
         product(g_late0[:, :BLOCK], 0, 2, late_av[0, 2])
         weave(g_late0[:, BLOCK:], g_rows0[:])
-        staged_second = placed("staged_second", [P, EARLY_SLOTS], F32, 8 * KIB)
+        staged_second = landed("staged_second", [P, EARLY_SLOTS], F32, 4 * KIB)
         nc.scalar.activation(staged_second[:], early_sums[1][:, early_cols], ACT.Copy)
         weave(g_late1[:, : (P - KEPT) * PACK], g_rows1[:, :, P - LAST :])
 

@@ -32,7 +32,6 @@ SCALE_ROW = 4
 LAST = 104
 KEPT = 52
 MIDDLE = EARLY_SLOTS - LAST - KEPT
-CAST_SHARE = 96
 KIB = 1024
 
 
@@ -245,13 +244,12 @@ def tile_attend_ghv_nce_kernel(tc, xT, w_words, w_scales, vT, wt, xm, offs, out)
 
         gather_v(PACK - 1, 0)
         quant_v(0, 1, slice(0, 1))
-        quant_v(1, 2, slice(3, 4))
         gather_v(PACK - 1, 1)
-
-        early_av = [[direction(h, b, "av") for b in range(2)] for h in range(HALVES)]
-        g_early = [tile("g_first0", [P, 2 * BLOCK], BF16), placed("g_first1", [P, 2 * BLOCK], BF16, 6 * KIB)]
-        product(g_early[0][:, :BLOCK], 0, 0, early_av[0][0])
+        quant_v(1, 2, slice(3, 4))
         quant_v(2, 4, slice(1, 3))
+
+        early_av = {(h, b): direction(h, b, "av") for h in range(HALVES) for b in range(2)}
+        g_early = [tile("g_first0", [P, 2 * BLOCK], BF16), tile("g_first1", [P, 2 * BLOCK], BF16)]
         late_av = {(h, b): direction(h, b, "wide") for h, b in ((0, 3), (1, 3), (1, 2), (0, 2))}
 
         m_bf_a = placed("m_bf_a", [P, 2, 2, BLOCK], BF16, 0)
@@ -262,8 +260,7 @@ def tile_attend_ghv_nce_kernel(tc, xT, w_words, w_scales, vT, wt, xm, offs, out)
         weave(m_bf_a[:, 0, 0, :], m_raw[0][0][:, :, :P])
         weave(m_bf_a[:, 1, 0, :], m_raw[0][0][:, :, P:])
         weave_on_gpsimd(m_bf_g[:, 0, :], m_raw[0][1][:, :, P:])
-        weave_on_gpsimd(m_bf_g[:, 1, : CAST_SHARE * PACK], m_raw[1][1][:, :, :CAST_SHARE])
-        weave(m_bf_g[:, 1, CAST_SHARE * PACK :], m_raw[1][1][:, :, CAST_SHARE:])
+        weave_on_gpsimd(m_bf_g[:, 1, :], m_raw[1][1][:])
         av_first = landed("av_first", [P, PACK, P], F32, 4 * KIB)
         nc.scalar.activation(av_first[:], late_av[0, 3][:], ACT.Copy)
         weave(m_bf_a[:, 1, 1, :], m_raw[1][0][:])
@@ -276,8 +273,8 @@ def tile_attend_ghv_nce_kernel(tc, xT, w_words, w_scales, vT, wt, xm, offs, out)
 
         m_codes = [tile("m_codes%d" % pair, [P, 2 * P], U32) for pair in range(D_BLOCKS)]
         m_bytes = [tile("m_bytes%d" % pair, [P, 2 * P], U8) for pair in range(D_BLOCKS)]
-        for h, b in ((0, 1), (1, 0), (1, 1)):
-            product(g_early[h][:, b * BLOCK : (b + 1) * BLOCK], h, b, early_av[h][b])
+        for h, b in early_av:
+            product(g_early[h][:, b * BLOCK : (b + 1) * BLOCK], h, b, early_av[h, b])
         quant_g(0, 0, EARLY_SLOTS, g_early[0][:])
         quant_m(0, m_bf_a[:, 0])
         quant_g(1, 0, EARLY_SLOTS, g_early[1][:])

@@ -25,13 +25,10 @@ SLOT_BLOCKS = N // P
 D_BLOCKS = D // P
 BLOCK = P * PACK
 EARLY_SLOTS = N // 2
-EARLY_BLOCKS = 3
 PSUM_BUFS = 4
 WT_ROW = 16
 SCALE_ROW = 4
-LAST = 104
-KEPT = 52
-MIDDLE = EARLY_SLOTS - LAST - KEPT
+SHARE = 128
 KIB = 1024
 
 
@@ -120,8 +117,7 @@ def tile_attend_ghv_nce_kernel(tc, xT, w_words, w_scales, vT, wt, xm, offs, out)
             nc.gpsimd.memset(g_codes[h][:, EARLY_SLOTS:].bitcast(I32), 0)
             nc.gpsimd.memset(g_bytes[h][:, EARLY_SLOTS:].bitcast(I32), 0)
         cast_x(0, 0, 0, PACK)
-        for u in range(2):
-            cast_x_on_scalar(u)
+        cast_x_on_scalar(0)
         wt_turned = ps.tile([P, PACK, P], F32, name="av")
         for t in range(PACK):
             nc.tensor.transpose(wt_turned[:, t, :], wt_rows[:, t:HALF:PACK], identity[:])
@@ -133,6 +129,7 @@ def tile_attend_ghv_nce_kernel(tc, xT, w_words, w_scales, vT, wt, xm, offs, out)
         for done, ahead in zip(pieces, pieces[1:]):
             cast_x(1, *ahead)
             quant_x(*done)
+        cast_x(1, 1, 0, PACK)
         quant_x(*pieces[-1])
         quant_x(1, 0, PACK)
 
@@ -162,17 +159,14 @@ def tile_attend_ghv_nce_kernel(tc, xT, w_words, w_scales, vT, wt, xm, offs, out)
 
         def affine(h, t):
             c, mc = quarter[:, h, t : t + 1], minus_quarter[:, h, t : t + 1]
-            if h == 0 or t == 0:
-                squared = sq_first[:, t, :] if h == 0 and t < 2 else sq[h][:, t, :]
-                nc.gpsimd.tensor_scalar(factor[:, h, t, :], squared, mc, c, ALU.mult, ALU.add)
+            if h == 0 or t < PACK - 1:
+                nc.gpsimd.tensor_scalar(factor[:, h, t, :], sq[h][:, t, :], mc, c, ALU.mult, ALU.add)
             else:
                 nc.scalar.activation(factor[:, h, t, :], sq[h][:, t, :], ACT.Identity, bias=c, scale=mc)
 
         for t in range(PACK):
             score(0, t)
-        sq_first = placed("sq_first", [P, 2, N], F32, 16 * KIB)
-        for t in range(2):
-            nc.gpsimd.tensor_tensor(sq_first[:, t, :], th[0][:, t, :], th[0][:, t, :], ALU.mult)
+        nc.vector.tensor_tensor(sq[0][:, :2, :], th[0][:, :2, :], th[0][:, :2, :], ALU.mult)
         square(0, 2, 4)
         for t0 in (0, 2):
             score(1, t0)
@@ -194,27 +188,27 @@ def tile_attend_ghv_nce_kernel(tc, xT, w_words, w_scales, vT, wt, xm, offs, out)
             for late in range(2):
                 gather_v(j, late)
 
-        m_raw = [[landed("m_raw00", [P, PACK, 2 * P], F32, 4 * KIB), landed("m_raw01", [P, PACK, 2 * P], F32, 0)],
-                 [landed("m_raw10", [P, PACK, P], F32, 8 * KIB), landed("m_raw11", [P, PACK, P], F32, 12 * KIB)],
-                 [landed("m_raw20", [P, PACK, P], F32, 18 * KIB), landed("m_raw21", [P, PACK, P], F32, 16 * KIB)]]
-        for u, (d0, d1) in enumerate(((0, 2 * P), (2 * P, 3 * P), (3 * P, D))):
-            for h in (1, 0):
-                rows = xm[0][h * HALF : (h + 1) * HALF, d0:d1]
+        m_raw = [[landed("m_raw%d%d" % (u, h), [P, PACK, 2 * P], F32, (8 * u + 4 * h) * KIB) for h in range(HALVES)]
+                 for u in range(2)]
+        for u in range(2):
+            for h in range(HALVES):
+                rows = xm[0][h * HALF : (h + 1) * HALF, 2 * u * P : 2 * (u + 1) * P]
                 nc.sync.dma_start(m_raw[u][h][:], rows.rearrange("(p t) d -> p t d", t=PACK))
 
-        v_codes = tile("v_codes", [P, N], U32)
-        v_bytes = tile("v_bytes", [P, N], U8)
+        av_early = placed("av_early", [P, BLOCK], F32, 24 * KIB)
+        v_codes = [tile("v_codes%d" % late, [P, EARLY_SLOTS], U32) for late in range(2)]
+        v_bytes = [tile("v_bytes%d" % late, [P, EARLY_SLOTS], U8) for late in range(2)]
 
-        def quant_v(b0, b1, places):
+        def quant_v(late, b0, b1, places):
             cols = slice(b0 * P, b1 * P)
-            nc.vector.quantize_mx(v_codes[:, cols].bitcast(E4M3), v_bytes[:, cols],
+            nc.vector.quantize_mx(v_codes[late][:, cols].bitcast(E4M3), v_bytes[late][:, cols],
                                   v_bf[:, places].rearrange("p b n j -> p (b n j)"))
 
         def direction(h, b, tag):
-            cols = slice(b * P, (b + 1) * P)
+            late, cols = b // 2, slice(b % 2 * P, (b % 2 + 1) * P)
             av = ps.tile([P, PACK, P], F32, name=tag)
             for t in range(PACK):
-                nc.tensor.matmul_mx(av[:, t, :], rhs=v_codes[:, cols].bitcast(E4M3), rhs_scale=v_bytes[:, cols],
+                nc.tensor.matmul_mx(av[:, t, :], rhs=v_codes[late][:, cols].bitcast(E4M3), rhs_scale=v_bytes[late][:, cols],
                                     start=True, stop=True, **stationary(x_codes[h], x_bytes[h], t))
             return av
 
@@ -224,119 +218,130 @@ def tile_attend_ghv_nce_kernel(tc, xT, w_words, w_scales, vT, wt, xm, offs, out)
         def as_tiles(rows):
             return rows.rearrange("p t (c i) -> p c t i", i=2)
 
-        def product(g_block, h, b, av):
-            nc.vector.tensor_tensor(as_words(g_block), as_tiles(av[:]), as_tiles(factor[:, h, :, b * P : (b + 1) * P]), ALU.mult)
+        def as_walked(values):
+            return values.rearrange("p (c t i) -> p c t i", t=PACK, i=2)
+
+        def product(g_slots, h, n0, n1, av):
+            nc.vector.tensor_tensor(as_words(g_slots), as_tiles(av), as_tiles(factor[:, h, :, n0:n1]), ALU.mult)
+
+        def product_on_gpsimd(g_slots, h, n0, n1, av):
+            nc.gpsimd.tensor_tensor(as_words(g_slots), as_walked(av), as_tiles(factor[:, h, :, n0:n1]), ALU.mult)
 
         def quant_g(h, n0, n1, g_slots):
             cols = slice(n0, n1)
             nc.vector.quantize_mx(g_codes[h][:, cols].bitcast(E5M2), g_bytes[h][:, cols], g_slots)
 
-        def weave(words, rows):
-            nc.scalar.activation(words.rearrange("p (c i t) -> p c t i", i=4, t=PACK),
+        def weave(j, h):
+            rows = m_raw[j // 2][h][:, :, j % 2 * P : (j % 2 + 1) * P]
+            nc.scalar.activation(m_bf[j][:, h, :].rearrange("p (c i t) -> p c t i", i=4, t=PACK),
                                  rows.rearrange("p t (c i) -> p c t i", i=4), ACT.Copy)
 
-        def weave_on_gpsimd(words, rows):
-            nc.gpsimd.tensor_scalar(words.rearrange("p (c t) -> p c t", t=PACK), rows.rearrange("p t c -> p c t"),
+        def weave_on_gpsimd(j, h):
+            rows = m_raw[j // 2][h][:, :, j % 2 * P : (j % 2 + 1) * P]
+            nc.gpsimd.tensor_scalar(m_bf[j][:, h, :].rearrange("p (c t) -> p c t", t=PACK), rows.rearrange("p t c -> p c t"),
                                     1.0, 0.0, ALU.mult, ALU.add)
 
-        def quant_m(pair, m_pair):
-            nc.vector.quantize_mx(m_codes[pair][:].bitcast(E4M3), m_bytes[pair][:], m_pair.rearrange("p k n -> p (k n)"))
+        def quant_m(j):
+            nc.vector.quantize_mx(m_codes[j][:].bitcast(E4M3), m_bytes[j][:], m_bf[j][:].rearrange("p h n -> p (h n)"))
 
-        gather_v(PACK - 1, 0)
-        quant_v(0, 1, slice(0, 1))
-        gather_v(PACK - 1, 1)
-        quant_v(1, 2, slice(3, 4))
-        quant_v(2, 4, slice(1, 3))
-
-        early_av = {(h, b): direction(h, b, "av") for h in range(HALVES) for b in range(2)}
-        g_early = [tile("g_first0", [P, 2 * BLOCK], BF16), tile("g_first1", [P, 2 * BLOCK], BF16)]
-        late_av = {(h, b): direction(h, b, "wide") for h, b in ((0, 3), (1, 3), (1, 2), (0, 2))}
-
-        m_bf_a = placed("m_bf_a", [P, 2, 2, BLOCK], BF16, 0)
-        m_bf_g = placed("m_bf_g", [P, 2, BLOCK], BF16, 4 * KIB)
-        m_place = {(0, 0): (0, 0), (0, 1): (0, 1), (1, 1): (1, 0), (2, 1): (1, 1),
-                   (1, 0): (2, 0), (2, 0): (2, 1), (3, 0): (3, 0), (3, 1): (3, 1)}
-        weave(m_bf_a[:, 0, 1, :], m_raw[0][1][:, :, :P])
-        weave(m_bf_a[:, 0, 0, :], m_raw[0][0][:, :, :P])
-        weave(m_bf_a[:, 1, 0, :], m_raw[0][0][:, :, P:])
-        weave_on_gpsimd(m_bf_g[:, 0, :], m_raw[0][1][:, :, P:])
-        weave_on_gpsimd(m_bf_g[:, 1, :], m_raw[1][1][:])
-        av_first = landed("av_first", [P, PACK, P], F32, 4 * KIB)
-        nc.scalar.activation(av_first[:], late_av[0, 3][:], ACT.Copy)
-        weave(m_bf_a[:, 1, 1, :], m_raw[1][0][:])
-        av_rest = landed("av_rest", [P, 2, BLOCK], F32, 8 * KIB)
-        av_second = av_rest[:, 0, : PACK * MIDDLE].rearrange("p (t c) -> p t c", t=PACK)
-        nc.scalar.activation(av_second[:, :, P - LAST :], late_av[1, 3][:, :, : P - KEPT], ACT.Copy)
-        nc.scalar.activation(av_second[:, :, : P - LAST], late_av[1, 2][:, :, LAST:], ACT.Copy)
-        av_third = av_rest[:, 1, : PACK * LAST].rearrange("p (c t i) -> p c t i", t=PACK, i=2)
-        nc.scalar.activation(av_third, as_tiles(late_av[1, 2][:, :, :LAST]), ACT.Copy)
-
-        m_codes = [tile("m_codes%d" % pair, [P, 2 * P], U32) for pair in range(D_BLOCKS)]
-        m_bytes = [tile("m_bytes%d" % pair, [P, 2 * P], U8) for pair in range(D_BLOCKS)]
-        for h, b in early_av:
-            product(g_early[h][:, b * BLOCK : (b + 1) * BLOCK], h, b, early_av[h, b])
-        quant_g(0, 0, EARLY_SLOTS, g_early[0][:])
-        quant_m(0, m_bf_a[:, 0])
-        quant_g(1, 0, EARLY_SLOTS, g_early[1][:])
-        quant_m(1, m_bf_g[:])
-        quant_m(2, m_bf_a[:, 1])
-
-        def dw_pass(bank, h, j):
-            pair, place = m_place[j, h]
+        def dw_pass(bank, h, j, first=0):
             nc.tensor.matmul_mx(bank[:], rhs=g_codes[h][:].bitcast(E5M2), rhs_scale=g_bytes[h][:],
-                                start=(h == 0), stop=(h == HALVES - 1),
-                                **stationary(m_codes[pair], m_bytes[pair], place))
+                                start=(h == first), stop=(h != first), **stationary(m_codes[j], m_bytes[j], h))
 
         def scatter(j, cols, values):
             nc.vector.tensor_copy(windows[j][:].indirect(listed(cols.start, cols.stop)), values)
 
-        early_cols = slice(0, EARLY_SLOTS)
-        early_sums = [ps.tile([P, N], F32, name="av") for j in range(EARLY_BLOCKS)]
-        for j in range(EARLY_BLOCKS):
-            for h in range(HALVES):
-                dw_pass(early_sums[j], h, j)
-        staged = [tile("staged%d" % j, [P, N], F32) for j in range(D_BLOCKS)]
-        nc.scalar.activation(staged[0][:, early_cols], early_sums[0][:, early_cols], ACT.Copy)
+        def scatter_on_scalar(j, cols, values):
+            nc.scalar.activation(windows[j][:].indirect(listed(cols.start, cols.stop)), values, ACT.Copy)
 
-        g_late0 = placed("g_late0", [P, 2 * BLOCK], BF16, KIB)
-        g_late1 = placed("g_late1", [P, BLOCK], BF16, 5 * KIB)
-        g_rows0 = placed("g_rows0", [P, PACK, P], BF16, 4 * KIB - KIB // 2)
-        g_rows1 = placed("g_rows1", [P, PACK, MIDDLE], BF16, 0)
-        nc.gpsimd.tensor_tensor(g_rows0[:], av_first[:], factor[:, 0, :, 3 * P :], ALU.mult)
-        nc.gpsimd.tensor_tensor(g_rows1[:], av_second, factor[:, 1, :, 2 * P + LAST : N - KEPT], ALU.mult)
-        nc.vector.tensor_tensor(as_words(g_late1[:, (P - KEPT) * PACK :]), as_tiles(late_av[1, 3][:, :, P - KEPT :]),
-                                as_tiles(factor[:, 1, :, N - KEPT :]), ALU.mult)
-        product(g_late0[:, :BLOCK], 0, 2, late_av[0, 2])
-        weave(g_late0[:, BLOCK:], g_rows0[:])
-        staged_second = landed("staged_second", [P, EARLY_SLOTS], F32, 4 * KIB)
-        nc.scalar.activation(staged_second[:], early_sums[1][:, early_cols], ACT.Copy)
-        weave(g_late1[:, : (P - KEPT) * PACK], g_rows1[:, :, P - LAST :])
-
-        scatter(0, early_cols, staged[0][:, early_cols])
-        quant_g(0, EARLY_SLOTS, N, g_late0[:])
-        g_last = placed("g_last", [P, BLOCK], BF16, KIB)
-        nc.gpsimd.tensor_tensor(as_words(g_last[:, : LAST * PACK]), av_third, as_tiles(factor[:, 1, :, 2 * P : 2 * P + LAST]), ALU.mult)
-        weave(g_last[:, LAST * PACK :], g_rows1[:, :, : P - LAST])
-        sums = [ps.tile([P, N], F32, name="wide") for j in range(D_BLOCKS)]
-        for j in range(EARLY_BLOCKS):
-            dw_pass(sums[j], 0, j)
-        scatter(1, early_cols, staged_second[:])
-        staged_third = placed("staged_third", [P, EARLY_SLOTS], F32, 0)
-        nc.scalar.activation(staged_third[:], early_sums[2][:, early_cols], ACT.Copy)
-        quant_g(1, 3 * P, N, g_late1[:])
-        quant_g(1, 2 * P, 3 * P, g_last[:])
-        m_bf_b = placed("m_bf_b", [P, HALVES, BLOCK], BF16, KIB)
-        for h in range(HALVES):
-            weave_on_gpsimd(m_bf_b[:, h, :], m_raw[2][h][:])
-        scatter(2, early_cols, staged_third[:])
-
-        for j in range(D_BLOCKS):
-            cols = slice(EARLY_SLOTS if j < EARLY_BLOCKS else 0, N)
-            if j == EARLY_BLOCKS:
-                dw_pass(sums[j], 0, j)
-            dw_pass(sums[j], 1, j)
-            nc.scalar.activation(staged[j][:, cols], sums[j][:, cols], ACT.Copy)
-            if j == 1:
-                quant_m(3, m_bf_b[:])
-            scatter(j, cols, staged[j][:, cols])
+        def store(j):
             nc.sync.dma_start(out[j * P : (j + 1) * P, :], windows[j][:])
+
+        early_cols, late_cols = slice(0, EARLY_SLOTS), slice(EARLY_SLOTS, N)
+
+        gather_v(PACK - 1, 0)
+        quant_v(0, 0, 1, slice(0, 1))
+        quant_v(0, 1, 2, slice(3, 4))
+        gather_v(PACK - 1, 1)
+        quant_v(1, 0, 2, slice(1, 3))
+
+        early_av = {(h, b): direction(h, b, "av") for h in range(HALVES) for b in range(2)}
+        late_av = {(h, b): direction(h, b, "wide") for h, b in ((0, 3), (0, 2), (1, 2), (1, 3))}
+        g_first = placed("g_first", [P, BLOCK], BF16, 5 * KIB)
+        g_second = tile("g_second", [P, BLOCK], BF16)
+        g_early = tile("g_early", [P, 2 * BLOCK], BF16)
+        m_bf = [placed("m_bf0", [P, HALVES, BLOCK], BF16, 8 * KIB), placed("m_bf1", [P, HALVES, BLOCK], BF16, 30 * KIB), None, None]
+        nc.scalar.activation(as_walked(av_early[:]), as_tiles(early_av[0, 0][:]), ACT.Copy)
+        for h in range(HALVES):
+            for j in range(2):
+                weave(j, h)
+        product_on_gpsimd(g_first[:], 0, 0, P, av_early[:])
+        product(g_second[:], 0, P, 2 * P, early_av[0, 1][:])
+        for b in range(2):
+            product(g_early[:, b * BLOCK : (b + 1) * BLOCK], 1, b * P, (b + 1) * P, early_av[1, b][:])
+
+        m_codes = [placed("m_codes%d" % j, [P, HALVES * P], U32, (24 + j) * KIB) for j in (0, 1)]
+        m_codes += [None, tile("m_codes3", [P, HALVES * P], U32)]
+        m_bytes = [tile("m_bytes%d" % j, [P, HALVES * P], U8) for j in range(D_BLOCKS)]
+        kept = EARLY_SLOTS - SHARE
+        av_late = tile("av_late", [P, PACK * SHARE], F32)
+        nc.scalar.activation(as_walked(av_late[:, PACK * (SHARE - P) :]), as_tiles(late_av[0, 3][:]), ACT.Copy)
+        quant_g(0, 0, P, g_first[:])
+        quant_g(0, P, 2 * P, g_second[:])
+        quant_m(0)
+        quant_g(1, 0, EARLY_SLOTS, g_early[:])
+        early_sums = [ps.tile([P, N], F32, name="av") for j in range(2)]
+        for h in range(HALVES):
+            dw_pass(early_sums[0], h, 0)
+        quant_m(1)
+        for h in range(HALVES):
+            dw_pass(early_sums[1], h, 1)
+
+        m_bf[2] = placed("m_bf2", [P, HALVES, BLOCK], BF16, 8 * KIB)
+        weave(2, 0)
+        staged = {j: tile("staged%d" % j, [P, N], F32) for j in (0, 2, 3)}
+        nc.scalar.activation(staged[0][:, early_cols], early_sums[0][:, early_cols], ACT.Copy)
+        scatter_on_scalar(0, early_cols, staged[0][:, early_cols])
+        weave(2, 1)
+
+        g_late = [placed("g_late0", [P, 2 * BLOCK], BF16, 31 * KIB), placed("g_late1", [P, 2 * BLOCK], BF16, 29 * KIB)]
+        product_on_gpsimd(g_late[0][:, kept * PACK :], 0, N - SHARE, N, av_late[:])
+        for b in (2, 3):
+            product(g_late[1][:, (b - 2) * BLOCK : (b - 1) * BLOCK], 1, b * P, (b + 1) * P, late_av[1, b][:])
+        product(g_late[0][:, : kept * PACK], 0, EARLY_SLOTS, N - SHARE, late_av[0, 2][:, :, :kept])
+        quant_g(1, EARLY_SLOTS, N, g_late[1][:])
+        quant_g(0, EARLY_SLOTS, N, g_late[0][:])
+        sums = [ps.tile([P, N], F32, name=tag) for tag in ("av", "av", "wide", "wide")]
+        for j in range(2):
+            for h in (1, 0):
+                dw_pass(sums[j], h, j, first=1)
+
+        nc.scalar.activation(staged[0][:, late_cols], sums[0][:, late_cols], ACT.Copy)
+        scatter_on_scalar(0, late_cols, staged[0][:, late_cols])
+        store(0)
+        staged_early = placed("staged_early", [P, EARLY_SLOTS], F32, 31 * KIB)
+        nc.vector.tensor_copy(staged_early[:], early_sums[1][:, early_cols])
+        m_codes[2] = placed("m_codes2", [P, HALVES * P], U32, 32 * KIB)
+        quant_m(2)
+        for h in range(HALVES):
+            dw_pass(sums[2], h, 2)
+        m_bf[3] = placed("m_bf3", [P, HALVES, BLOCK], BF16, 8 * KIB)
+        for h in range(HALVES):
+            weave_on_gpsimd(3, h)
+        scatter(1, early_cols, staged_early[:])
+        quant_m(3)
+        for h in range(HALVES):
+            dw_pass(sums[3], h, 3)
+        staged_late = placed("staged_late", [P, EARLY_SLOTS], F32, 8 * KIB)
+        nc.vector.tensor_copy(staged_late[:], sums[1][:, late_cols])
+        scatter(1, late_cols, staged_late[:])
+        store(1)
+        for cols in (early_cols, late_cols):
+            nc.scalar.activation(staged[2][:, cols], sums[2][:, cols], ACT.Copy)
+            scatter_on_scalar(2, cols, staged[2][:, cols])
+        store(2)
+        for cols in (early_cols, late_cols):
+            nc.vector.tensor_copy(staged[3][:, cols], sums[3][:, cols])
+        for cols in (early_cols, late_cols):
+            scatter(3, cols, staged[3][:, cols])
+        store(3)

@@ -117,7 +117,8 @@ def tile_attend_ghv_nce_kernel(tc, xT, w_words, w_scales, vT, wt, xm, offs, out)
             nc.gpsimd.memset(g_codes[h][:, EARLY_SLOTS:].bitcast(I32), 0)
             nc.gpsimd.memset(g_bytes[h][:, EARLY_SLOTS:].bitcast(I32), 0)
         cast_x(0, 0, 0, PACK)
-        cast_x_on_scalar(0)
+        for u in range(2):
+            cast_x_on_scalar(u)
         wt_turned = ps.tile([P, PACK, P], F32, name="av")
         for t in range(PACK):
             nc.tensor.transpose(wt_turned[:, t, :], wt_rows[:, t:HALF:PACK], identity[:])
@@ -129,7 +130,6 @@ def tile_attend_ghv_nce_kernel(tc, xT, w_words, w_scales, vT, wt, xm, offs, out)
         for done, ahead in zip(pieces, pieces[1:]):
             cast_x(1, *ahead)
             quant_x(*done)
-        cast_x(1, 1, 0, PACK)
         quant_x(*pieces[-1])
         quant_x(1, 0, PACK)
 
@@ -159,14 +159,17 @@ def tile_attend_ghv_nce_kernel(tc, xT, w_words, w_scales, vT, wt, xm, offs, out)
 
         def affine(h, t):
             c, mc = quarter[:, h, t : t + 1], minus_quarter[:, h, t : t + 1]
-            if h == 0 or t < PACK - 1:
-                nc.gpsimd.tensor_scalar(factor[:, h, t, :], sq[h][:, t, :], mc, c, ALU.mult, ALU.add)
+            if h == 0 or t == 0:
+                squared = sq_first[:, t, :] if h == 0 and t < 2 else sq[h][:, t, :]
+                nc.gpsimd.tensor_scalar(factor[:, h, t, :], squared, mc, c, ALU.mult, ALU.add)
             else:
                 nc.scalar.activation(factor[:, h, t, :], sq[h][:, t, :], ACT.Identity, bias=c, scale=mc)
 
         for t in range(PACK):
             score(0, t)
-        nc.vector.tensor_tensor(sq[0][:, :2, :], th[0][:, :2, :], th[0][:, :2, :], ALU.mult)
+        sq_first = placed("sq_first", [P, 2, N], F32, 16 * KIB)
+        for t in range(2):
+            nc.gpsimd.tensor_tensor(sq_first[:, t, :], th[0][:, t, :], th[0][:, t, :], ALU.mult)
         square(0, 2, 4)
         for t0 in (0, 2):
             score(1, t0)
@@ -191,11 +194,10 @@ def tile_attend_ghv_nce_kernel(tc, xT, w_words, w_scales, vT, wt, xm, offs, out)
         m_raw = [[landed("m_raw%d%d" % (u, h), [P, PACK, 2 * P], F32, (8 * u + 4 * h) * KIB) for h in range(HALVES)]
                  for u in range(2)]
         for u in range(2):
-            for h in range(HALVES):
+            for h in (1, 0):
                 rows = xm[0][h * HALF : (h + 1) * HALF, 2 * u * P : 2 * (u + 1) * P]
                 nc.sync.dma_start(m_raw[u][h][:], rows.rearrange("(p t) d -> p t d", t=PACK))
 
-        av_early = placed("av_early", [P, BLOCK], F32, 24 * KIB)
         v_codes = [tile("v_codes%d" % late, [P, EARLY_SLOTS], U32) for late in range(2)]
         v_bytes = [tile("v_bytes%d" % late, [P, EARLY_SLOTS], U8) for late in range(2)]
 
@@ -263,33 +265,27 @@ def tile_attend_ghv_nce_kernel(tc, xT, w_words, w_scales, vT, wt, xm, offs, out)
         quant_v(0, 0, 1, slice(0, 1))
         quant_v(0, 1, 2, slice(3, 4))
         gather_v(PACK - 1, 1)
-        quant_v(1, 0, 2, slice(1, 3))
 
         early_av = {(h, b): direction(h, b, "av") for h in range(HALVES) for b in range(2)}
-        late_av = {(h, b): direction(h, b, "wide") for h, b in ((0, 3), (0, 2), (1, 2), (1, 3))}
-        g_first = placed("g_first", [P, BLOCK], BF16, 5 * KIB)
-        g_second = tile("g_second", [P, BLOCK], BF16)
-        g_early = tile("g_early", [P, 2 * BLOCK], BF16)
-        m_bf = [placed("m_bf0", [P, HALVES, BLOCK], BF16, 8 * KIB), placed("m_bf1", [P, HALVES, BLOCK], BF16, 30 * KIB), None, None]
-        nc.scalar.activation(as_walked(av_early[:]), as_tiles(early_av[0, 0][:]), ACT.Copy)
-        for h in range(HALVES):
-            for j in range(2):
-                weave(j, h)
-        product_on_gpsimd(g_first[:], 0, 0, P, av_early[:])
-        product(g_second[:], 0, P, 2 * P, early_av[0, 1][:])
-        for b in range(2):
-            product(g_early[:, b * BLOCK : (b + 1) * BLOCK], 1, b * P, (b + 1) * P, early_av[1, b][:])
+        g_early = [tile("g_early%d" % h, [P, 2 * BLOCK], BF16) for h in range(HALVES)]
+        product(g_early[0][:, :BLOCK], 0, 0, P, early_av[0, 0][:])
+        quant_v(1, 0, 2, slice(1, 3))
+        late_av = {(h, b): direction(h, b, "wide") for h, b in ((0, 3), (1, 2), (1, 3), (0, 2))}
+        m_bf = [placed("m_bf%d" % j, [P, HALVES, BLOCK], BF16, (4 + 2 * j) * KIB) for j in range(2)] + [None, None]
+        for j in range(2):
+            weave(j, 0)
+            weave_on_gpsimd(j, 1)
+        for h, b in ((0, 1), (1, 0), (1, 1)):
+            product(g_early[h][:, b * BLOCK : (b + 1) * BLOCK], h, b * P, (b + 1) * P, early_av[h, b][:])
 
-        m_codes = [placed("m_codes%d" % j, [P, HALVES * P], U32, (24 + j) * KIB) for j in (0, 1)]
-        m_codes += [None, tile("m_codes3", [P, HALVES * P], U32)]
+        m_codes = [tile("m_codes%d" % j, [P, HALVES * P], U32) for j in (0, 1)] + [None, tile("m_codes3", [P, HALVES * P], U32)]
         m_bytes = [tile("m_bytes%d" % j, [P, HALVES * P], U8) for j in range(D_BLOCKS)]
         kept = EARLY_SLOTS - SHARE
         av_late = tile("av_late", [P, PACK * SHARE], F32)
         nc.scalar.activation(as_walked(av_late[:, PACK * (SHARE - P) :]), as_tiles(late_av[0, 3][:]), ACT.Copy)
-        quant_g(0, 0, P, g_first[:])
-        quant_g(0, P, 2 * P, g_second[:])
+        quant_g(0, 0, EARLY_SLOTS, g_early[0][:])
         quant_m(0)
-        quant_g(1, 0, EARLY_SLOTS, g_early[:])
+        quant_g(1, 0, EARLY_SLOTS, g_early[1][:])
         early_sums = [ps.tile([P, N], F32, name="av") for j in range(2)]
         for h in range(HALVES):
             dw_pass(early_sums[0], h, 0)
@@ -297,20 +293,20 @@ def tile_attend_ghv_nce_kernel(tc, xT, w_words, w_scales, vT, wt, xm, offs, out)
         for h in range(HALVES):
             dw_pass(early_sums[1], h, 1)
 
-        m_bf[2] = placed("m_bf2", [P, HALVES, BLOCK], BF16, 8 * KIB)
-        weave(2, 0)
+        m_bf[2] = placed("m_bf2", [P, HALVES, BLOCK], BF16, 4 * KIB)
+        weave(2, 1)
         staged = {j: tile("staged%d" % j, [P, N], F32) for j in (0, 2, 3)}
         nc.scalar.activation(staged[0][:, early_cols], early_sums[0][:, early_cols], ACT.Copy)
         scatter_on_scalar(0, early_cols, staged[0][:, early_cols])
-        weave(2, 1)
+        weave(2, 0)
 
-        g_late = [placed("g_late0", [P, 2 * BLOCK], BF16, 31 * KIB), placed("g_late1", [P, 2 * BLOCK], BF16, 29 * KIB)]
-        product_on_gpsimd(g_late[0][:, kept * PACK :], 0, N - SHARE, N, av_late[:])
+        g_late = placed("g_late", [P, HALVES, 2 * BLOCK], BF16, 7 * KIB)
+        product_on_gpsimd(g_late[:, 0, kept * PACK :], 0, N - SHARE, N, av_late[:])
         for b in (2, 3):
-            product(g_late[1][:, (b - 2) * BLOCK : (b - 1) * BLOCK], 1, b * P, (b + 1) * P, late_av[1, b][:])
-        product(g_late[0][:, : kept * PACK], 0, EARLY_SLOTS, N - SHARE, late_av[0, 2][:, :, :kept])
-        quant_g(1, EARLY_SLOTS, N, g_late[1][:])
-        quant_g(0, EARLY_SLOTS, N, g_late[0][:])
+            product(g_late[:, 1, (b - 2) * BLOCK : (b - 1) * BLOCK], 1, b * P, (b + 1) * P, late_av[1, b][:])
+        product(g_late[:, 0, : kept * PACK], 0, EARLY_SLOTS, N - SHARE, late_av[0, 2][:, :, :kept])
+        quant_g(1, EARLY_SLOTS, N, g_late[:, 1, :])
+        quant_g(0, EARLY_SLOTS, N, g_late[:, 0, :])
         sums = [ps.tile([P, N], F32, name=tag) for tag in ("av", "av", "wide", "wide")]
         for j in range(2):
             for h in (1, 0):
@@ -319,20 +315,20 @@ def tile_attend_ghv_nce_kernel(tc, xT, w_words, w_scales, vT, wt, xm, offs, out)
         nc.scalar.activation(staged[0][:, late_cols], sums[0][:, late_cols], ACT.Copy)
         scatter_on_scalar(0, late_cols, staged[0][:, late_cols])
         store(0)
-        staged_early = placed("staged_early", [P, EARLY_SLOTS], F32, 31 * KIB)
+        staged_early = placed("staged_early", [P, EARLY_SLOTS], F32, 8 * KIB)
         nc.vector.tensor_copy(staged_early[:], early_sums[1][:, early_cols])
-        m_codes[2] = placed("m_codes2", [P, HALVES * P], U32, 32 * KIB)
+        m_codes[2] = placed("m_codes2", [P, HALVES * P], U32, 9 * KIB)
         quant_m(2)
         for h in range(HALVES):
             dw_pass(sums[2], h, 2)
-        m_bf[3] = placed("m_bf3", [P, HALVES, BLOCK], BF16, 8 * KIB)
+        m_bf[3] = placed("m_bf3", [P, HALVES, BLOCK], BF16, 4 * KIB)
         for h in range(HALVES):
             weave_on_gpsimd(3, h)
         scatter(1, early_cols, staged_early[:])
         quant_m(3)
         for h in range(HALVES):
             dw_pass(sums[3], h, 3)
-        staged_late = placed("staged_late", [P, EARLY_SLOTS], F32, 8 * KIB)
+        staged_late = placed("staged_late", [P, EARLY_SLOTS], F32, 4 * KIB)
         nc.vector.tensor_copy(staged_late[:], sums[1][:, late_cols])
         scatter(1, late_cols, staged_late[:])
         store(1)

@@ -99,10 +99,10 @@ def tile_attend_ghv_nce_kernel(tc, xT, w_words, w_scales, vT, wt, xm, offs, out)
                 x_raw[u][:, :, h * HALF : (h + 1) * HALF].rearrange("p j (m t) -> p m j t", t=PACK)[:, :, :, t0:t1],
             )
 
-        def cast_x_on_scalar(u):
+        def cast_x_on_scalar(u, t1):
             nc.scalar.copy(
-                x_bf[1][:].rearrange("p (t m i j) -> p m t i j", t=PACK, i=2, j=PACK)[:, :, :, :, 2 * u : 2 * u + 2],
-                x_raw[u][:, :, HALF:].rearrange("p j (m i t) -> p m t i j", i=2, t=PACK),
+                x_bf[1][:].rearrange("p (t m i j) -> p m t i j", t=PACK, i=2, j=PACK)[:, :, :t1, :, 2 * u : 2 * u + 2],
+                x_raw[u][:, :, HALF:].rearrange("p j (m i t) -> p m t i j", i=2, t=PACK)[:, :, :t1],
             )
 
         def quant_x(h, t0, t1):
@@ -117,8 +117,8 @@ def tile_attend_ghv_nce_kernel(tc, xT, w_words, w_scales, vT, wt, xm, offs, out)
             nc.gpsimd.memset(g_codes[h][:, EARLY_SLOTS:].bitcast(I32), 0)
             nc.gpsimd.memset(g_bytes[h][:, EARLY_SLOTS:].bitcast(I32), 0)
         cast_x(0, 0, 0, PACK)
-        for u in range(2):
-            cast_x_on_scalar(u)
+        cast_x_on_scalar(0, PACK)
+        cast_x_on_scalar(1, 2)
         wt_turned = ps.tile([P, PACK, P], F32, name="av")
         for t in range(PACK):
             nc.tensor.transpose(wt_turned[:, t, :], wt_rows[:, t:HALF:PACK], identity[:])
@@ -130,6 +130,7 @@ def tile_attend_ghv_nce_kernel(tc, xT, w_words, w_scales, vT, wt, xm, offs, out)
         for done, ahead in zip(pieces, pieces[1:]):
             cast_x(1, *ahead)
             quant_x(*done)
+        cast_x(1, 1, 2, PACK)
         quant_x(*pieces[-1])
         quant_x(1, 0, PACK)
 
@@ -159,7 +160,7 @@ def tile_attend_ghv_nce_kernel(tc, xT, w_words, w_scales, vT, wt, xm, offs, out)
 
         def affine(h, t):
             c, mc = quarter[:, h, t : t + 1], minus_quarter[:, h, t : t + 1]
-            if h == 0 or t == 0:
+            if h == 0 or t < 2:
                 squared = sq_first[:, t, :] if h == 0 and t < 2 else sq[h][:, t, :]
                 nc.gpsimd.tensor_scalar(factor[:, h, t, :], squared, mc, c, ALU.mult, ALU.add)
             else:
@@ -233,18 +234,25 @@ def tile_attend_ghv_nce_kernel(tc, xT, w_words, w_scales, vT, wt, xm, offs, out)
             cols = slice(n0, n1)
             nc.vector.quantize_mx(g_codes[h][:, cols].bitcast(E5M2), g_bytes[h][:, cols], g_slots)
 
-        def weave(j, h):
-            rows = m_raw[j // 2][h][:, :, j % 2 * P : (j % 2 + 1) * P]
-            nc.scalar.activation(m_bf[j][:, h, :].rearrange("p (c i t) -> p c t i", i=4, t=PACK),
-                                 rows.rearrange("p t (c i) -> p c t i", i=4), ACT.Copy)
+        def raw(j, h):
+            return m_raw[j // 2][h][:, :, j % 2 * P : (j % 2 + 1) * P]
 
-        def weave_on_gpsimd(j, h):
-            rows = m_raw[j // 2][h][:, :, j % 2 * P : (j % 2 + 1) * P]
-            nc.gpsimd.tensor_scalar(m_bf[j][:, h, :].rearrange("p (c t) -> p c t", t=PACK), rows.rearrange("p t c -> p c t"),
+        def as_quads(words, rows):
+            return words.rearrange("p (c i t) -> p c t i", i=4, t=PACK), rows.rearrange("p t (c i) -> p c t i", i=4)
+
+        def weave(words, j, h):
+            nc.scalar.activation(*as_quads(words, raw(j, h)), ACT.Copy)
+
+        def weave_on_gpsimd(words, j, h):
+            nc.gpsimd.tensor_scalar(words.rearrange("p (c t) -> p c t", t=PACK), raw(j, h).rearrange("p t c -> p c t"),
                                     1.0, 0.0, ALU.mult, ALU.add)
 
-        def quant_m(j):
-            nc.vector.quantize_mx(m_codes[j][:].bitcast(E4M3), m_bytes[j][:], m_bf[j][:].rearrange("p h n -> p (h n)"))
+        def quant_m(j, h0, h1, words):
+            cols = slice(h0 * P, h1 * P)
+            nc.vector.quantize_mx(m_codes[j][:, cols].bitcast(E4M3), m_bytes[j][:, cols], words)
+
+        def both(m_block):
+            return m_block[:].rearrange("p h n -> p (h n)")
 
         def dw_pass(bank, h, j, first=0):
             nc.tensor.matmul_mx(bank[:], rhs=g_codes[h][:].bitcast(E5M2), rhs_scale=g_bytes[h][:],
@@ -271,10 +279,10 @@ def tile_attend_ghv_nce_kernel(tc, xT, w_words, w_scales, vT, wt, xm, offs, out)
         product(g_early[0][:, :BLOCK], 0, 0, P, early_av[0, 0][:])
         quant_v(1, 0, 2, slice(1, 3))
         late_av = {(h, b): direction(h, b, "wide") for h, b in ((0, 3), (1, 2), (1, 3), (0, 2))}
-        m_bf = [placed("m_bf%d" % j, [P, HALVES, BLOCK], BF16, (4 + 2 * j) * KIB) for j in range(2)] + [None, None]
+        m_bf = [placed("m_bf%d" % j, [P, HALVES, BLOCK], BF16, (4 + 2 * j) * KIB) for j in range(2)]
         for j in range(2):
-            weave(j, 0)
-            weave_on_gpsimd(j, 1)
+            weave(m_bf[j][:, 0, :], j, 0)
+            weave_on_gpsimd(m_bf[j][:, 1, :], j, 1)
         for h, b in ((0, 1), (1, 0), (1, 1)):
             product(g_early[h][:, b * BLOCK : (b + 1) * BLOCK], h, b * P, (b + 1) * P, early_av[h, b][:])
 
@@ -284,21 +292,20 @@ def tile_attend_ghv_nce_kernel(tc, xT, w_words, w_scales, vT, wt, xm, offs, out)
         av_late = tile("av_late", [P, PACK * SHARE], F32)
         nc.scalar.activation(as_walked(av_late[:, PACK * (SHARE - P) :]), as_tiles(late_av[0, 3][:]), ACT.Copy)
         quant_g(0, 0, EARLY_SLOTS, g_early[0][:])
-        quant_m(0)
+        quant_m(0, 0, HALVES, both(m_bf[0]))
         quant_g(1, 0, EARLY_SLOTS, g_early[1][:])
         early_sums = [ps.tile([P, N], F32, name="av") for j in range(2)]
         for h in range(HALVES):
             dw_pass(early_sums[0], h, 0)
-        quant_m(1)
+        quant_m(1, 0, HALVES, both(m_bf[1]))
         for h in range(HALVES):
             dw_pass(early_sums[1], h, 1)
 
-        m_bf[2] = placed("m_bf2", [P, HALVES, BLOCK], BF16, 4 * KIB)
-        weave(2, 1)
-        staged = {j: tile("staged%d" % j, [P, N], F32) for j in (0, 2, 3)}
+        m_third = [None, placed("m_third1", [P, BLOCK], BF16, 4 * KIB)]
+        weave(m_third[1][:], 2, 1)
+        staged = {j: tile("staged%d" % j, [P, N], F32) for j in (0, 1, 3)}
         nc.scalar.activation(staged[0][:, early_cols], early_sums[0][:, early_cols], ACT.Copy)
         scatter_on_scalar(0, early_cols, staged[0][:, early_cols])
-        weave(2, 0)
 
         g_late = placed("g_late", [P, HALVES, 2 * BLOCK], BF16, 7 * KIB)
         product_on_gpsimd(g_late[:, 0, kept * PACK :], 0, N - SHARE, N, av_late[:])
@@ -312,32 +319,36 @@ def tile_attend_ghv_nce_kernel(tc, xT, w_words, w_scales, vT, wt, xm, offs, out)
             for h in (1, 0):
                 dw_pass(sums[j], h, j, first=1)
 
-        nc.scalar.activation(staged[0][:, late_cols], sums[0][:, late_cols], ACT.Copy)
+        for j in range(2):
+            nc.scalar.activation(staged[j][:, late_cols], sums[j][:, late_cols], ACT.Copy)
         scatter_on_scalar(0, late_cols, staged[0][:, late_cols])
         store(0)
+        m_third[0] = placed("m_third0", [P, BLOCK], BF16, 10 * KIB)
+        nc.vector.tensor_copy(*as_quads(m_third[0][:], raw(2, 0)))
         staged_early = placed("staged_early", [P, EARLY_SLOTS], F32, 8 * KIB)
         nc.vector.tensor_copy(staged_early[:], early_sums[1][:, early_cols])
         m_codes[2] = placed("m_codes2", [P, HALVES * P], U32, 9 * KIB)
-        quant_m(2)
+        for h in (1, 0):
+            quant_m(2, h, h + 1, m_third[h][:])
         for h in range(HALVES):
             dw_pass(sums[2], h, 2)
-        m_bf[3] = placed("m_bf3", [P, HALVES, BLOCK], BF16, 4 * KIB)
+        m_last = placed("m_last", [P, HALVES, BLOCK], BF16, 10 * KIB)
         for h in range(HALVES):
-            weave_on_gpsimd(3, h)
+            weave_on_gpsimd(m_last[:, h, :], 3, h)
         scatter(1, early_cols, staged_early[:])
-        quant_m(3)
+        scatter_on_scalar(1, late_cols, staged[1][:, late_cols])
+        store(1)
+        quant_m(3, 0, HALVES, both(m_last))
         for h in range(HALVES):
             dw_pass(sums[3], h, 3)
-        staged_late = placed("staged_late", [P, EARLY_SLOTS], F32, 4 * KIB)
-        nc.vector.tensor_copy(staged_late[:], sums[1][:, late_cols])
-        scatter(1, late_cols, staged_late[:])
-        store(1)
+
+        staged[2] = placed("staged2", [P, N], F32, 10 * KIB)
         for cols in (early_cols, late_cols):
-            nc.scalar.activation(staged[2][:, cols], sums[2][:, cols], ACT.Copy)
-            scatter_on_scalar(2, cols, staged[2][:, cols])
+            nc.vector.tensor_copy(staged[2][:, cols], sums[2][:, cols])
+        for cols in (early_cols, late_cols):
+            scatter(2, cols, staged[2][:, cols])
         store(2)
-        for cols in (early_cols, late_cols):
-            nc.vector.tensor_copy(staged[3][:, cols], sums[3][:, cols])
-        for cols in (early_cols, late_cols):
-            scatter(3, cols, staged[3][:, cols])
+        nc.scalar.activation(staged[3][:], sums[3][:], ACT.Copy)
+        scatter_on_scalar(3, early_cols, staged[3][:, early_cols])
+        scatter(3, late_cols, staged[3][:, late_cols])
         store(3)

@@ -99,10 +99,10 @@ def tile_attend_ghv_nce_kernel(tc, xT, w_words, w_scales, vT, wt, xm, offs, out)
                 x_raw[u][:, :, h * HALF : (h + 1) * HALF].rearrange("p j (m t) -> p m j t", t=PACK)[:, :, :, t0:t1],
             )
 
-        def cast_x_on_scalar(u, t1):
+        def cast_x_on_scalar(u):
             nc.scalar.copy(
-                x_bf[1][:].rearrange("p (t m i j) -> p m t i j", t=PACK, i=2, j=PACK)[:, :, :t1, :, 2 * u : 2 * u + 2],
-                x_raw[u][:, :, HALF:].rearrange("p j (m i t) -> p m t i j", i=2, t=PACK)[:, :, :t1],
+                x_bf[1][:].rearrange("p (t m i j) -> p m t i j", t=PACK, i=2, j=PACK)[:, :, :, :, 2 * u : 2 * u + 2],
+                x_raw[u][:, :, HALF:].rearrange("p j (m i t) -> p m t i j", i=2, t=PACK),
             )
 
         def quant_x(h, t0, t1):
@@ -117,8 +117,8 @@ def tile_attend_ghv_nce_kernel(tc, xT, w_words, w_scales, vT, wt, xm, offs, out)
             nc.gpsimd.memset(g_codes[h][:, EARLY_SLOTS:].bitcast(I32), 0)
             nc.gpsimd.memset(g_bytes[h][:, EARLY_SLOTS:].bitcast(I32), 0)
         cast_x(0, 0, 0, PACK)
-        cast_x_on_scalar(0, PACK)
-        cast_x_on_scalar(1, 2)
+        for u in range(2):
+            cast_x_on_scalar(u)
         wt_turned = ps.tile([P, PACK, P], F32, name="av")
         for t in range(PACK):
             nc.tensor.transpose(wt_turned[:, t, :], wt_rows[:, t:HALF:PACK], identity[:])
@@ -130,7 +130,6 @@ def tile_attend_ghv_nce_kernel(tc, xT, w_words, w_scales, vT, wt, xm, offs, out)
         for done, ahead in zip(pieces, pieces[1:]):
             cast_x(1, *ahead)
             quant_x(*done)
-        cast_x(1, 1, 2, PACK)
         quant_x(*pieces[-1])
         quant_x(1, 0, PACK)
 
@@ -160,7 +159,7 @@ def tile_attend_ghv_nce_kernel(tc, xT, w_words, w_scales, vT, wt, xm, offs, out)
 
         def affine(h, t):
             c, mc = quarter[:, h, t : t + 1], minus_quarter[:, h, t : t + 1]
-            if h == 0 or t < 2:
+            if h == 0 or t == 0:
                 squared = sq_first[:, t, :] if h == 0 and t < 2 else sq[h][:, t, :]
                 nc.gpsimd.tensor_scalar(factor[:, h, t, :], squared, mc, c, ALU.mult, ALU.add)
             else:
@@ -319,30 +318,30 @@ def tile_attend_ghv_nce_kernel(tc, xT, w_words, w_scales, vT, wt, xm, offs, out)
             for h in (1, 0):
                 dw_pass(sums[j], h, j, first=1)
 
-        for j in range(2):
-            nc.scalar.activation(staged[j][:, late_cols], sums[j][:, late_cols], ACT.Copy)
-        scatter_on_scalar(0, late_cols, staged[0][:, late_cols])
-        store(0)
+        nc.scalar.activation(staged[1][:, late_cols], sums[1][:, late_cols], ACT.Copy)
         m_third[0] = placed("m_third0", [P, BLOCK], BF16, 10 * KIB)
         nc.vector.tensor_copy(*as_quads(m_third[0][:], raw(2, 0)))
-        staged_early = placed("staged_early", [P, EARLY_SLOTS], F32, 8 * KIB)
-        nc.vector.tensor_copy(staged_early[:], early_sums[1][:, early_cols])
-        m_codes[2] = placed("m_codes2", [P, HALVES * P], U32, 9 * KIB)
+        m_codes[2] = placed("m_codes2", [P, HALVES * P], U32, 8 * KIB)
         for h in (1, 0):
             quant_m(2, h, h + 1, m_third[h][:])
         for h in range(HALVES):
             dw_pass(sums[2], h, 2)
-        m_last = placed("m_last", [P, HALVES, BLOCK], BF16, 10 * KIB)
+        nc.vector.tensor_copy(staged[0][:, late_cols], sums[0][:, late_cols])
+        staged_early = placed("staged_early", [P, EARLY_SLOTS], F32, 9 * KIB + KIB // 2)
+        nc.vector.tensor_copy(staged_early[:], early_sums[1][:, early_cols])
+        m_last = placed("m_last", [P, HALVES, BLOCK], BF16, 10 * KIB + KIB // 2)
         for h in range(HALVES):
             weave_on_gpsimd(m_last[:, h, :], 3, h)
-        scatter(1, early_cols, staged_early[:])
+        scatter(0, late_cols, staged[0][:, late_cols])
+        store(0)
+        scatter_on_scalar(1, early_cols, staged_early[:])
         scatter_on_scalar(1, late_cols, staged[1][:, late_cols])
         store(1)
         quant_m(3, 0, HALVES, both(m_last))
         for h in range(HALVES):
             dw_pass(sums[3], h, 3)
 
-        staged[2] = placed("staged2", [P, N], F32, 10 * KIB)
+        staged[2] = placed("staged2", [P, N], F32, 11 * KIB)
         for cols in (early_cols, late_cols):
             nc.vector.tensor_copy(staged[2][:, cols], sums[2][:, cols])
         for cols in (early_cols, late_cols):

from contextlib import ExitStack

import concourse.mybir as mybir
from concourse.masks import make_identity

N, T, D, R = 512, 2048, 512, 1024
FLOPS = 3 * 2 * D * R * N

F32 = mybir.dt.float32
BF16 = mybir.dt.bfloat16
I32 = mybir.dt.int32
U32 = mybir.dt.uint32
U16 = mybir.dt.uint16
U8 = mybir.dt.uint8
E4M3 = mybir.dt.float8_e4m3fn_x4
E5M2 = mybir.dt.float8_e5m2_x4
ACT = mybir.ActivationFunctionType
ALU = mybir.AluOpType

P = 128
PACK = 4
HALF = P * PACK
HALVES = R // HALF
SLOT_BLOCKS = N // P
D_BLOCKS = D // P
BLOCK = P * PACK
EARLY_SLOTS = N // 2
PSUM_BUFS = 4
WT_ROW = 16
SCALE_ROW = 4
SHARE = 128
KIB = 1024


def tile_attend_ghv_nce_kernel(tc, xT, w_words, w_scales, vT, wt, xm, offs, out):
    nc = tc.nc
    with ExitStack() as ctx:
        sb = ctx.enter_context(tc.tile_pool(name="sb", bufs=1))
        loads = ctx.enter_context(tc.tile_pool(name="loads", bufs=1))
        reused = ctx.enter_context(tc.tile_pool(name="reused", bufs=1))
        ps = ctx.enter_context(tc.psum_pool(name="ps", bufs=PSUM_BUFS))

        def tile(name, shape, dtype):
            return sb.tile(shape, dtype, name=name, align_bytes=64)

        def placed(name, shape, dtype, offset):
            return reused.tile(shape, dtype, name=name, align_bytes=64, offset=offset)

        def landed(name, shape, dtype, offset):
            return loads.tile(shape, dtype, name=name, align_bytes=64, offset=offset)

        offsets = sb.tile([P, N // 16], U16, name="offsets")
        w_table = tile("w_table", [P, T], U32)
        s_table = landed("s_table", [P, T], U8, 7 * KIB)
        x_raw = [landed("x_raw%d" % u, [P, 2, R], F32, (16 + 8 * u) * KIB) for u in range(2)]
        wt_rows = tile("wt_rows", [P, HALF], F32)
        identity = tile("identity", [P, P], F32)
        windows = [tile("window%d" % j, [P, T], F32) for j in range(D_BLOCKS)]

        def zero_on_vector(words):
            odd = words.shape[1] // 2 - 1
            nc.vector.memset(words[:, :odd], 0)
            nc.vector.memset(words[:, odd:], 0)

        s_spread = tile("s_spread", [P, N], U8)
        w_bytes = tile("w_bytes", [P, N], U8)
        nc.gpsimd.memset(s_table[:].bitcast(I32), 0)
        zero_on_vector(wt_rows[:].bitcast(I32))
        zero_on_vector(w_bytes[:].bitcast(I32))
        make_identity(nc, identity[:])

        nc.sync.dma_start(w_table[:].bitcast(I32), w_words[0].rearrange("p n t -> p (n t)").bitcast(I32))
        nc.sync.dma_start(s_table[SCALE_ROW:P:8, :].bitcast(I32), w_scales[0].bitcast(I32))
        nc.sync.dma_start(offsets[:], offs)
        x_rows = xT[0].rearrange("(p j) r -> p j r", j=PACK)
        nc.sync.dma_start(x_raw[0][:], x_rows[:, :2, :])
        nc.sync.dma_start(wt_rows[WT_ROW:P:64, :], wt[0].rearrange("(h r) o -> h (r o)", h=HALVES))
        nc.sync.dma_start(x_raw[1][:], x_rows[:, 2:, :])

        zero_on_vector(windows[0][:].bitcast(I32))
        for window in windows[1:]:
            nc.gpsimd.memset(window[:].bitcast(I32), 0)

        w_codes = tile("w_codes", [P, N], U32)
        nc.vector.tensor_copy(s_spread[:], s_table[:].indirect(offsets[:]))
        for i in range(4):
            nc.sync.dma_start(w_bytes[i:P:32, :].bitcast(I32), s_spread[SCALE_ROW + 8 * i : P : 32, :].bitcast(I32))
        nc.vector.tensor_copy(w_codes[:], w_table[:].indirect(offsets[:]))

        x_bf = [tile("x_bf0", [P, HALF * PACK], BF16), placed("x_bf1", [P, HALF * PACK], BF16, 16 * KIB)]
        x_codes = [tile("x_codes%d" % h, [P, HALF], U32) for h in range(HALVES)]
        x_bytes = [tile("x_bytes%d" % h, [P, HALF], U8) for h in range(HALVES)]
        quarter = tile("quarter", [P, HALVES, PACK], F32)
        minus_quarter = tile("minus_quarter", [P, HALVES, PACK], F32)

        def cast_x(u, h, t0, t1):
            nc.vector.tensor_copy(
                x_bf[h][:].rearrange("p (t m j) -> p m j t", t=PACK, j=PACK)[:, :, 2 * u : 2 * u + 2, t0:t1],
                x_raw[u][:, :, h * HALF : (h + 1) * HALF].rearrange("p j (m t) -> p m j t", t=PACK)[:, :, :, t0:t1],
            )

        def cast_x_on_scalar(u):
            nc.scalar.copy(
                x_bf[1][:].rearrange("p (t m i j) -> p m t i j", t=PACK, i=2, j=PACK)[:, :, :, :, 2 * u : 2 * u + 2],
                x_raw[u][:, :, HALF:].rearrange("p j (m i t) -> p m t i j", i=2, t=PACK),
            )

        def quant_x(h, t0, t1):
            cols = slice(t0 * P, t1 * P)
            nc.vector.quantize_mx(x_codes[h][:, cols].bitcast(E4M3), x_bytes[h][:, cols],
                                  x_bf[h][:, t0 * P * PACK : t1 * P * PACK])

        g_codes = [tile("g_codes%d" % h, [P, N], U32) for h in range(HALVES)]
        g_bytes = [tile("g_bytes%d" % h, [P, N], U8) for h in range(HALVES)]

        for h in range(HALVES):
            nc.gpsimd.memset(g_codes[h][:, EARLY_SLOTS:].bitcast(I32), 0)
            nc.gpsimd.memset(g_bytes[h][:, EARLY_SLOTS:].bitcast(I32), 0)
        cast_x(0, 0, 0, PACK)
        for u in range(2):
            cast_x_on_scalar(u)
        wt_turned = ps.tile([P, PACK, P], F32, name="av")
        for t in range(PACK):
            nc.tensor.transpose(wt_turned[:, t, :], wt_rows[:, t:HALF:PACK], identity[:])
        wt_columns = wt_turned[:, :, WT_ROW:P:64].rearrange("p t h -> p h t")
        nc.vector.tensor_scalar(quarter[:], wt_columns, 0.25, None, ALU.mult)
        nc.vector.tensor_scalar(minus_quarter[:], wt_columns, -0.25, None, ALU.mult)
        pieces = [(0, 0, 1), (0, 1, 3), (0, 3, 4)]
        cast_x(1, *pieces[0])
        for done, ahead in zip(pieces, pieces[1:]):
            cast_x(1, *ahead)
            quant_x(*done)
        quant_x(*pieces[-1])
        quant_x(1, 0, PACK)

        v_table = [landed("v_table%d" % j, [P, T], F32, 8 * j * KIB) for j in range(PACK)]
        v_rows = vT.rearrange("(p j) c -> p j c", j=PACK)
        for j in range(PACK):
            nc.sync.dma_start(v_table[j][:], v_rows[:, j, :])

        def stationary(codes, scale_bytes, place):
            cols = slice(place * P, (place + 1) * P)
            return dict(lhsT=codes[:, cols].bitcast(E4M3), lhsT_scale=scale_bytes[:, cols])

        th = [tile("th%d" % h, [P, PACK, N], F32) for h in range(HALVES)]
        sq = [tile("sq%d" % h, [P, PACK, N], F32) for h in range(HALVES)]
        factor = tile("factor", [P, HALVES, PACK, N], F32)
        v_bf = placed("v_bf", [P, SLOT_BLOCKS, P, PACK], BF16, 4 * KIB)
        v_place = (slice(0, 4, 3), slice(1, 3))

        def score(h, t):
            a = ps.tile([P, N], F32, name="wide")
            nc.tensor.matmul_mx(a[:], rhs=w_codes[:].bitcast(E4M3), rhs_scale=w_bytes[:], start=True, stop=True,
                                **stationary(x_codes[h], x_bytes[h], t))
            nc.scalar.activation(th[h][:, t, :], a[:], ACT.Tanh, scale=0.5)

        def square(h, t0, t1):
            nc.scalar.activation(sq[h][:, t0:t1, :], th[h][:, t0:t1, :], ACT.Square)

        def affine(h, t):
            c, mc = quarter[:, h, t : t + 1], minus_quarter[:, h, t : t + 1]
            if h == 0 or t == 0:
                squared = sq_first[:, t, :] if h == 0 and t < 2 else sq[h][:, t, :]
                nc.gpsimd.tensor_scalar(factor[:, h, t, :], squared, mc, c, ALU.mult, ALU.add)
            else:
                nc.scalar.activation(factor[:, h, t, :], sq[h][:, t, :], ACT.Identity, bias=c, scale=mc)

        for t in range(PACK):
            score(0, t)
        sq_first = placed("sq_first", [P, 2, N], F32, 16 * KIB)
        for t in range(2):
            nc.gpsimd.tensor_tensor(sq_first[:, t, :], th[0][:, t, :], th[0][:, t, :], ALU.mult)
        square(0, 2, 4)
        for t0 in (0, 2):
            score(1, t0)
            score(1, t0 + 1)
            square(1, t0, t0 + 1)
            square(1, t0 + 1, t0 + 2)
        for h in range(HALVES):
            for t in range(PACK):
                affine(h, t)

        def listed(n0, n1):
            return offsets[:, n0 // 16 : n1 // 16]

        def gather_v(j, late):
            nc.vector.tensor_copy(v_bf[:, v_place[late], :, j],
                                  v_table[j][:].indirect(listed(late * EARLY_SLOTS, (late + 1) * EARLY_SLOTS)))

        for j in range(PACK - 1):
            for late in range(2):
                gather_v(j, late)

        m_raw = [[landed("m_raw%d%d" % (u, h), [P, PACK, 2 * P], F32, (8 * u + 4 * h) * KIB) for h in range(HALVES)]
                 for u in range(2)]
        for u in range(2):
            for h in (1, 0):
                rows = xm[0][h * HALF : (h + 1) * HALF, 2 * u * P : 2 * (u + 1) * P]
                nc.sync.dma_start(m_raw[u][h][:], rows.rearrange("(p t) d -> p t d", t=PACK))

        v_codes = [tile("v_codes%d" % late, [P, EARLY_SLOTS], U32) for late in range(2)]
        v_bytes = [tile("v_bytes%d" % late, [P, EARLY_SLOTS], U8) for late in range(2)]

        def quant_v(late, b0, b1, places):
            cols = slice(b0 * P, b1 * P)
            nc.vector.quantize_mx(v_codes[late][:, cols].bitcast(E4M3), v_bytes[late][:, cols],
                                  v_bf[:, places].rearrange("p b n j -> p (b n j)"))

        def direction(h, b, tag):
            late, cols = b // 2, slice(b % 2 * P, (b % 2 + 1) * P)
            av = ps.tile([P, PACK, P], F32, name=tag)
            for t in range(PACK):
                nc.tensor.matmul_mx(av[:, t, :], rhs=v_codes[late][:, cols].bitcast(E4M3), rhs_scale=v_bytes[late][:, cols],
                                    start=True, stop=True, **stationary(x_codes[h], x_bytes[h], t))
            return av

        def as_words(g_slots):
            return g_slots.rearrange("p (c i t) -> p c t i", i=2, t=PACK)

        def as_tiles(rows):
            return rows.rearrange("p t (c i) -> p c t i", i=2)

        def as_walked(values):
            return values.rearrange("p (c t i) -> p c t i", t=PACK, i=2)

        def product(g_slots, h, n0, n1, av):
            nc.vector.tensor_tensor(as_words(g_slots), as_tiles(av), as_tiles(factor[:, h, :, n0:n1]), ALU.mult)

        def product_on_gpsimd(g_slots, h, n0, n1, av):
            nc.gpsimd.tensor_tensor(as_words(g_slots), as_walked(av), as_tiles(factor[:, h, :, n0:n1]), ALU.mult)

        def quant_g(h, n0, n1, g_slots):
            cols = slice(n0, n1)
            nc.vector.quantize_mx(g_codes[h][:, cols].bitcast(E5M2), g_bytes[h][:, cols], g_slots)

        def raw(j, h):
            return m_raw[j // 2][h][:, :, j % 2 * P : (j % 2 + 1) * P]

        def as_quads(words, rows):
            return words.rearrange("p (c i t) -> p c t i", i=4, t=PACK), rows.rearrange("p t (c i) -> p c t i", i=4)

        def weave(words, j, h):
            nc.scalar.activation(*as_quads(words, raw(j, h)), ACT.Copy)

        def weave_on_gpsimd(words, j, h):
            nc.gpsimd.tensor_scalar(words.rearrange("p (c t) -> p c t", t=PACK), raw(j, h).rearrange("p t c -> p c t"),
                                    1.0, 0.0, ALU.mult, ALU.add)

        def quant_m(j, h0, h1, words):
            cols = slice(h0 * P, h1 * P)
            nc.vector.quantize_mx(m_codes[j][:, cols].bitcast(E4M3), m_bytes[j][:, cols], words)

        def both(m_block):
            return m_block[:].rearrange("p h n -> p (h n)")

        def dw_pass(bank, h, j, first=0):
            nc.tensor.matmul_mx(bank[:], rhs=g_codes[h][:].bitcast(E5M2), rhs_scale=g_bytes[h][:],
                                start=(h == first), stop=(h != first), **stationary(m_codes[j], m_bytes[j], h))

        def scatter(j, cols, values):
            nc.vector.tensor_copy(windows[j][:].indirect(listed(cols.start, cols.stop)), values)

        def scatter_on_scalar(j, cols, values):
            nc.scalar.activation(windows[j][:].indirect(listed(cols.start, cols.stop)), values, ACT.Copy)

        def store(j):
            nc.sync.dma_start(out[j * P : (j + 1) * P, :], windows[j][:])

        early_cols, late_cols = slice(0, EARLY_SLOTS), slice(EARLY_SLOTS, N)

        gather_v(PACK - 1, 0)
        quant_v(0, 0, 1, slice(0, 1))
        quant_v(0, 1, 2, slice(3, 4))
        gather_v(PACK - 1, 1)

        early_av = {(h, b): direction(h, b, "av") for h in range(HALVES) for b in range(2)}
        g_early = [tile("g_early%d" % h, [P, 2 * BLOCK], BF16) for h in range(HALVES)]
        product(g_early[0][:, :BLOCK], 0, 0, P, early_av[0, 0][:])
        quant_v(1, 0, 2, slice(1, 3))
        late_av = {(h, b): direction(h, b, "wide") for h, b in ((0, 3), (1, 2), (1, 3), (0, 2))}
        m_bf = [placed("m_bf%d" % j, [P, HALVES, BLOCK], BF16, (4 + 2 * j) * KIB) for j in range(2)]
        for j in range(2):
            weave(m_bf[j][:, 0, :], j, 0)
            weave_on_gpsimd(m_bf[j][:, 1, :], j, 1)
        for h, b in ((0, 1), (1, 0), (1, 1)):
            product(g_early[h][:, b * BLOCK : (b + 1) * BLOCK], h, b * P, (b + 1) * P, early_av[h, b][:])

        m_codes = [tile("m_codes%d" % j, [P, HALVES * P], U32) for j in (0, 1)] + [None, tile("m_codes3", [P, HALVES * P], U32)]
        m_bytes = [tile("m_bytes%d" % j, [P, HALVES * P], U8) for j in range(D_BLOCKS)]
        kept = EARLY_SLOTS - SHARE
        av_late = tile("av_late", [P, PACK * SHARE], F32)
        nc.scalar.activation(as_walked(av_late[:, PACK * (SHARE - P) :]), as_tiles(late_av[0, 3][:]), ACT.Copy)
        quant_g(0, 0, EARLY_SLOTS, g_early[0][:])
        quant_m(0, 0, HALVES, both(m_bf[0]))
        quant_g(1, 0, EARLY_SLOTS, g_early[1][:])
        early_sums = [ps.tile([P, N], F32, name="av") for j in range(2)]
        for h in range(HALVES):
            dw_pass(early_sums[0], h, 0)
        quant_m(1, 0, HALVES, both(m_bf[1]))
        for h in range(HALVES):
            dw_pass(early_sums[1], h, 1)

        m_third = [None, placed("m_third1", [P, BLOCK], BF16, 4 * KIB)]
        weave(m_third[1][:], 2, 1)
        staged = {j: tile("staged%d" % j, [P, N], F32) for j in (0, 1, 3)}
        nc.scalar.activation(staged[0][:, early_cols], early_sums[0][:, early_cols], ACT.Copy)
        scatter_on_scalar(0, early_cols, staged[0][:, early_cols])

        g_late = placed("g_late", [P, HALVES, 2 * BLOCK], BF16, 7 * KIB)
        product_on_gpsimd(g_late[:, 0, kept * PACK :], 0, N - SHARE, N, av_late[:])
        for b in (2, 3):
            product(g_late[:, 1, (b - 2) * BLOCK : (b - 1) * BLOCK], 1, b * P, (b + 1) * P, late_av[1, b][:])
        product(g_late[:, 0, : kept * PACK], 0, EARLY_SLOTS, N - SHARE, late_av[0, 2][:, :, :kept])
        quant_g(1, EARLY_SLOTS, N, g_late[:, 1, :])
        quant_g(0, EARLY_SLOTS, N, g_late[:, 0, :])
        sums = [ps.tile([P, N], F32, name=tag) for tag in ("av", "av", "wide", "wide")]
        for j in range(2):
            for h in (1, 0):
                dw_pass(sums[j], h, j, first=1)

        nc.scalar.activation(staged[1][:, late_cols], sums[1][:, late_cols], ACT.Copy)
        m_third[0] = placed("m_third0", [P, BLOCK], BF16, 10 * KIB)
        nc.vector.tensor_copy(*as_quads(m_third[0][:], raw(2, 0)))
        m_codes[2] = placed("m_codes2", [P, HALVES * P], U32, 8 * KIB)
        for h in (1, 0):
            quant_m(2, h, h + 1, m_third[h][:])
        for h in range(HALVES):
            dw_pass(sums[2], h, 2)
        nc.vector.tensor_copy(staged[0][:, late_cols], sums[0][:, late_cols])
        staged_early = placed("staged_early", [P, EARLY_SLOTS], F32, 9 * KIB + KIB // 2)
        nc.vector.tensor_copy(staged_early[:], early_sums[1][:, early_cols])
        m_last = placed("m_last", [P, HALVES, BLOCK], BF16, 10 * KIB + KIB // 2)
        for h in range(HALVES):
            weave_on_gpsimd(m_last[:, h, :], 3, h)
        scatter(0, late_cols, staged[0][:, late_cols])
        store(0)
        scatter_on_scalar(1, early_cols, staged_early[:])
        scatter_on_scalar(1, late_cols, staged[1][:, late_cols])
        store(1)
        quant_m(3, 0, HALVES, both(m_last))
        for h in range(HALVES):
            dw_pass(sums[3], h, 3)

        staged[2] = placed("staged2", [P, N], F32, 11 * KIB)
        for cols in (early_cols, late_cols):
            nc.vector.tensor_copy(staged[2][:, cols], sums[2][:, cols])
        for cols in (early_cols, late_cols):
            scatter(2, cols, staged[2][:, cols])
        store(2)
        nc.scalar.activation(staged[3][:], sums[3][:], ACT.Copy)
        scatter_on_scalar(3, early_cols, staged[3][:, early_cols])
        scatter(3, late_cols, staged[3][:, late_cols])
        store(3)
